import numpy as np, ml_dtypes
CORES = [10,34,74,98]
N = 4
import mx_ref
BF = ml_dtypes.bfloat16
def gcols(t, e):
    v = np.concatenate([t.reshape(8, 16, -1, 4), np.zeros((8, 16, 1, 4), BF)], axis=2)
    return np.ascontiguousarray(np.stack([v[g][:, e[g]] for g in range(8)])).reshape(128, -1)
def tile(rs):
    return np.stack(rs, axis=2).reshape(128, -1).astype(BF)
def pick(q, e):
    c = np.concatenate([q[0].reshape(128, -1, 4), np.zeros((128, 1, 4), np.uint8)], axis=1); s = np.concatenate([q[1], np.ones((16, 1), np.uint8)], axis=1)
    return (np.ascontiguousarray(c[:, e].reshape(128, -1)), np.ascontiguousarray(s[:, e]))
def join(*qs):
    return (np.concatenate([q[0] for q in qs], axis=1), np.concatenate([q[1] for q in qs], axis=1))
def put(q, e, v):
    c, s = q[0].reshape(128, -1, 4).copy(), q[1].copy(); c[:, e] = v[0].reshape(128, -1, 4); s[:, e] = v[1]
    return (c.reshape(128, -1), s)
def pk(c, s):
    return (np.ascontiguousarray(c), mx_ref.live(s))
def emit(q):
    return q[0], q[1]
def packed(v, rng):
    q = [mx_ref.quantize(np.ascontiguousarray(v[r])) for r in range(N)]
    return np.stack([a for a, b in q]), np.stack([mx_ref.plane(b, rng) for a, b in q])
def values_of_codes():
    e, c = np.zeros((128, 128, 4), np.float32), np.zeros((128, 2, 4), np.uint8)
    e[np.arange(128), np.arange(128), 0] = 1
    c[:127, :, 0] = np.arange(256).reshape(2, 128).T[:127]
    return mx_ref.matmul(mx_ref.quantize(e.reshape(128, 512).astype(BF)), (c.reshape(128, 8), np.full((16, 2), 127, np.uint8))).T.reshape(-1).astype(np.float64)
CODE_VALUE, SCALE_VALUE = values_of_codes(), 2.0 ** (np.arange(256) - 127.0)
def decode(q):
    return (CODE_VALUE[q[0]].reshape(16, 8, -1, 4) * SCALE_VALUE[q[1]][:, None, :, None] + 0.0).reshape(128, -1).astype(np.float32)
def f(rng, *shape):
    return mx_ref.flush((rng.standard_normal(shape, dtype=np.float32) * np.exp2(rng.integers(-2, 3, shape[:-1] + (1,)))).astype(BF))
def wide(rng, *shape, cols=0):
    v = rng.standard_normal(shape, dtype=np.float32) * np.exp2(rng.integers(-12, 13, shape)).astype(np.float32)
    if cols: v *= np.repeat(np.exp2(rng.integers(-cols, cols + 1, shape[:-2] + (1, shape[-1] // 4))) * (rng.random(shape[:-2] + (1, shape[-1] // 4)) > 0.0625), 4, axis=-1).astype(np.float32)
    return mx_ref.flush(v.astype(BF))
C, A, LIFE, T = 320, 160, 80, 8
STEPS = [2, 1, 3]
BEFORE = np.tri(C, k=-1, dtype=bool)
def big(v):
    v = v.astype(np.float32)
    v[np.abs(v) < np.float32(2.0 ** -16)] = 0
    return v.astype(BF)
def numbers_of(rng):
    x = f(rng, N, 128, 4 * C).astype(np.float32) + np.float32(0.5) * np.tile(f(rng, N, 128, 4).astype(np.float32), C)
    return {"x": big(x), "u": np.array(f(rng, N, 128, 512)), "v": np.array(f(rng, N, 128, 512))}
def layers(rng):
    return big(f(rng, N, 128, 2048)).reshape(N, 8, 16, 4, 8, 16, 4)
def weights(rng, w):
    c, p = packed(np.ascontiguousarray(w).reshape(N, 128, 2048), rng)
    return {"wc": c, "ws": p}
def bare(d):
    u = d["u"].astype(np.float32).reshape(N, 8, 16, 128, 4)
    u[:, :, :, np.arange(128) % 16 < 12] = 0
    return d["x"].astype(np.float32).reshape(N, 8, 16, C, 4), u
def planted(rng, d, x, u, w):
    return {"x": x.astype(np.float32).reshape(N, 128, 4 * C).astype(BF), "u": u.reshape(N, 128, 512).astype(BF), "v": d["v"], **weights(rng, w)}
def setup_inputs(rng):
    return {**numbers_of(rng), **weights(rng, layers(rng))}
def setup_inputs_ties(rng):
    d = numbers_of(rng)
    x, u = bare(d)
    o = rng.permutation(N) % 4
    q, half = C // LIFE, LIFE // 2
    sizes = [[LIFE] * q + [0] * (4 - q), [LIFE - 1] * 3 + [C - 3 * (LIFE - 1)], [half] * 3 + [C - 3 * half], [1, 1, 0, C - 2]]
    b = np.arange(4)
    x[:, :, :5] = 0
    for r in range(N):
        shared = [int(g) for g in rng.permutation(8)[:4]] if q == 3 and o[r] == 0 else []
        for g in range(8):
            k = rng.permutation(np.repeat(b, [LIFE, LIFE, half, half] if g in shared else sizes[o[r]]))[:, None]
            top = float(rng.choice([-1.0, 1.0, 2.0]))
            x[r, g, 0] = np.where(b < k, top - 1, np.where(b == k, top, top - rng.integers(0, 2, (C, 4))))
            n = rng.permutation(C)
            x[r, g, 1] = b == (n % 4)[:, None]
            x[r, g, 2, :, 0] = rng.integers(0, 3, C)
            x[r, g, 3, :, 0] = np.where(n < A, 2, 1)
            x[r, g, 4, :, 0] = (n % 4 == 2) & (n < 4 * (T - 1))
            x[r, g, 4, :, 1] = (n % 4 < q) & (n < 4 * (T - 1))
            u[r, g, 3, 16 * g, 0] = 1
            if g in shared: u[r, g, 4, 16 * g + 10:16 * g + 12, 0] = 2048
            elif o[r] == 0: u[r, g, 4, 16 * g + 8:16 * g + 12, 1] = 2048
            for j in range(4):
                u[r, g, 0, 16 * g + 4 + j, j] = 1
                u[r, g, 1, 16 * g + 8 + j, j // 2 if o[r] == 2 else j] = 1024
                u[r, g, 2, 16 * g + 8 + j, 0] = 1
    w = layers(rng)
    w[:, :, :, :, :, :8] = 0
    return planted(rng, d, x, u, w)
def setup_inputs_near(rng):
    d = numbers_of(rng)
    x, u = bare(d)
    o = rng.permutation(N) % 4
    still = [0, 1] + [i for i in range(8, 16)]
    x[:, :, still] = 0
    x[:, :, 0, :, 0] = rng.integers(0, 2, (N, 8, C)) * 2.0 - 1.0
    x[:, :, 1, :, 0] = 2.0 ** -10
    s = rng.integers(0, 16, (N, 8, 4, C))
    x[:, :, 8:12] = ((s[..., None] >> np.arange(4)) & 1) * 2.0 ** (np.arange(4) - 23.0)
    x[:, :, 12] = rng.integers(-1, 2, (N, 8, C, 4)) * 2.0 ** -29
    for r in range(N):
        for g in rng.permutation(8)[:4]: x[r, g, 0, rng.integers(C), 0] = 2.0 ** 29 * float(rng.choice([-1.0, 1.0]))
        k = 1.0 if o[r] == 0 else 2.0 ** -30
        for g in range(8):
            for i in range(9):
                j = (i - 1) % 4
                c = 16 * g + (0 if i == 0 else 3 + i)
                p = 8 if i == 0 else 8 + j if i < 5 else 8 + (j + 1) % 4
                if o[r] < 2:
                    u[r, g, 0, c, 0] = -k if i in (5, 7) else k
                    u[r, g, 1, c, 0] = k
                    u[r, g, p, c] = k
                elif o[r] == 2:
                    if i in (4, 8): u[r, g, 0, c, 0] = 1
                    else: u[r, g, p, c] = k
                else:
                    u[r, g, 12, c, p - 8] = k * (1 + 0.125 * j)
                    if i > 4: u[r, g, 12, c, (p - 7) % 4] = k * 1.125
    w = layers(rng)
    w[:, :, still] = 0
    w[:, :, :, :, :, still] = 0
    return planted(rng, d, x, u, w)
def setup_inputs_late(rng):
    d = numbers_of(rng)
    x, u = bare(d)
    x[:, :, 0] = 0
    e = rng.integers(0, 4, (N, 8))
    for r in range(N):
        for g in range(8): x[r, g, 0, :, e[r, g]] = 2.0 ** -6
    k = 1 + 0.125 * (2 * rng.integers(0, 4, (N, 8, 7, C, 4)) + 1)
    x[:, :, 9:] = k * rng.choice([-1.0, 1.0], k.shape) * 2.0 ** np.array([-14.0, -13.0, -12.0, -11.0, -10.0, -9.0, -8.0])[:, None, None]
    x[:, :, 8] = 0
    x[:, :, 8, :, 0] = 1.96875
    for g in range(8):
        u[:, g, 0, 16 * g] = 1
        for j in range(4):
            u[:, g, 0, 16 * g + 4 + j, j] = 1
            u[:, g, 9 + j, 16 * g + 8 + j] = 1
    w = layers(rng)
    w[:, :, :, :, :, 8:] = 0
    return planted(rng, d, x, u, w)
def setup_inputs_huge(rng):
    d = numbers_of(rng)
    u = bare(d)[1]
    h = rng.permutation(8)
    o = rng.permutation(N) % 3
    most = rng.integers(0, 4, (N, 8, 1, C, 1))
    x = -np.where(np.arange(4) == most, 0.95, 0.75) - 0.05 * rng.random((N, 8, 16, C, 4))
    x[:, h[6:]] *= rng.choice([-1.0, 1.0], (N, 2, 1, C, 1))
    for r in range(N):
        parts = h[6:] if o[r] == 1 else h[:6]
        k = -2.0 ** 30 if o[r] == 2 else 2.0 ** 30
        for g in range(8):
            some = rng.permutation(parts)[:len(parts) // 2]
            for m in parts:
                u[r, m, :, 16 * g] = k * (1 - 0.1 * rng.random((16, 4)))
                for j in range(4):
                    u[r, m, :, 16 * g + 4 + j] = k
                    u[r, m, :, 16 * g + 8 + j] = k
                    if m in some:
                        u[r, m, :, 16 * g + 4 + j, j] = 0.5 * k
                        u[r, m, :, 16 * g + 8 + j, (j + 1) % 4] = 0.5 * k
    a = int(h[0])
    for r in range(N): x[r, a, :, int(rng.integers(C))] = 1.0
    for i in (0, 8, 9, 10, 11):
        u[:, :, :, 16 * a + i] = 0
        u[:, a, :, 16 * a + i] = 2.0 ** 30
    w = np.zeros((N, 128, 4, 128, 4), np.float32)
    i = np.arange(128)
    for b in range(4): w[:, i, b, i, b] = -1
    return planted(rng, d, 2.0 ** 30 * x, u, w.astype(BF))
def setup_inputs_spread(rng):
    d = setup_inputs(rng)
    d["x"] = big(wide(rng, N, 128, 4 * C, cols=6))
    return d
def check_inputs(d):
    b = []
    for k in ("x", "u", "v"):
        a = np.abs(d[k].astype(np.float32))
        if not (np.isfinite(a).all() and ((a == 0) | (a >= 2.0 ** -30) & (a <= 2.0 ** 30)).all()): b.append("a value of " + k)
    none, least, most = [emit(mx_ref.quantize(np.full((128, 16), k, np.float32).astype(BF)))[1][0, 0] for k in (0.0, 2.0 ** -30, 2.0 ** 30)]
    for r in range(N):
        if ((d["wc"][r] == 0x7F) | (d["wc"][r] == 0xFF)).any(): b.append("wc: a code that is no number")
        s = mx_ref.live(d["ws"][r])
        if ((s != none) & ((s < least) | (s > most))).any(): b.append("ws: a scale out of range")
    return b
def reference(x, u, v, wc, ws):
    qu = [mx_ref.quantize(u[r]) for r in range(N)]
    lay = [pk(wc[r], ws[r]) for r in range(N)]
    now = [x[r] for r in range(N)]
    taken = np.zeros((N, 8, C), np.int64)
    g = np.arange(8)
    for step in STEPS:
        score, given = [], []
        for r in range(N):
            s = (mx_ref.matmul(qu[r], mx_ref.quantize(now[r])) + np.float32(0.0)).reshape(8, 16, C)
            o = np.argsort(-s[:, 0], axis=1, kind="stable")[:, :A]
            score.append(s)
            given.append(mx_ref.quantize(gcols(now[r], o)))
        made = []
        for r in range(N):
            came = given[r ^ step]
            objects = decode(came).astype(BF)
            kind = np.argmax(score[r][:, 4:8], axis=1)
            size = np.count_nonzero(kind[:, None] == np.arange(4)[:, None], axis=2)
            stand = np.count_nonzero((kind[:, :, None] == kind[:, None, :]) & BEFORE, axis=2)
            like = (mx_ref.matmul(qu[r], came) + np.float32(0.0)).reshape(8, 16, A)[:, 8:12]
            bites, meals = np.zeros((8, A), np.int64), np.zeros((8, 4, T), np.int64)
            for t in range(T):
                e = np.argmax(np.where((bites < LIFE)[:, None], like, -np.float32(np.inf)), axis=2)
                for k in range(4): bites[g, e[:, k]] += size[:, k]
                meals[:, :, t] = e
            taken[r] = meals[g[:, None], kind, stand % T]
            z = mx_ref.quantize(((now[r].astype(np.float32) + gcols(objects, taken[r]).astype(np.float32)) * np.float32(0.5)).astype(BF))
            made.append(tile([mx_ref.matmul(pick(lay[r], np.arange(128 * b, 128 * b + 128)), z) * np.float32(0.03125) + now[r][:, b::4].astype(np.float32) for b in range(4)]))
        now = made
    y, ol = np.zeros((N, 128, C), np.float32), np.zeros((N, 8, C), np.float32)
    oc, osc = np.zeros((N, 128, 4 * C), np.uint8), np.zeros((N, 16, C), np.uint8)
    for r in range(N):
        q = mx_ref.quantize(now[r])
        y[r] = mx_ref.matmul(mx_ref.quantize(v[r]), q)
        ol[r] = taken[r]
        oc[r], osc[r] = emit(q)
    return {"y": y, "ol": ol, "oc": oc, "osc": osc}

@@ -1,0 +1,495 @@
+from concourse.mybir import dt, AluOpType, AxisListType, ActivationFunctionType
+
+C, A, LIFE, TICKS = 320, 160, 80, 8
+STEPS = [2, 1, 3]
+BIG = 1.0e29
+PAD = 16
+ROW = PAD + A
+UNIT = 512.0
+VETO = -2.0e6
+TILES = [(0, 320, [None, 19, 18, 17]), (320, 256, [16, 15, 14, 13]), (576, 192, [12, 11, 10, 9]),
+         (768, 128, [8, 7, 6, 5]), (896, 128, [4, 3, 2, 1])]
+ON_SCALAR = (19, 18)
+
+F32, BF, I32, U16, CODE, U8 = "float32", "bfloat16", "int32", "uint16", "float8_e4m3fn_x4", "uint8"
+
+
+def _sb(n, d):
+    return ("sbuf", [128, n], d)
+
+
+SCRATCH = {
+    "Xt": _sb(4 * C, BF), "X32": _sb(4 * C, BF), "Xh": _sb(4 * C, BF), "Zt": _sb(4 * C, BF), "Mt": _sb(4 * A, BF),
+    "ut": _sb(512, BF), "vt": _sb(512, BF),
+    "qx": _sb(C, CODE), "sx": _sb(C, U8), "qz": _sb(C, CODE), "sz": _sb(C, U8),
+    "qu": _sb(128, CODE), "su": _sb(128, U8), "qv": _sb(128, CODE), "sv": _sb(128, U8),
+    "uq": _sb(768, CODE), "us": _sb(768, U8), "wq": _sb(512, CODE), "wp": _sb(512, U8),
+    "cq": _sb(768, CODE), "cs": _sb(768, U8),
+    "ones": _sb(516, BF), "ctmp": _sb(512, BF), "cg": _sb(512, BF), "ctl": _sb(512, BF), "ce": _sb(516, BF),
+    "Gt": _sb(4096, BF), "gq": _sb(1024, CODE), "gs": _sb(1024, U8),
+    "i1": _sb(C, I32), "i1m": _sb(C, I32), "m16": _sb(C, F32), "K1": _sb(C, F32), "R1": _sb(C, F32),
+    "R16": _sb(C, F32), "R16b": _sb(C, BF), "R4": _sb(A, BF), "m4": _sb(A, BF), "j4": _sb(A, BF),
+    "pi": _sb(4, I32), "pt": _sb(8, I32), "cols": _sb(16, F32), "c16": _sb(20, F32), "cst": _sb(20, F32),
+    "offU": _sb(48, U16), "src": _sb(C, BF), "tab": _sb(328, F32), "jrow": _sb(ROW, BF),
+    "k32": _sb(96, F32), "a32": _sb(32, F32), "cx": _sb(128, F32), "Call": _sb(224, F32), "Wt": _sb(224, F32),
+    "st": _sb(4, F32), "offY": _sb(6, U16), "kill": _sb(A, F32), "one14": _sb(14, F32), "offm": _sb(14, U16),
+    "msk": _sb(C, F32), "own": _sb(C, F32), "sg": _sb(2 * C, BF), "junk": _sb(3072, BF), "rows": _sb(20, F32),
+    "seg": _sb(C, BF), "b1": _sb(20, F32), "b2": _sb(20, F32), "Hm": _sb(C, F32), "Hs": _sb(C, F32),
+    "rk": _sb(20, F32), "offR": _sb(20, U16), "Ow": _sb(C, BF), "H3": _sb(A, BF), "H3s": _sb(A, BF),
+    "offM": _sb(40, U16),
+    "r1": _sb(C, F32), "mx": _sb(C, F32), "fk": _sb(C, F32), "cum": _sb(C, F32), "mcol": _sb(2, F32),
+    "vp": _sb(384, F32), "vT": _sb(384, F32), "s01": _sb(24, F32), "s23": _sb(24, F32), "sa": _sb(24, F32),
+    "si": _sb(24, I32), "a1": _sb(24, I32), "a2": _sb(24, I32), "s3": _sb(24, F32),
+    "Yb": _sb(96, F32), "YT": _sb(96, F32), "offZ": _sb(80, U16),
+    "like": _sb(ROW, F32), "rm": _sb(ROW, F32), "meal": _sb(8, F32), "hist": _sb(8, F32), "off": _sb(2, U16),
+    "Rw": _sb(ROW, BF), "prod": _sb(32, F32), "tot": _sb(2, F32), "off2": _sb(2, U16),
+    "Bh": _sb(PAD + 4 * A, BF), "Bm": _sb(128, BF), "idt": _sb(128, F32), "olw": _sb(4 * C, F32), "olr": _sb(C, F32),
+    "ys": _sb(C, F32),
+}
+for _r in range(3):
+    SCRATCH["qm%d" % _r] = _sb(A, CODE)
+    SCRATCH["sm%d" % _r] = _sb(A, U8)
+    SCRATCH["lq%d" % _r] = _sb(A, CODE)
+    SCRATCH["ls%d" % _r] = _sb(A, U8)
+for _b in range(8):
+    SCRATCH["p%d" % _b] = ("psum", [128, 512], F32)
+
+SEMAPHORES = ["V", "S", "P", "Gc", "ldx", "ldu", "ldw", "lds", "ldv", "sent", "arr0", "arr1", "arr2", "stored"]
+
+
+def rank_program(g, core, T, topo):
+    rank = T.rank_of(core)
+    if rank is None:
+        return
+    Op, Fn = AluOpType, ActivationFunctionType
+    queue = {"V": g.vector, "S": g.scalar, "P": g.tensor, "Gc": g, "Y": g.sync}
+    count = {}
+    known = {e: {} for e in queue}
+    writer, readers = {}, {}
+
+    def wait(e, ev):
+        sem, val, clock = ev
+        if known[e].get(sem, 0) >= val:
+            return
+        queue[e].wait_ge(T.sem[sem], val)
+        for name, n in clock.items():
+            if known[e].get(name, 0) < n:
+                known[e][name] = n
+
+    def order(e, reads, writes):
+        need = []
+        for k in reads:
+            if k in writer:
+                need.append(writer[k])
+            if k[0] == "p" and k[1:].isdigit():
+                need += [ev for ev in readers.get(k, []) if ev[0] != e]
+        for k in writes:
+            if k in writer and not (e == "P" and writer[k][0] == e):
+                need.append(writer[k])
+            need += readers.get(k, [])
+        best = {}
+        for ev in need:
+            if ev[0] not in best or best[ev[0]][1] < ev[1]:
+                best[ev[0]] = ev
+        for ev in sorted(best.values(), key=lambda x: -len(x[2])):
+            wait(e, ev)
+
+    def note(e, sem, inc, reads, writes):
+        count[sem] = count.get(sem, 0) + inc
+        clock = dict(known[e])
+        clock[sem] = count[sem]
+        ev = (sem, count[sem], clock)
+        for k in reads:
+            readers.setdefault(k, []).append(ev)
+        for k in writes:
+            writer[k] = ev
+            readers[k] = []
+        return ev
+
+    def run(e, call, reads, writes):
+        order(e, reads, writes)
+        call().then_inc(T.sem[e], 1)
+        return note(e, e, 1, reads, writes)
+
+    def dma(e, sem, out, in_, reads, writes):
+        order(e, reads, writes)
+        queue[e].dma_start(out, in_).then_inc(T.sem[sem], 16)
+        return note(e, sem, 16, reads, writes)
+
+    v, s = g.vector, g.scalar
+
+    def ts(out, in0, s1, s2, o0, o1, r, w):
+        if s2 is None:
+            return run("V", lambda: v.tensor_scalar(out, in0, s1, None, o0), r, w)
+        return run("V", lambda: v.tensor_scalar(out, in0, s1, s2, o0, o1), r, w)
+
+    def tt(out, a, b, op, r, w):
+        return run("V", lambda: v.tensor_tensor(out, a, b, op), r, w)
+
+    def cp(out, a, r, w):
+        return run("V", lambda: v.tensor_copy(out, a), r, w)
+
+    def scan(out, d0, d1, init, o0, o1, r, w):
+        return run("V", lambda: v.tensor_tensor_scan(out, d0, d1, init, o0, o1), r, w)
+
+    def turn(out, a, r, w):
+        return run("V", lambda: v.transpose(out, a), r, w)
+
+    def fill(ap, c, w):
+        return run("V", lambda: v.memset(ap, c), [], w)
+
+    def quant(q, sc, tile, r, w):
+        return run("V", lambda: v.quantize_mx(q, sc, tile), r, w)
+
+    def act(out, a, fn, r, w, **kw):
+        return run("S", lambda: s.activation(out, a, fn, **kw), r, w)
+
+    def put(ap, n, c, w):
+        return act(ap, T.ones[:, 0:n], Fn.Copy, ["ones"], w, scale=c)
+
+    def affine(out, a, scale, bias, r, w):
+        return act(out, a, Fn.Identity, r, w, scale=scale, bias=bias)
+
+    def mm(bank, n, lq, ls, rq, rs, r, start=True, stop=True):
+        return run("P", lambda: g.tensor.matmul_mx(T[bank][:, 0:n], lq, ls, rq, rs, start, stop), r, [bank])
+
+    def iota(out, pattern, base, cm, w, whole=False):
+        if whole:
+            return run("Gc", lambda: g.iota(out, pattern, base, cm), [], w)
+        return run("Gc", lambda: g.iota(out, pattern, base, cm, allow_small_or_imprecise_dtypes=True), [], w)
+
+    def keep(out, a, pattern, op, base, cm, r, w):
+        return run("Gc", lambda: g.affine_select(out, a, pattern, op, 0.0, base, cm), r, w)
+
+    def col(name, j):
+        return T[name][:, j:j + 1]
+
+    def block(name, j):
+        return T[name][:, 128 * j:128 * j + 128]
+
+    def pick(lo, hi, keys):
+        offs = T.offU[:, 8 * lo:8 * hi]
+        cp(T.uq[:, 128 * lo:128 * hi].bitcast(dt.uint32), T.qu[:, 0:128].bitcast(dt.uint32).indirect(offs),
+           ["qu"] + keys, ["uq%d" % j for j in range(lo, hi)])
+        act(T.us[:, 128 * lo:128 * hi], T.su[:, 0:128].indirect(offs), Fn.Copy, ["qu"] + keys,
+            ["us%d" % j for j in range(lo, hi)])
+
+    XK = ["X%d" % k for k in range(8)]
+    X32K = ["X32_%d" % k for k in range(8)]
+    dma("S", "ldu", T.ut[:], T.u[:], [], ["ut"])
+    dma("Y", "ldx", T.Xt[:], T.x[:], [], XK)
+    dma("Y", "ldw", T.wq[:].bitcast(dt.uint8), T.wc[:], [], ["wq"])
+    dma("Y", "lds", T.wp[:], T.ws[:], [], ["wp"])
+    dma("Y", "ldv", T.vt[:], T.v[:], [], ["vt"])
+
+    fill(T.ones[:], 1.0, ["ones"])
+    iota(T.pi[:], [[1, 4]], 0, 1, ["pi"], whole=True)
+    iota(T.i1[:], [[1, C]], 128, -1, ["i1"], whole=True)
+    iota(T.c16[:], [[16, 20]], 0, 0, ["c16"])
+    keep(T.ctmp[:], T.ones[:, 0:512], [[-16, 8], [0, 64]], Op.is_ge, 0, 1, ["ones"], ["ctmp"])
+    keep(T.cg[:], T.ctmp[:], [[16, 8], [0, 64]], Op.is_ge, 15, -1, ["ctmp"], ["cg"])
+    iota(T.src[:], [[1, C]], -A, 0, ["src"])
+    iota(T.j4[:], [[0, A // 4], [1, 4]], 0, 0, ["j4"])
+    iota(T.k32[:], [[0, 24], [1, 4]], 0, 0, ["k32"])
+    iota(T.a32[:], [[0, 2], [1, 4], [0, 4]], 0, 0, ["a32"])
+    keep(T.ctmp[:], T.ones[:, 0:512], [[-4, 32], [0, 4], [-512, 4]], Op.is_ge, 0, 1, ["ones"], ["ctmp"])
+    keep(T.ctl[:], T.ctmp[:], [[4, 32], [1, 4], [0, 4]], Op.is_gt, 0, -1, ["ctmp"], ["ctl"])
+    iota(T.tab[:], [[int(UNIT), 328]], 0, 0, ["tab"])
+    iota(T.jrow[:], [[1, ROW]], 0, 0, ["jrow"])
+    keep(T.ce[:], T.ones[:], [[-1, 516]], Op.is_equal, 3, 4, ["ones"], ["ce"])
+
+    put(T.R1[:], C, BIG, ["R1"])
+    put(T.R16b[:], C, 1.0, ["R16b"])
+    put(T.R16[:], C, 1.0, ["R16"])
+    put(T.R4[:], A, 1.0, ["R4"])
+    put(T.rows[:], 20, 0.0, ["rows%d" % c for c in range(20)])
+    put(T.R1[:, 0:C:16], 20, -BIG, ["R1"])
+    put(T.R16b[:, 0:C:16], 20, 0.0, ["R16b"])
+    put(T.R16[:, 0:C:16], 20, 0.0, ["R16"])
+    put(T.R4[:, 0:A:4], 40, 0.0, ["R4"])
+
+    for first, width, blocks in TILES:
+        lo = first + 16 * blocks[3]
+        fill(T.Gt[:, 4 * lo:4 * (first + width)], 0.0, ["G%s" % b for b in blocks])
+    ts(T.pt[:, 0:4], T.pi[:], 3, None, Op.bitwise_and, None, ["pi"], ["pt0"])
+    ts(T.pt[:, 4:5], T.pi[:, 0:1], 2, 3, Op.logical_shift_right, Op.bitwise_and, ["pi"], ["pt1"])
+    ts(T.pt[:, 5:6], T.pi[:, 0:1], 15, None, Op.bitwise_and, None, ["pi"], ["pt2"])
+    ts(T.i1m[:], T.i1[:], 15, None, Op.bitwise_and, None, ["i1"], ["i1m"])
+    cp(T.cols[:, 0:6], T.pt[:, 0:6], ["pt0", "pt1", "pt2"], ["cols"])
+    ts(T.m16[:], T.i1m[:], 0.0, None, Op.is_equal, None, ["i1m"], ["m16"])
+    cp(T.offU[:, 0:8], T.c16[:, 0:8], ["c16"], ["offUa"])
+    for j in range(4):
+        ts(T.offU[:, 8 + 8 * j:16 + 8 * j], T.c16[:, 0:8], col("cols", j), 4.0, Op.add, Op.add, ["c16", "cols"], ["offU%d" % j])
+    ts(T.offU[:, 40:48], T.c16[:, 0:8], col("cols", 0), 8.0, Op.add, Op.add, ["c16", "cols"], ["offU4"])
+    affine(T.K1[:], T.m16[:], 2 * BIG, -BIG, ["m16"], ["K1"])
+    affine(col("cols", 9), col("cols", 5), -1.0, 15.0, ["cols"], ["c9"])
+    affine(col("cols", 6), col("cols", 0), 1.0, float(4 * A), ["cols"], ["c6"])
+    affine(T.cst[:], T.c16[:], 1.0, col("cols", 9), ["c16", "c9"], ["cst"])
+    quant(T.qu[:], T.su[:], T.ut[:], ["ut"], ["qu"])
+    pick(0, 1, ["offUa"])
+
+    def scalar_constants():
+        act(T.X32[:], T.Xt[:], Fn.Copy, XK, X32K, scale=32.0)
+        put(T.vp[:], 384, 0.0, ["vp0", "vp1", "vp2", "vp3"])
+        put(T.Call[:], 224, 0.0, ["Call"])
+        put(T.kill[:], A, -BIG, ["kill"])
+        put(T.one14[:], 14, 1.0, ["one14"])
+        put(T.like[:, 0:PAD], PAD, -BIG, ["like"])
+        put(T.rm[:, 0:PAD], PAD, -BIG, ["rm"])
+        put(T.Bh[:, 0:PAD], PAD, 0.0, ["Bhp"])
+        act(col("cols", 7), col("cols", 0), Fn.Copy, ["cols"], ["c7"], scale=512.0)
+        act(col("cols", 8), col("cols", 4), Fn.Copy, ["cols"], ["c8"], scale=6.0)
+
+    def tick_constants():
+        ts(T.cx[:, 64:96], T.a32[:], col("cols", 4), VETO, Op.not_equal, Op.mult, ["a32", "cols"], ["cx2"])
+        ts(T.cx[:, 0:32], T.k32[:, 0:32], col("cols", 0), VETO, Op.is_lt, Op.mult, ["k32", "cols"], ["cx0"])
+        ts(T.cx[:, 32:64], T.k32[:, 0:32], col("cols", 0), None, Op.is_equal, None, ["k32", "cols"], ["cx1"])
+        ts(T.cx[:, 64:96], T.cx[:, 64:96], -(LIFE - 0.5) * UNIT, None, Op.add, None, ["cx2"], ["cx2"])
+        quant(block("cq", 1), block("cs", 1), T.ctl[:], ["ctl"], ["cq1"])
+        tt(T.cx[:, 96:128], T.cx[:, 64:96], T.cx[:, 32:64], Op.mult, ["cx2", "cx1"], ["cx3"])
+        ts(T.st[:], T.k32[:, 0:4], col("cols", 4), None, Op.is_equal, None, ["k32", "cols"], ["st"])
+        tt(T.cx[:, 32:64], T.cx[:, 96:128], T.cx[:, 0:32], Op.add, ["cx3", "cx0"], ["cx1"])
+        for t in range(TICKS - 1):
+            act(T.Call[:, 36 * t:36 * t + 4], T.cx[:, 32 + 4 * t:36 + 4 * t], Fn.Copy, ["cx1", "Call"], ["Call%d" % t])
+
+    def unpackers(b):
+        quant(block("cq", 2 + b), block("cs", 2 + b), T.ce[:, 3 - b:515 - b], ["ce"], ["cqE%d" % b])
+
+    def slot(c):
+        for first, width, blocks in TILES:
+            if c in blocks:
+                n = C if c is None else 16 * c
+                return T.Gt[:, 4 * first + blocks.index(c):4 * (first + n):4], n
+
+    def tastes():
+        for j in range(4):
+            mm("p%d" % (4 + j), C, block("uq", 1 + j), block("us", 1 + j), T.qx[:], T.sx[:],
+               ["uq%d" % (1 + j), "us%d" % (1 + j), "qx"])
+
+    for rnd, step in enumerate(STEPS):
+        last = rnd == len(STEPS) - 1
+        peer = T.cores[rank ^ step]
+        qm, sm, lq, ls = T["qm%d" % rnd], T["sm%d" % rnd], T["lq%d" % rnd], T["ls%d" % rnd]
+
+        quant(T.qx[:], T.sx[:], T.Xt[:], XK, ["qx"])
+        mm("p0", C, block("uq", 0), block("us", 0), T.qx[:], T.sx[:], ["uq0", "us0", "qx"])
+        mm("p1", C, block("uq", 0), block("us", 0), T.qx[:], T.sx[:], ["uq0", "us0", "qx"])
+        if rnd == 0:
+            pick(1, 4, ["offU0", "offU1", "offU2"])
+        else:
+            tastes()
+        tt(T.msk[:], T.p0[:, 0:C], T.K1[:], Op.min, ["p0", "K1"], ["msk"])
+        scan(T.own[:], T.R1[:], T.msk[:], -BIG, Op.min, Op.max, ["R1", "msk"], ["own"])
+        if rnd > 0:
+            act(T.r1[:], T.p5[:, 0:C], Fn.Copy, ["p5"], ["r1"])
+
+        def own(c):
+            return col("own", 16 * c + 15)
+
+        for i, c in enumerate(ON_SCALAR):
+            n = 16 * c
+            act(T.sg[:, C * i:C * i + n], T.p1[:, 0:n], Fn.Sign, ["p1", "own"], ["sg%d" % i], bias=own(c), scale=-1.0)
+        for i, c in enumerate(ON_SCALAR):
+            view, n = slot(c)
+            act(view, T.sg[:, C * i:C * i + n], Fn.Relu, ["sg%d" % i], ["G%d" % c, "rows%d" % c], accum_out=col("rows", c))
+
+        def compare(c):
+            view, n = slot(c)
+            ts(view, T.p0[:, 0:n], own(c), None, Op.is_lt, None, ["p0", "own"], ["G%d" % c])
+            act(T.junk[:, 8 * c * (c - 1):8 * c * (c + 1)], view, Fn.Copy, ["G%d" % c], ["junk%d" % c, "rows%d" % c],
+                accum_out=col("rows", c))
+
+        def fold(tiles):
+            first = TILES[tiles[0]][0]
+            end = TILES[tiles[-1]][0] + TILES[tiles[-1]][1]
+            keys = ["G%s" % b for k in tiles for b in TILES[k][2]]
+            quant(T.gq[:, first:end], T.gs[:, first:end], T.Gt[:, 4 * first:4 * end], keys, ["gq%d" % k for k in tiles])
+            for k in tiles:
+                f0, width, _ = TILES[k]
+                mm("p2", width, block("cq", 0), block("cs", 0), T.gq[:, f0:f0 + width], T.gs[:, f0:f0 + width],
+                   ["cq0", "gq%d" % k], start=k == 0, stop=k == len(TILES) - 1)
+
+        diag, _ = slot(None)
+        tt(diag, T.p0[:, 0:C], T.own[:], Op.is_le, ["p0", "own"], ["GNone"])
+        for c in (17, 16, 15):
+            compare(c)
+        scan(T.seg[:], T.R16b[:], diag, 0.0, Op.mult, Op.add, ["R16b", "GNone"], ["seg"])
+        for c in (14, 13):
+            compare(c)
+        if rnd == 0:
+            quant(block("cq", 0), block("cs", 0), T.cg[:], ["cg"], ["cq0"])
+        fold([0])
+        tt(T.b1[:], T.cst[:], T.seg[:, 15:C:16], Op.subtract, ["cst", "seg"], ["b1"])
+        compare(12)
+        fold([1])
+        for c in (11, 10, 9, 8, 7):
+            compare(c)
+        fold([2])
+        for c in (6, 5, 4, 3, 2, 1):
+            compare(c)
+        fold([3, 4])
+        if rnd == 0:
+            ts(T.m4[:], T.j4[:], col("cols", 4), None, Op.is_equal, None, ["j4", "cols"], ["m4"])
+            pick(4, 6, ["offU3", "offU4"])
+            tastes()
+            scalar_constants()
+            act(T.r1[:], T.p5[:, 0:C], Fn.Copy, ["p5"], ["r1"])
+        else:
+            tt(T.mx[:], T.p6[:, 0:C], T.r1[:], Op.max, ["p6", "r1"], ["mx"])
+        tt(T.b2[:], T.b1[:], T.rows[:], Op.subtract, ["b1"] + ["rows%d" % c for c in range(20)], ["b2"])
+        tt(T.Hm[:], T.p2[:, 0:C], T.m16[:], Op.mult, ["p2", "m16"], ["Hm"])
+        scan(T.Hs[:], T.R16[:], T.Hm[:], 0.0, Op.mult, Op.add, ["R16", "Hm"], ["Hs"])
+        tt(T.rk[:], T.Hs[:, 15:C:16], T.b2[:], Op.add, ["Hs", "b2"], ["rk"])
+        cp(T.offR[:], T.rk[:], ["rk"], ["offR"])
+        cp(T.Ow[:].indirect(T.offR[:]), T.src[:], ["offR", "src"], ["Ow"])
+        tt(T.H3[:], T.Ow[:, 0:A], T.m4[:], Op.mult, ["Ow", "m4"], ["H3"])
+        scan(T.H3s[:], T.R4[:], T.H3[:], 0.0, Op.mult, Op.add, ["R4", "H3"], ["H3s"])
+        ts(T.offM[:], T.H3s[:, 3:A:4], 4.0, col("cols", 6), Op.mult, Op.add, ["H3s", "c6"], ["offM"])
+        act(T.Mt[:, 2 * A:4 * A], T.Xt[:].indirect(T.offM[:, 20:40]), Fn.Copy, XK + ["offM"], ["Mb"])
+        cp(T.Mt[:, 0:2 * A], T.Xt[:].indirect(T.offM[:, 0:20]), XK + ["offM"], ["Ma"])
+        quant(qm[:], sm[:], T.Mt[:], ["Ma", "Mb"], ["qm"])
+
+        order("Gc", ["qm"], [])
+        rid, pid, _ = topo.addr(peer)
+        mask = topo.mask(core, peer)
+        lanes = len(topo.engines(core, peer))
+        arr = "arr%d" % rnd
+        g.remote_dma(lq[:].bitcast(dt.uint8), qm[:].bitcast(dt.uint8), T.sem[arr], T.sem.sent, pid, rid, mask)
+        g.remote_dma(ls[:], sm[:], T.sem[arr], T.sem.sent, pid, rid, mask)
+        count["sent"] = count.get("sent", 0) + 2 * lanes
+        writer["land"] = (arr, 2 * lanes, {arr: 2 * lanes})
+        writer.pop("qm")
+
+        act(T.Xh[:], T.Xt[:], Fn.Copy, XK, ["Xh"], scale=0.5)
+        if rnd == 0:
+            tick_constants()
+            tt(T.mx[:], T.p6[:, 0:C], T.r1[:], Op.max, ["p6", "r1"], ["mx"])
+        tt(T.mx[:], T.p7[:, 0:C], T.mx[:], Op.max, ["p7", "mx"], ["mx"])
+        tt(diag, T.p4[:, 0:C], T.mx[:], Op.is_ge, ["p4", "mx"], ["GNone"])
+        quant(T.gq[:, 0:C], T.gs[:, 0:C], T.Gt[:, 0:4 * C], ["G%s" % b for b in TILES[0][2]], ["gq0"])
+        mm("p2", C, block("cq", 1), block("cs", 1), T.gq[:, 0:C], T.gs[:, 0:C], ["cq1", "gq0"])
+        if rnd == 0:
+            unpackers(0)
+            unpackers(1)
+        tt(T.fk[:], T.p2[:, 0:C], diag, Op.is_lt, ["p2", "GNone"], ["fk"])
+        scan(T.cum[:], T.fk[:], T.fk[:], col("cols", 7), Op.add, Op.max, ["fk", "c7"], ["cum"])
+        ts(col("mcol", 0), col("cum", C - 1), col("cols", 7), None, Op.subtract, None, ["cum", "c7"], ["mcol"])
+
+        def standing(a):
+            tt(T.vp[:, 96 * a:96 * a + 80], T.cum[:, a:C:4], T.fk[:, a:C:4], Op.mult, ["cum", "fk"], ["vp%d" % a])
+
+        def weights():
+            tt(T.Wt[:], T.tab[:].indirect(T.offm[:]), T.Call[:], Op.add,
+               ["tab", "offm", "Call"] + ["Call%d" % t for t in range(TICKS - 1)], ["Wt"])
+
+        def unpack():
+            for b in range(4):
+                mm("p%d" % (4 + b), A, block("cq", 2 + b), block("cs", 2 + b), lq[:], ls[:], ["cqE%d" % b, "land"])
+
+        standing(0)
+        ts(T.offm[:], T.one14[:], col("mcol", 0), None, Op.mult, None, ["one14", "mcol"], ["offm"])
+        standing(1)
+        weights()
+
+        spare = [[] for _ in range(TICKS)]
+        if rnd == 0:
+            spare[0] += [lambda: unpackers(2)]
+            spare[1] += [lambda: unpackers(3), unpack, lambda: standing(2)]
+            spare[2] += [lambda: standing(3), lambda: ts(T.offY[:], T.c16[:, 0:6], 1.0 / 16, col("cols", 8), Op.mult, Op.add,
+                                                         ["c16", "c8"], ["offY"])]
+        else:
+            spare[1] += [lambda: standing(2), lambda: standing(3)]
+        at = 3 if rnd == 0 else 2
+        spare[at].append(lambda: turn(T.vT[:], T.vp[:], ["vp0", "vp1", "vp2", "vp3"], ["vT"]))
+        spare[at + 1].append(lambda: tt(T.s01[:], T.vT[:, 0:384:16], T.vT[:, 1:384:16], Op.add, ["vT"], ["s01"]))
+        spare[at + 1].append(lambda: tt(T.s23[:], T.vT[:, 2:384:16], T.vT[:, 3:384:16], Op.add, ["vT"], ["s23"]))
+        spare[at + 1].append(lambda: tt(T.sa[:], T.s01[:], T.s23[:], Op.add, ["s01", "s23"], ["sa"]))
+        spare[at + 2].append(lambda: ts(T.si[:], T.sa[:], -1.0, 16.0, Op.add, Op.mult, ["sa"], ["si"]))
+        spare[at + 2].append(lambda: ts(T.a1[:], T.si[:], 16 * (TICKS - 1), None, Op.bitwise_and, None, ["si"], ["a1"]))
+        spare[at + 2].append(lambda: ts(T.a2[:], T.si[:], 11, 12, Op.arith_shift_right, Op.bitwise_and, ["si"], ["a2"]))
+        spare[at + 3].append(lambda: tt(T.s3[:], T.a1[:], T.a2[:], Op.add, ["a1", "a2"], ["s3"]))
+        spare[at + 3].append(lambda: tt(T.Yb[:], T.s3[:].indirect(T.offY[:]), T.k32[:], Op.add, ["s3", "offY", "k32"], ["Yb"]))
+        spare[at + 4].append(lambda: turn(T.YT[:], T.Yb[:], ["Yb"], ["YT"]))
+        spare[at + 4].append(lambda: cp(T.offZ[:], T.YT[:, 0:80], ["YT"], ["offZ"]))
+        if last:
+            spare[7].append(lambda: quant(T.qv[:], T.sv[:], T.vt[:], ["vt"], ["qv"]))
+
+        mm("p3", A, block("uq", 5), block("us", 5), lq[:], ls[:], ["uq5", "us5", "land"])
+        if rnd > 0:
+            unpack()
+
+        for t in range(TICKS):
+            cc = t // 4
+            if t == 0:
+                scan(T.rm[:, PAD:ROW], T.p3[:, 0:A], T.kill[:], -BIG, Op.max, Op.max, ["p3", "kill"], ["rm"])
+            else:
+                scan(T.rm[:, PAD:ROW], T.like[:, PAD:ROW], T.kill[:], -BIG, Op.max, Op.max, ["like", "kill"], ["rm"])
+            act(T.sg[:, 0:ROW], T.rm[:], Fn.Sign, ["rm"], ["sg0", "meal%d" % t], bias=col("rm", ROW - 1), scale=-1.0,
+                accum_out=col("meal", t))
+            keys = ["meal%d" % t, "st"] + (["hist%d" % (t - 1)] if t % 4 else [])
+            if t % 4 == 0:
+                act(col("hist", t), col("meal", t), Fn.Copy, keys, ["hist%d" % t], scale=col("st", 0))
+            elif t % 4 < 3:
+                affine(col("hist", t), col("meal", t), col("st", t % 4), col("hist", t - 1), keys, ["hist%d" % t])
+            if 2 <= t < 6:
+                b = t - 2
+                act(T.Bh[:, PAD + A * b:PAD + A * (b + 1)], T["p%d" % (4 + b)][:, 0:A], Fn.Copy, ["p%d" % (4 + b)],
+                    ["Bh%d" % b], scale=0.5)
+            if t == 0:
+                cp(T.like[:, PAD:ROW], T.p3[:, 0:A], ["p3"], ["like"])
+            for job in spare[t]:
+                job()
+            if t % 4 == 0:
+                ts(col("off", cc), col("meal", t), col("st", 0), None, Op.mult, None, keys, ["off"])
+            else:
+                ts(col("off", cc), col("meal", t), col("st", t % 4), col("hist", t - 1), Op.mult, Op.add, keys, ["off"])
+            if t == TICKS - 1:
+                break
+            ts(T.Rw[:], T.jrow[:], col("meal", t), None, Op.is_equal, None, ["jrow", "meal%d" % t], ["Rw"])
+            n = 16 * (cc + 1)
+            tt(T.prod[:, 0:n], T.Rw[:].indirect(T.off[:, 0:cc + 1]), T.Wt[:, 32 * t:32 * t + n], Op.mult, ["Rw", "off", "Wt"], ["prod"])
+            run("V", lambda: v.tensor_reduce(col("tot", 0), T.prod[:, 0:n], AxisListType.X, Op.add), ["prod"], ["tot"])
+            ts(col("off2", 0), col("tot", 0), col("cols", 5), col("meal", t), Op.max, Op.min, ["tot", "cols", "meal%d" % t], ["off2"])
+            cp(T.like[:].indirect(T.off2[:, 0:1]), T.kill[:, 0:16], ["off2", "kill"], ["like"])
+
+        planes = ["Bhp", "Bh0", "Bh1", "Bh2", "Bh3", "off"]
+        for b in (1, 3):
+            act(T.Bm[:, b:128:4], T.Bh[:, A * b:A * b + ROW].indirect(T.off[:]), Fn.Copy, planes, ["Bm%d" % b])
+        for b in (0, 2):
+            cp(T.Bm[:, b:128:4], T.Bh[:, A * b:A * b + ROW].indirect(T.off[:]), planes, ["Bm%d" % b])
+        for h in range(2):
+            lo, hi = A * h, A * (h + 1)
+            tt(T.Zt[:, 4 * lo:4 * hi], T.Bm[:].indirect(T.offZ[:, 40 * h:40 * h + 40]), T.Xh[:, 4 * lo:4 * hi], Op.add,
+               ["Bm0", "Bm1", "Bm2", "Bm3", "offZ", "Xh"], ["Z%d" % h])
+            quant(T.qz[:, lo:hi], T.sz[:, lo:hi], T.Zt[:, 4 * lo:4 * hi], ["Z%d" % h], ["qz%d" % h])
+            for b in range(4):
+                mm("p%d" % (4 * h + b), A, block("wq", b), block("wp", b), T.qz[:, lo:hi], T.sz[:, lo:hi],
+                   ["wq", "wp", "qz%d" % h])
+        if last:
+            for t in range(4):
+                act(T.idt[:, t:128:4], T.tab[:].indirect(T.off[:]), Fn.Identity, ["tab", "off"], ["idt%d" % t],
+                    scale=1.0 / UNIT, bias=-float(PAD))
+            act(T.olw[:], T.idt[:].indirect(T.offZ[:]), Fn.Copy, ["idt0", "idt1", "idt2", "idt3", "offZ"], ["olw"])
+        for h in range(2):
+            for b in range(4):
+                k = 4 * h + b
+                big = T.X32[:, 4 * A * h + b:4 * A * (h + 1):4]
+                new = T.Xt[:, 4 * A * h + b:4 * A * (h + 1):4]
+                tt(big, T["p%d" % k][:, 0:A], big, Op.add, ["p%d" % k, X32K[k]], [X32K[k]])
+                if k < 7:
+                    act(new, big, Fn.Copy, [X32K[k]], [XK[k]], scale=1.0 / 32)
+                else:
+                    ts(new, big, 1.0 / 32, None, Op.mult, None, [X32K[k]], [XK[k]])
+
+    quant(T.qx[:], T.sx[:], T.Xt[:], XK, ["qx"])
+    act(T.olr[:], T.olw[:, 0:4 * C:4], Fn.Copy, ["olw"], ["olr"])
+    mm("p0", C, T.qv[:], T.sv[:], T.qx[:], T.sx[:], ["qv", "qx"])
+    dma("Y", "stored", T.oc[:], T.qx[:].bitcast(dt.uint8), ["qx"], [])
+    cp(T.ys[:], T.p0[:, 0:C], ["p0"], ["ys"])
+    dma("S", "stored", T.ol[:], T.olr[0:128:16, :], ["olr"], [])
+    dma("Y", "stored", T.y[:], T.ys[:], ["ys"], [])
+    for k in range(4):
+        dma("S", "stored", T.osc[4 * k:4 * k + 4, :], T.sx[32 * k:32 * k + 4, :], ["qx"], [])
+    for sem in ("Gc", "sent", "S", "P", "V"):
+        g.wait_ge(T.sem[sem], count[sem])
+    g.sync.wait_ge(T.sem.stored, count["stored"])

@@ -28,7 +28,7 @@ SCRATCH = {
     "ones": _sb(516, BF), "ctmp": _sb(512, BF), "cg": _sb(512, BF), "ctl": _sb(512, BF), "ce": _sb(516, BF),
     "Gt": _sb(4096, BF), "gq": _sb(1024, CODE), "gs": _sb(1024, U8),
     "i1": _sb(C, I32), "i1m": _sb(C, I32), "m16": _sb(C, F32), "K1": _sb(C, F32), "R1": _sb(C, F32),
-    "R16": _sb(C, F32), "R16b": _sb(C, BF), "R4": _sb(A, BF), "m4": _sb(A, BF), "j4": _sb(A, BF),
+    "R16": _sb(C, F32), "R16b": _sb(C, BF), "R4": _sb(A, BF),
     "pi": _sb(4, I32), "pt": _sb(8, I32), "cols": _sb(16, F32), "c16": _sb(20, F32), "cst": _sb(20, F32),
     "offU": _sb(48, U16), "src": _sb(C, BF), "tab": _sb(328, F32), "jrow": _sb(ROW, BF),
     "k32": _sb(96, F32), "a32": _sb(32, F32), "cx": _sb(128, F32), "Call": _sb(224, F32), "Wt": _sb(224, F32),
@@ -189,7 +189,6 @@ def rank_program(g, core, T, topo):
     keep(T.ctmp[:], T.ones[:, 0:512], [[-16, 8], [0, 64]], Op.is_ge, 0, 1, ["ones"], ["ctmp"])
     keep(T.cg[:], T.ctmp[:], [[16, 8], [0, 64]], Op.is_ge, 15, -1, ["ctmp"], ["cg"])
     iota(T.src[:], [[1, C]], -A, 0, ["src"])
-    iota(T.j4[:], [[0, A // 4], [1, 4]], 0, 0, ["j4"])
     iota(T.k32[:], [[0, 24], [1, 4]], 0, 0, ["k32"])
     iota(T.a32[:], [[0, 2], [1, 4], [0, 4]], 0, 0, ["a32"])
     keep(T.ctmp[:], T.ones[:, 0:512], [[-4, 32], [0, 4], [-512, 4]], Op.is_ge, 0, 1, ["ones"], ["ctmp"])
@@ -226,12 +225,13 @@ def rank_program(g, core, T, topo):
     affine(col("cols", 6), col("cols", 0), 1.0, float(4 * A), ["cols"], ["c6"])
     affine(T.cst[:], T.c16[:], 1.0, col("cols", 9), ["c16", "c9"], ["cst"])
     quant(T.qu[:], T.su[:], T.ut[:], ["ut"], ["qu"])
+    quant(T.qx[:], T.sx[:], T.Xt[:], XK, ["qx"])
     pick(0, 1, ["offUa"])
 
     def scalar_constants():
+        put(T.Call[:], 224, 0.0, ["Call"])
         act(T.X32[:], T.Xt[:], Fn.Copy, XK, X32K, scale=32.0)
         put(T.vp[:], 384, 0.0, ["vp0", "vp1", "vp2", "vp3"])
-        put(T.Call[:], 224, 0.0, ["Call"])
         put(T.kill[:], A, -BIG, ["kill"])
         put(T.one14[:], 14, 1.0, ["one14"])
         put(T.like[:, 0:PAD], PAD, -BIG, ["like"])
@@ -240,17 +240,21 @@ def rank_program(g, core, T, topo):
         act(col("cols", 7), col("cols", 0), Fn.Copy, ["cols"], ["c7"], scale=512.0)
         act(col("cols", 8), col("cols", 4), Fn.Copy, ["cols"], ["c8"], scale=6.0)
 
-    def tick_constants():
-        ts(T.cx[:, 64:96], T.a32[:], col("cols", 4), VETO, Op.not_equal, Op.mult, ["a32", "cols"], ["cx2"])
-        ts(T.cx[:, 0:32], T.k32[:, 0:32], col("cols", 0), VETO, Op.is_lt, Op.mult, ["k32", "cols"], ["cx0"])
-        ts(T.cx[:, 32:64], T.k32[:, 0:32], col("cols", 0), None, Op.is_equal, None, ["k32", "cols"], ["cx1"])
-        ts(T.cx[:, 64:96], T.cx[:, 64:96], -(LIFE - 0.5) * UNIT, None, Op.add, None, ["cx2"], ["cx2"])
-        quant(block("cq", 1), block("cs", 1), T.ctl[:], ["ctl"], ["cq1"])
-        tt(T.cx[:, 96:128], T.cx[:, 64:96], T.cx[:, 32:64], Op.mult, ["cx2", "cx1"], ["cx3"])
-        ts(T.st[:], T.k32[:, 0:4], col("cols", 4), None, Op.is_equal, None, ["k32", "cols"], ["st"])
-        tt(T.cx[:, 32:64], T.cx[:, 96:128], T.cx[:, 0:32], Op.add, ["cx3", "cx0"], ["cx1"])
-        for t in range(TICKS - 1):
-            act(T.Call[:, 36 * t:36 * t + 4], T.cx[:, 32 + 4 * t:36 + 4 * t], Fn.Copy, ["cx1", "Call"], ["Call%d" % t])
+    def tick_constants(part):
+        if part == 0:
+            ts(T.cx[:, 64:96], T.a32[:], col("cols", 4), VETO, Op.not_equal, Op.mult, ["a32", "cols"], ["cx2"])
+            ts(T.cx[:, 0:32], T.k32[:, 0:32], col("cols", 0), VETO, Op.is_lt, Op.mult, ["k32", "cols"], ["cx0"])
+            ts(T.cx[:, 32:64], T.k32[:, 0:32], col("cols", 0), None, Op.is_equal, None, ["k32", "cols"], ["cx1"])
+        elif part == 1:
+            ts(T.cx[:, 64:96], T.cx[:, 64:96], -(LIFE - 0.5) * UNIT, None, Op.add, None, ["cx2"], ["cx2"])
+            quant(block("cq", 1), block("cs", 1), T.ctl[:], ["ctl"], ["cq1"])
+        elif part == 2:
+            tt(T.cx[:, 96:128], T.cx[:, 64:96], T.cx[:, 32:64], Op.mult, ["cx2", "cx1"], ["cx3"])
+        elif part == 3:
+            tt(T.cx[:, 32:64], T.cx[:, 96:128], T.cx[:, 0:32], Op.add, ["cx3", "cx0"], ["cx1"])
+        else:
+            for t in range(TICKS - 1):
+                act(T.Call[:, 36 * t:36 * t + 4], T.cx[:, 32 + 4 * t:36 + 4 * t], Fn.Copy, ["cx1", "Call"], ["Call%d" % t])
 
     def unpackers(b):
         quant(block("cq", 2 + b), block("cs", 2 + b), T.ce[:, 3 - b:515 - b], ["ce"], ["cqE%d" % b])
@@ -266,51 +270,65 @@ def rank_program(g, core, T, topo):
             mm("p%d" % (4 + j), C, block("uq", 1 + j), block("us", 1 + j), T.qx[:], T.sx[:],
                ["uq%d" % (1 + j), "us%d" % (1 + j), "qx"])
 
+    halves = ((0, A), (A, C))
+
     for rnd, step in enumerate(STEPS):
         last = rnd == len(STEPS) - 1
         peer = T.cores[rank ^ step]
         qm, sm, lq, ls = T["qm%d" % rnd], T["sm%d" % rnd], T["lq%d" % rnd], T["ls%d" % rnd]
 
-        quant(T.qx[:], T.sx[:], T.Xt[:], XK, ["qx"])
         mm("p0", C, block("uq", 0), block("us", 0), T.qx[:], T.sx[:], ["uq0", "us0", "qx"])
         mm("p1", C, block("uq", 0), block("us", 0), T.qx[:], T.sx[:], ["uq0", "us0", "qx"])
+
+        def hold(h):
+            lo, hi = halves[h]
+            scan(T.own[:, lo:hi], T.R1[:, lo:hi], T.msk[:, lo:hi], -BIG, Op.min, Op.max, ["R1", "msk%d" % h], ["own%d" % h])
+
         if rnd == 0:
             pick(1, 4, ["offU0", "offU1", "offU2"])
+            tt(T.msk[:, 0:A], T.p0[:, 0:A], T.K1[:, 0:A], Op.min, ["p0", "K1"], ["msk0"])
+            tt(T.msk[:, A:C], T.p0[:, A:C], T.K1[:, A:C], Op.min, ["p0", "K1"], ["msk1"])
+            hold(0)
         else:
             tastes()
-        tt(T.msk[:], T.p0[:, 0:C], T.K1[:], Op.min, ["p0", "K1"], ["msk"])
-        scan(T.own[:], T.R1[:], T.msk[:], -BIG, Op.min, Op.max, ["R1", "msk"], ["own"])
-        if rnd > 0:
-            act(T.r1[:], T.p5[:, 0:C], Fn.Copy, ["p5"], ["r1"])
+            tt(T.msk[:, 0:A], T.p2[:, 0:A], T.K1[:, 0:A], Op.min, ["p2", "K1"], ["msk0"])
+            hold(0)
+            tt(T.msk[:, A:C], T.p3[:, 0:A], T.K1[:, A:C], Op.min, ["p3", "K1"], ["msk1"])
+        hold(1)
 
         def own(c):
             return col("own", 16 * c + 15)
 
         for i, c in enumerate(ON_SCALAR):
             n = 16 * c
-            act(T.sg[:, C * i:C * i + n], T.p1[:, 0:n], Fn.Sign, ["p1", "own"], ["sg%d" % i], bias=own(c), scale=-1.0)
+            act(T.sg[:, C * i:C * i + n], T.p1[:, 0:n], Fn.Sign, ["p1", "own1"], ["sg%d" % i], bias=own(c), scale=-1.0)
         for i, c in enumerate(ON_SCALAR):
             view, n = slot(c)
             act(view, T.sg[:, C * i:C * i + n], Fn.Relu, ["sg%d" % i], ["G%d" % c, "rows%d" % c], accum_out=col("rows", c))
 
-        def compare(c):
+        def beats(c):
             view, n = slot(c)
-            ts(view, T.p0[:, 0:n], own(c), None, Op.is_lt, None, ["p0", "own"], ["G%d" % c])
+            ts(view, T.p0[:, 0:n], own(c), None, Op.is_lt, None, ["p0", "own%d" % (c // 10)], ["G%d" % c])
+
+        def row(c):
+            view, n = slot(c)
             act(T.junk[:, 8 * c * (c - 1):8 * c * (c + 1)], view, Fn.Copy, ["G%d" % c], ["junk%d" % c, "rows%d" % c],
                 accum_out=col("rows", c))
 
-        def fold(tiles):
-            first = TILES[tiles[0]][0]
-            end = TILES[tiles[-1]][0] + TILES[tiles[-1]][1]
-            keys = ["G%s" % b for k in tiles for b in TILES[k][2]]
-            quant(T.gq[:, first:end], T.gs[:, first:end], T.Gt[:, 4 * first:4 * end], keys, ["gq%d" % k for k in tiles])
-            for k in tiles:
-                f0, width, _ = TILES[k]
-                mm("p2", width, block("cq", 0), block("cs", 0), T.gq[:, f0:f0 + width], T.gs[:, f0:f0 + width],
-                   ["cq0", "gq%d" % k], start=k == 0, stop=k == len(TILES) - 1)
+        def compare(c):
+            beats(c)
+            row(c)
+
+        def fold(k):
+            f0, width, blocks = TILES[k]
+            quant(T.gq[:, f0:f0 + width], T.gs[:, f0:f0 + width], T.Gt[:, 4 * f0:4 * (f0 + width)],
+                  ["G%s" % b for b in blocks], ["gq%d" % k])
+            mm("p2", width, block("cq", 0), block("cs", 0), T.gq[:, f0:f0 + width], T.gs[:, f0:f0 + width],
+               ["cq0", "gq%d" % k], start=k == 0, stop=k == len(TILES) - 1)
 
         diag, _ = slot(None)
-        tt(diag, T.p0[:, 0:C], T.own[:], Op.is_le, ["p0", "own"], ["GNone"])
+        compare(9)
+        tt(diag, T.p0[:, 0:C], T.own[:], Op.is_le, ["p0", "own0", "own1"], ["GNone"])
         for c in (17, 16, 15):
             compare(c)
         scan(T.seg[:], T.R16b[:], diag, 0.0, Op.mult, Op.add, ["R16b", "GNone"], ["seg"])
@@ -318,32 +336,46 @@ def rank_program(g, core, T, topo):
             compare(c)
         if rnd == 0:
             quant(block("cq", 0), block("cs", 0), T.cg[:], ["cg"], ["cq0"])
-        fold([0])
+        fold(0)
         tt(T.b1[:], T.cst[:], T.seg[:, 15:C:16], Op.subtract, ["cst", "seg"], ["b1"])
         compare(12)
-        fold([1])
-        for c in (11, 10, 9, 8, 7):
+        fold(1)
+        for c in (11, 10, 8, 7):
             compare(c)
-        fold([2])
+        fold(2)
         for c in (6, 5, 4, 3, 2, 1):
             compare(c)
-        fold([3, 4])
+        fold(3)
+        fold(4)
         if rnd == 0:
-            ts(T.m4[:], T.j4[:], col("cols", 4), None, Op.is_equal, None, ["j4", "cols"], ["m4"])
+            ts(T.st[:], T.k32[:, 0:4], col("cols", 4), None, Op.is_equal, None, ["k32", "cols"], ["st"])
             pick(4, 6, ["offU3", "offU4"])
             tastes()
+        act(T.r1[:], T.p5[:, 0:C], Fn.Copy, ["p5"], ["r1"])
+        if rnd == 0:
             scalar_constants()
-            act(T.r1[:], T.p5[:, 0:C], Fn.Copy, ["p5"], ["r1"])
-        else:
-            tt(T.mx[:], T.p6[:, 0:C], T.r1[:], Op.max, ["p6", "r1"], ["mx"])
         tt(T.b2[:], T.b1[:], T.rows[:], Op.subtract, ["b1"] + ["rows%d" % c for c in range(20)], ["b2"])
-        tt(T.Hm[:], T.p2[:, 0:C], T.m16[:], Op.mult, ["p2", "m16"], ["Hm"])
-        scan(T.Hs[:], T.R16[:], T.Hm[:], 0.0, Op.mult, Op.add, ["R16", "Hm"], ["Hs"])
-        tt(T.rk[:], T.Hs[:, 15:C:16], T.b2[:], Op.add, ["Hs", "b2"], ["rk"])
+        for h, (lo, hi) in enumerate(halves):
+            tt(T.Hm[:, lo:hi], T.p2[:, lo:hi], T.m16[:, lo:hi], Op.mult, ["p2", "m16"], ["Hm%d" % h])
+        for h, (lo, hi) in enumerate(halves):
+            scan(T.Hs[:, lo:hi], T.R16[:, lo:hi], T.Hm[:, lo:hi], 0.0, Op.mult, Op.add, ["R16", "Hm%d" % h], ["Hs%d" % h])
+        if rnd == 0:
+            tick_constants(0)
+        tt(T.rk[:], T.Hs[:, 15:C:16], T.b2[:], Op.add, ["Hs0", "Hs1", "b2"], ["rk"])
+        tt(T.mx[:], T.p6[:, 0:C], T.r1[:], Op.max, ["p6", "r1"], ["mx"])
         cp(T.offR[:], T.rk[:], ["rk"], ["offR"])
+        if rnd == 0:
+            tick_constants(1)
         cp(T.Ow[:].indirect(T.offR[:]), T.src[:], ["offR", "src"], ["Ow"])
-        tt(T.H3[:], T.Ow[:, 0:A], T.m4[:], Op.mult, ["Ow", "m4"], ["H3"])
-        scan(T.H3s[:], T.R4[:], T.H3[:], 0.0, Op.mult, Op.add, ["R4", "H3"], ["H3s"])
+        tt(T.mx[:], T.p7[:, 0:C], T.mx[:], Op.max, ["p7", "mx"], ["mx"])
+        act(T.H3[:, 3:A:4], T.Ow[:, 3:A:4], Fn.Copy, ["Ow", "st"], ["H33"], scale=col("st", 3))
+        for a in range(3):
+            ts(T.H3[:, a:A:4], T.Ow[:, a:A:4], col("st", a), None, Op.mult, None, ["Ow", "st"], ["H3%d" % a])
+        if rnd == 0:
+            tick_constants(2)
+        scan(T.H3s[:], T.R4[:], T.H3[:], 0.0, Op.mult, Op.add, ["R4", "H30", "H31", "H32", "H33"], ["H3s"])
+        if rnd == 0:
+            tick_constants(3)
         ts(T.offM[:], T.H3s[:, 3:A:4], 4.0, col("cols", 6), Op.mult, Op.add, ["H3s", "c6"], ["offM"])
         act(T.Mt[:, 2 * A:4 * A], T.Xt[:].indirect(T.offM[:, 20:40]), Fn.Copy, XK + ["offM"], ["Mb"])
         cp(T.Mt[:, 0:2 * A], T.Xt[:].indirect(T.offM[:, 0:20]), XK + ["offM"], ["Ma"])
@@ -360,17 +392,15 @@ def rank_program(g, core, T, topo):
         writer["land"] = (arr, 2 * lanes, {arr: 2 * lanes})
         writer.pop("qm")
 
-        act(T.Xh[:], T.Xt[:], Fn.Copy, XK, ["Xh"], scale=0.5)
         if rnd == 0:
-            tick_constants()
-            tt(T.mx[:], T.p6[:, 0:C], T.r1[:], Op.max, ["p6", "r1"], ["mx"])
-        tt(T.mx[:], T.p7[:, 0:C], T.mx[:], Op.max, ["p7", "mx"], ["mx"])
+            tick_constants(4)
+        act(T.Xh[:], T.Xt[:], Fn.Copy, XK, ["Xh"], scale=0.5)
         tt(diag, T.p4[:, 0:C], T.mx[:], Op.is_ge, ["p4", "mx"], ["GNone"])
         quant(T.gq[:, 0:C], T.gs[:, 0:C], T.Gt[:, 0:4 * C], ["G%s" % b for b in TILES[0][2]], ["gq0"])
         mm("p2", C, block("cq", 1), block("cs", 1), T.gq[:, 0:C], T.gs[:, 0:C], ["cq1", "gq0"])
         if rnd == 0:
-            unpackers(0)
-            unpackers(1)
+            for b in range(4):
+                unpackers(b)
         tt(T.fk[:], T.p2[:, 0:C], diag, Op.is_lt, ["p2", "GNone"], ["fk"])
         scan(T.cum[:], T.fk[:], T.fk[:], col("cols", 7), Op.add, Op.max, ["fk", "c7"], ["cum"])
         ts(col("mcol", 0), col("cum", C - 1), col("cols", 7), None, Op.subtract, None, ["cum", "c7"], ["mcol"])
@@ -378,45 +408,33 @@ def rank_program(g, core, T, topo):
         def standing(a):
             tt(T.vp[:, 96 * a:96 * a + 80], T.cum[:, a:C:4], T.fk[:, a:C:4], Op.mult, ["cum", "fk"], ["vp%d" % a])
 
-        def weights():
-            tt(T.Wt[:], T.tab[:].indirect(T.offm[:]), T.Call[:], Op.add,
-               ["tab", "offm", "Call"] + ["Call%d" % t for t in range(TICKS - 1)], ["Wt"])
-
-        def unpack():
-            for b in range(4):
-                mm("p%d" % (4 + b), A, block("cq", 2 + b), block("cs", 2 + b), lq[:], ls[:], ["cqE%d" % b, "land"])
-
         standing(0)
         ts(T.offm[:], T.one14[:], col("mcol", 0), None, Op.mult, None, ["one14", "mcol"], ["offm"])
         standing(1)
-        weights()
+        tt(T.Wt[:], T.tab[:].indirect(T.offm[:]), T.Call[:], Op.add,
+           ["tab", "offm", "Call"] + ["Call%d" % t for t in range(TICKS - 1)], ["Wt"])
 
         spare = [[] for _ in range(TICKS)]
+        spare[1] += [lambda: standing(2), lambda: standing(3)]
         if rnd == 0:
-            spare[0] += [lambda: unpackers(2)]
-            spare[1] += [lambda: unpackers(3), unpack, lambda: standing(2)]
-            spare[2] += [lambda: standing(3), lambda: ts(T.offY[:], T.c16[:, 0:6], 1.0 / 16, col("cols", 8), Op.mult, Op.add,
-                                                         ["c16", "c8"], ["offY"])]
-        else:
-            spare[1] += [lambda: standing(2), lambda: standing(3)]
-        at = 3 if rnd == 0 else 2
-        spare[at].append(lambda: turn(T.vT[:], T.vp[:], ["vp0", "vp1", "vp2", "vp3"], ["vT"]))
-        spare[at + 1].append(lambda: tt(T.s01[:], T.vT[:, 0:384:16], T.vT[:, 1:384:16], Op.add, ["vT"], ["s01"]))
-        spare[at + 1].append(lambda: tt(T.s23[:], T.vT[:, 2:384:16], T.vT[:, 3:384:16], Op.add, ["vT"], ["s23"]))
-        spare[at + 1].append(lambda: tt(T.sa[:], T.s01[:], T.s23[:], Op.add, ["s01", "s23"], ["sa"]))
-        spare[at + 2].append(lambda: ts(T.si[:], T.sa[:], -1.0, 16.0, Op.add, Op.mult, ["sa"], ["si"]))
-        spare[at + 2].append(lambda: ts(T.a1[:], T.si[:], 16 * (TICKS - 1), None, Op.bitwise_and, None, ["si"], ["a1"]))
-        spare[at + 2].append(lambda: ts(T.a2[:], T.si[:], 11, 12, Op.arith_shift_right, Op.bitwise_and, ["si"], ["a2"]))
-        spare[at + 3].append(lambda: tt(T.s3[:], T.a1[:], T.a2[:], Op.add, ["a1", "a2"], ["s3"]))
-        spare[at + 3].append(lambda: tt(T.Yb[:], T.s3[:].indirect(T.offY[:]), T.k32[:], Op.add, ["s3", "offY", "k32"], ["Yb"]))
-        spare[at + 4].append(lambda: turn(T.YT[:], T.Yb[:], ["Yb"], ["YT"]))
-        spare[at + 4].append(lambda: cp(T.offZ[:], T.YT[:, 0:80], ["YT"], ["offZ"]))
+            spare[1].append(lambda: ts(T.offY[:], T.c16[:, 0:6], 1.0 / 16, col("cols", 8), Op.mult, Op.add, ["c16", "c8"], ["offY"]))
+        spare[2].append(lambda: turn(T.vT[:], T.vp[:], ["vp0", "vp1", "vp2", "vp3"], ["vT"]))
+        spare[3].append(lambda: tt(T.s01[:], T.vT[:, 0:384:16], T.vT[:, 1:384:16], Op.add, ["vT"], ["s01"]))
+        spare[3].append(lambda: tt(T.s23[:], T.vT[:, 2:384:16], T.vT[:, 3:384:16], Op.add, ["vT"], ["s23"]))
+        spare[3].append(lambda: tt(T.sa[:], T.s01[:], T.s23[:], Op.add, ["s01", "s23"], ["sa"]))
+        spare[4].append(lambda: ts(T.si[:], T.sa[:], -1.0, 16.0, Op.add, Op.mult, ["sa"], ["si"]))
+        spare[4].append(lambda: ts(T.a1[:], T.si[:], 16 * (TICKS - 1), None, Op.bitwise_and, None, ["si"], ["a1"]))
+        spare[4].append(lambda: ts(T.a2[:], T.si[:], 11, 12, Op.arith_shift_right, Op.bitwise_and, ["si"], ["a2"]))
+        spare[5].append(lambda: tt(T.s3[:], T.a1[:], T.a2[:], Op.add, ["a1", "a2"], ["s3"]))
+        spare[5].append(lambda: tt(T.Yb[:], T.s3[:].indirect(T.offY[:]), T.k32[:], Op.add, ["s3", "offY", "k32"], ["Yb"]))
+        spare[6].append(lambda: turn(T.YT[:], T.Yb[:], ["Yb"], ["YT"]))
+        spare[7].append(lambda: cp(T.offZ[:], T.YT[:, 0:80], ["YT"], ["offZ"]))
         if last:
             spare[7].append(lambda: quant(T.qv[:], T.sv[:], T.vt[:], ["vt"], ["qv"]))
 
         mm("p3", A, block("uq", 5), block("us", 5), lq[:], ls[:], ["uq5", "us5", "land"])
-        if rnd > 0:
-            unpack()
+        for b in range(4):
+            mm("p%d" % (4 + b), A, block("cq", 2 + b), block("cs", 2 + b), lq[:], ls[:], ["cqE%d" % b, "land"])
 
         for t in range(TICKS):
             cc = t // 4
@@ -457,37 +475,62 @@ def rank_program(g, core, T, topo):
             act(T.Bm[:, b:128:4], T.Bh[:, A * b:A * b + ROW].indirect(T.off[:]), Fn.Copy, planes, ["Bm%d" % b])
         for b in (0, 2):
             cp(T.Bm[:, b:128:4], T.Bh[:, A * b:A * b + ROW].indirect(T.off[:]), planes, ["Bm%d" % b])
-        for h in range(2):
-            lo, hi = A * h, A * (h + 1)
-            tt(T.Zt[:, 4 * lo:4 * hi], T.Bm[:].indirect(T.offZ[:, 40 * h:40 * h + 40]), T.Xh[:, 4 * lo:4 * hi], Op.add,
-               ["Bm0", "Bm1", "Bm2", "Bm3", "offZ", "Xh"], ["Z%d" % h])
-            quant(T.qz[:, lo:hi], T.sz[:, lo:hi], T.Zt[:, 4 * lo:4 * hi], ["Z%d" % h], ["qz%d" % h])
+
+        def take(lo, hi, key):
+            tt(T.Zt[:, 4 * lo:4 * hi], T.Bm[:].indirect(T.offZ[:, lo // 4:hi // 4]), T.Xh[:, 4 * lo:4 * hi], Op.add,
+               ["Bm0", "Bm1", "Bm2", "Bm3", "offZ", "Xh"], [key])
+
+        def layer(h, keys):
+            lo, hi = halves[h]
+            quant(T.qz[:, lo:hi], T.sz[:, lo:hi], T.Zt[:, 4 * lo:4 * hi], keys, ["qz%d" % h])
             for b in range(4):
                 mm("p%d" % (4 * h + b), A, block("wq", b), block("wp", b), T.qz[:, lo:hi], T.sz[:, lo:hi],
                    ["wq", "wp", "qz%d" % h])
+
+        def grow(k):
+            h, b = k // 4, k % 4
+            big = T.X32[:, 4 * A * h + b:4 * A * (h + 1):4]
+            tt(big, T["p%d" % k][:, 0:A], big, Op.add, ["p%d" % k, X32K[k]], [X32K[k]])
+
+        def shrink(k, on_vector):
+            h, b = k // 4, k % 4
+            big = T.X32[:, 4 * A * h + b:4 * A * (h + 1):4]
+            new = T.Xt[:, 4 * A * h + b:4 * A * (h + 1):4]
+            if on_vector:
+                ts(new, big, 1.0 / 32, None, Op.mult, None, [X32K[k]], [XK[k]])
+            else:
+                act(new, big, Fn.Copy, [X32K[k]], [XK[k]], scale=1.0 / 32)
+
+        take(0, A, "Z0")
+        take(A, A + 48, "Z1")
+        layer(0, ["Z0"])
+        take(A + 48, C, "Z2")
         if last:
             for t in range(4):
                 act(T.idt[:, t:128:4], T.tab[:].indirect(T.off[:]), Fn.Identity, ["tab", "off"], ["idt%d" % t],
                     scale=1.0 / UNIT, bias=-float(PAD))
             act(T.olw[:], T.idt[:].indirect(T.offZ[:]), Fn.Copy, ["idt0", "idt1", "idt2", "idt3", "offZ"], ["olw"])
-        for h in range(2):
-            for b in range(4):
-                k = 4 * h + b
-                big = T.X32[:, 4 * A * h + b:4 * A * (h + 1):4]
-                new = T.Xt[:, 4 * A * h + b:4 * A * (h + 1):4]
-                tt(big, T["p%d" % k][:, 0:A], big, Op.add, ["p%d" % k, X32K[k]], [X32K[k]])
-                if k < 7:
-                    act(new, big, Fn.Copy, [X32K[k]], [XK[k]], scale=1.0 / 32)
-                else:
-                    ts(new, big, 1.0 / 32, None, Op.mult, None, [X32K[k]], [XK[k]])
+        grow(0)
+        shrink(0, False)
+        layer(1, ["Z1", "Z2"])
+        for k in range(1, 8):
+            grow(k)
+            if k < 6:
+                shrink(k, False)
+        side = (T.qv[:], T.sv[:], ["qv"]) if last else (block("uq", 0), block("us", 0), ["uq0", "us0"])
+        quant(T.qx[:, 0:A], T.sx[:, 0:A], T.Xt[:, 0:4 * A], XK[0:4], ["qx", "qx0"])
+        mm("p2", A, side[0], side[1], T.qx[:, 0:A], T.sx[:, 0:A], side[2] + ["qx0"])
+        shrink(6, True)
+        shrink(7, True)
+        quant(T.qx[:, A:C], T.sx[:, A:C], T.Xt[:, 4 * A:4 * C], XK[4:8], ["qx"])
+        mm("p3", A, side[0], side[1], T.qx[:, A:C], T.sx[:, A:C], side[2] + ["qx"])
 
-    quant(T.qx[:], T.sx[:], T.Xt[:], XK, ["qx"])
     act(T.olr[:], T.olw[:, 0:4 * C:4], Fn.Copy, ["olw"], ["olr"])
-    mm("p0", C, T.qv[:], T.sv[:], T.qx[:], T.sx[:], ["qv", "qx"])
     dma("Y", "stored", T.oc[:], T.qx[:].bitcast(dt.uint8), ["qx"], [])
-    cp(T.ys[:], T.p0[:, 0:C], ["p0"], ["ys"])
+    cp(T.ys[:, 0:A], T.p2[:, 0:A], ["p2"], ["ys0"])
+    cp(T.ys[:, A:C], T.p3[:, 0:A], ["p3"], ["ys1"])
     dma("S", "stored", T.ol[:], T.olr[0:128:16, :], ["olr"], [])
-    dma("Y", "stored", T.y[:], T.ys[:], ["ys"], [])
+    dma("Y", "stored", T.y[:], T.ys[:], ["ys0", "ys1"], [])
     for k in range(4):
         dma("S", "stored", T.osc[4 * k:4 * k + 4, :], T.sx[32 * k:32 * k + 4, :], ["qx"], [])
     for sem in ("Gc", "sent", "S", "P", "V"):

@@ -3,58 +3,38 @@ from concourse.mybir import dt, AluOpType, AxisListType, ActivationFunctionType
 C, A, LIFE, TICKS = 320, 160, 80, 8
 STEPS = [2, 1, 3]
 BIG = 1.0e29
-PAD = 16
-ROW = PAD + A
-UNIT = 512.0
-VETO = -2.0e6
-TILES = [(0, 320, [None, 19, 18, 17]), (320, 256, [16, 15, 14, 13]), (576, 192, [12, 11, 10, 9]),
-         (768, 128, [8, 7, 6, 5]), (896, 128, [4, 3, 2, 1])]
-ON_SCALAR = (19, 18)
+UNIT = 512
+VETO = 2.0e6
+LIFT, DROP = 1024.0, 4096.0
+TAB = 328
+TILES = [(0, 320, [None, 19, 18, 17]), (320, 288, [16, 15, 14, 13]), (608, 288, [12, 11, 10, 9]),
+         (896, 128, [8, 7, 6, 5]), (1024, 128, [4, 3, 2, 1])]
+WIDE = 1152
+ON_SCALAR = (9, 8, 7, 14, 13, 12, 11, 10)
 
 F32, BF, I32, U16, CODE, U8 = "float32", "bfloat16", "int32", "uint16", "float8_e4m3fn_x4", "uint8"
-
-
-def _sb(n, d):
-    return ("sbuf", [128, n], d)
-
-
-SCRATCH = {
-    "Xt": _sb(4 * C, BF), "X32": _sb(4 * C, BF), "Xh": _sb(4 * C, BF), "Zt": _sb(4 * C, BF), "Mt": _sb(4 * A, BF),
-    "ut": _sb(512, BF), "vt": _sb(512, BF),
-    "qx": _sb(C, CODE), "sx": _sb(C, U8), "qz": _sb(C, CODE), "sz": _sb(C, U8),
-    "qu": _sb(128, CODE), "su": _sb(128, U8), "qv": _sb(128, CODE), "sv": _sb(128, U8),
-    "uq": _sb(768, CODE), "us": _sb(768, U8), "wq": _sb(512, CODE), "wp": _sb(512, U8),
-    "cq": _sb(768, CODE), "cs": _sb(768, U8),
-    "ones": _sb(516, BF), "ctmp": _sb(512, BF), "cg": _sb(512, BF), "ctl": _sb(512, BF), "ce": _sb(516, BF),
-    "Gt": _sb(4096, BF), "gq": _sb(1024, CODE), "gs": _sb(1024, U8),
-    "i1": _sb(C, I32), "i1m": _sb(C, I32), "m16": _sb(C, F32), "K1": _sb(C, F32), "R1": _sb(C, F32),
-    "R16": _sb(C, F32), "R16b": _sb(C, BF), "R4": _sb(A, BF),
-    "pi": _sb(4, I32), "pt": _sb(8, I32), "cols": _sb(16, F32), "c16": _sb(20, F32), "cst": _sb(20, F32),
-    "offU": _sb(48, U16), "src": _sb(C, BF), "tab": _sb(328, F32), "jrow": _sb(ROW, BF),
-    "k32": _sb(96, F32), "a32": _sb(32, F32), "cx": _sb(128, F32), "Call": _sb(224, F32), "Wt": _sb(224, F32),
-    "st": _sb(4, F32), "offY": _sb(6, U16), "kill": _sb(A, F32), "one14": _sb(14, F32), "offm": _sb(14, U16),
-    "msk": _sb(C, F32), "own": _sb(C, F32), "sg": _sb(2 * C, BF), "junk": _sb(3072, BF), "rows": _sb(20, F32),
-    "seg": _sb(C, BF), "b1": _sb(20, F32), "b2": _sb(20, F32), "Hm": _sb(C, F32), "Hs": _sb(C, F32),
-    "rk": _sb(20, F32), "offR": _sb(20, U16), "Ow": _sb(C, BF), "H3": _sb(A, BF), "H3s": _sb(A, BF),
-    "offM": _sb(40, U16),
-    "r1": _sb(C, F32), "mx": _sb(C, F32), "fk": _sb(C, F32), "cum": _sb(C, F32), "mcol": _sb(2, F32),
-    "vp": _sb(384, F32), "vT": _sb(384, F32), "s01": _sb(24, F32), "s23": _sb(24, F32), "sa": _sb(24, F32),
-    "si": _sb(24, I32), "a1": _sb(24, I32), "a2": _sb(24, I32), "s3": _sb(24, F32),
-    "Yb": _sb(96, F32), "YT": _sb(96, F32), "offZ": _sb(80, U16),
-    "like": _sb(ROW, F32), "rm": _sb(ROW, F32), "meal": _sb(8, F32), "hist": _sb(8, F32), "off": _sb(2, U16),
-    "Rw": _sb(ROW, BF), "prod": _sb(32, F32), "tot": _sb(2, F32), "off2": _sb(2, U16),
-    "Bh": _sb(PAD + 4 * A, BF), "Bm": _sb(128, BF), "idt": _sb(128, F32), "olw": _sb(4 * C, F32), "olr": _sb(C, F32),
-    "ys": _sb(C, F32),
+SIZES = {
+    BF: dict(Xt=4 * C, X32=4 * C, Xh=4 * C, Zt=4 * C, Mt=4 * A, ut=512, vt=512, ones=516, cg=512, ck=516, ce=516, g128=128,
+             Gt=4 * WIDE, Gc=4 * A, junk=3072, step=A + 16, Bh=4 * A, Bm=128, kq=128),
+    F32: dict(j16=A, j4=A, c16=20, k128=128, k4=96, sgn=64, Bv=64, tab=2 * TAB, jq=4 * A, src=C, cols=32, K1=A, R1=A, Rc=C,
+              lift=C, lift4=A, msk=C, own=C, seg=C, rowW=20, b1=10, Hs=C, Ow=C, Os=A, Qs=C, fk=C, cum=C, s16=4,
+              Wt=64, vp=384, vT=384, s01=24, s23=24, sa=24, Yb=96, YT=96, like=A + 16, rm=A, kill=A, meal=8, hist=4,
+              prod=64, nil=64, tot=64, idt=128, olw=4 * C, olr=C, ys=C),
+    I32: dict(pi=1, pt=8, si=24, a1=24),
+    U16: dict(offU=32, offR=20, offM=40, offm=4, offY=6, offZ=80, off=4, off2=2, offB=10),
+    CODE: dict(qx=C, qz=C, qu=128, qv=128, uq=512, wq=512, cq=896, gq=WIDE, kc=A),
+    U8: dict(sx=C, sz=C, su=128, sv=128, us=512, wp=512, cs=896, gs=WIDE, ks=A),
 }
 for _r in range(3):
-    SCRATCH["qm%d" % _r] = _sb(A, CODE)
-    SCRATCH["sm%d" % _r] = _sb(A, U8)
-    SCRATCH["lq%d" % _r] = _sb(A, CODE)
-    SCRATCH["ls%d" % _r] = _sb(A, U8)
+    SIZES[CODE].update({"qm%d" % _r: A, "lq%d" % _r: A})
+    SIZES[U8].update({"sm%d" % _r: A, "ls%d" % _r: A})
+SCRATCH = {_n: ("sbuf", [128, _w], _d) for _d in SIZES for _n, _w in SIZES[_d].items()}
 for _b in range(8):
     SCRATCH["p%d" % _b] = ("psum", [128, 512], F32)
 
-SEMAPHORES = ["V", "S", "P", "Gc", "ldx", "ldu", "ldw", "lds", "ldv", "sent", "arr0", "arr1", "arr2", "stored"]
+SEMAPHORES = ["V", "S", "P", "Gc", "ldx0", "ldx1", "ldu", "ldw", "lds", "ldv", "sent", "arr0", "arr1", "arr2", "stored"]
+COLS = ["k", "a", "q", "g", "odd", "q4", "q0", "a4", "a3", "rc", "tm", "mo", "even", "late", "one", "lim", "pad", "fb",
+        "a6", "s", "w", "kp", "lo", "hi", "sg0", "sg", "l0", "l1"]
 
 
 def rank_program(g, core, T, topo):
@@ -65,7 +45,39 @@ def rank_program(g, core, T, topo):
     queue = {"V": g.vector, "S": g.scalar, "P": g.tensor, "Gc": g, "Y": g.sync}
     count = {}
     known = {e: {} for e in queue}
-    writer, readers = {}, {}
+    wrote, read = {}, {}
+
+    def at(name, lo=0, hi=None, step=1):
+        hi = SCRATCH[name][1][1] if hi is None else hi
+        if SCRATCH[name][0] == "psum":
+            bits = 1
+        elif step == 1:
+            bits = (1 << hi) - (1 << lo)
+        else:
+            bits = sum(1 << i for i in range(lo, hi, step))
+        return (T[name][:, lo:hi:step] if step > 1 else T[name][:, lo:hi], name, bits, None)
+
+    def by(win, off):
+        return (win[0].indirect(off[0]), win[1], win[2], off)
+
+    def words(view, off=None):
+        ap = view[0].bitcast(dt.uint32)
+        return (ap if off is None else ap.indirect(off[0]), view[1], view[2], off)
+
+    def col(name, j):
+        return at(name, j, j + 1)
+
+    def cc(name):
+        return col("cols", COLS.index(name))
+
+    def block(name, j):
+        return at(name, 128 * j, 128 * j + 128)
+
+    def half(name, h, k=1):
+        return at(name, k * A * h, k * A * (h + 1))
+
+    def raw(x):
+        return x[0] if isinstance(x, tuple) else x
 
     def wait(e, ev):
         sem, val, clock = ev
@@ -76,17 +88,20 @@ def rank_program(g, core, T, topo):
             if known[e].get(name, 0) < n:
                 known[e][name] = n
 
+    def sides(reads, writes):
+        reads = [x for x in reads if isinstance(x, tuple)]
+        writes = [x for x in writes if isinstance(x, tuple)]
+        return reads + [x[3] for x in reads + writes if x[3] is not None], writes
+
     def order(e, reads, writes):
         need = []
-        for k in reads:
-            if k in writer:
-                need.append(writer[k])
-            if k[0] == "p" and k[1:].isdigit():
-                need += [ev for ev in readers.get(k, []) if ev[0] != e]
-        for k in writes:
-            if k in writer and not (e == "P" and writer[k][0] == e):
-                need.append(writer[k])
-            need += readers.get(k, [])
+        for _, name, bits, _ in reads:
+            need += [ev for m, ev in wrote.get(name, []) if m & bits]
+            if SCRATCH[name][0] == "psum":
+                need += [ev for m, ev in read.get(name, []) if ev[0] != e]
+        for _, name, bits, _ in writes:
+            need += [ev for m, ev in wrote.get(name, []) if m & bits and not e == ev[0] == "P"]
+            need += [ev for m, ev in read.get(name, []) if m & bits]
         best = {}
         for ev in need:
             if ev[0] not in best or best[ev[0]][1] < ev[1]:
@@ -99,440 +114,499 @@ def rank_program(g, core, T, topo):
         clock = dict(known[e])
         clock[sem] = count[sem]
         ev = (sem, count[sem], clock)
-        for k in reads:
-            readers.setdefault(k, []).append(ev)
-        for k in writes:
-            writer[k] = ev
-            readers[k] = []
-        return ev
+        for _, name, bits, _ in writes:
+            for book in (wrote, read):
+                book[name] = [(m & ~bits, x) for m, x in book.get(name, []) if m & ~bits]
+            wrote[name].append((bits, ev))
+        for _, name, bits, _ in reads:
+            read.setdefault(name, []).append((bits, ev))
 
     def run(e, call, reads, writes):
+        reads, writes = sides(reads, writes)
         order(e, reads, writes)
         call().then_inc(T.sem[e], 1)
-        return note(e, e, 1, reads, writes)
+        note(e, e, 1, reads, writes)
 
-    def dma(e, sem, out, in_, reads, writes):
-        order(e, reads, writes)
-        queue[e].dma_start(out, in_).then_inc(T.sem[sem], 16)
-        return note(e, sem, 16, reads, writes)
+    def load(e, sem, view, ap, src):
+        order(e, [], [view])
+        queue[e].dma_start(ap, src).then_inc(T.sem[sem], 16)
+        note(e, sem, 16, [], [view])
+
+    def store(e, dst, view, ap):
+        order(e, [view], [])
+        queue[e].dma_start(dst, ap).then_inc(T.sem.stored, 16)
+        count["stored"] = count.get("stored", 0) + 16
 
     v, s = g.vector, g.scalar
 
-    def ts(out, in0, s1, s2, o0, o1, r, w):
+    def ts(out, a, s1, o0, s2=None, o1=None):
         if s2 is None:
-            return run("V", lambda: v.tensor_scalar(out, in0, s1, None, o0), r, w)
-        return run("V", lambda: v.tensor_scalar(out, in0, s1, s2, o0, o1), r, w)
-
-    def tt(out, a, b, op, r, w):
-        return run("V", lambda: v.tensor_tensor(out, a, b, op), r, w)
-
-    def cp(out, a, r, w):
-        return run("V", lambda: v.tensor_copy(out, a), r, w)
-
-    def scan(out, d0, d1, init, o0, o1, r, w):
-        return run("V", lambda: v.tensor_tensor_scan(out, d0, d1, init, o0, o1), r, w)
-
-    def turn(out, a, r, w):
-        return run("V", lambda: v.transpose(out, a), r, w)
-
-    def fill(ap, c, w):
-        return run("V", lambda: v.memset(ap, c), [], w)
-
-    def quant(q, sc, tile, r, w):
-        return run("V", lambda: v.quantize_mx(q, sc, tile), r, w)
-
-    def act(out, a, fn, r, w, **kw):
-        return run("S", lambda: s.activation(out, a, fn, **kw), r, w)
-
-    def put(ap, n, c, w):
-        return act(ap, T.ones[:, 0:n], Fn.Copy, ["ones"], w, scale=c)
-
-    def affine(out, a, scale, bias, r, w):
-        return act(out, a, Fn.Identity, r, w, scale=scale, bias=bias)
-
-    def mm(bank, n, lq, ls, rq, rs, r, start=True, stop=True):
-        return run("P", lambda: g.tensor.matmul_mx(T[bank][:, 0:n], lq, ls, rq, rs, start, stop), r, [bank])
-
-    def iota(out, pattern, base, cm, w, whole=False):
-        if whole:
-            return run("Gc", lambda: g.iota(out, pattern, base, cm), [], w)
-        return run("Gc", lambda: g.iota(out, pattern, base, cm, allow_small_or_imprecise_dtypes=True), [], w)
-
-    def keep(out, a, pattern, op, base, cm, r, w):
-        return run("Gc", lambda: g.affine_select(out, a, pattern, op, 0.0, base, cm), r, w)
-
-    def col(name, j):
-        return T[name][:, j:j + 1]
-
-    def block(name, j):
-        return T[name][:, 128 * j:128 * j + 128]
-
-    def pick(lo, hi, keys):
-        offs = T.offU[:, 8 * lo:8 * hi]
-        cp(T.uq[:, 128 * lo:128 * hi].bitcast(dt.uint32), T.qu[:, 0:128].bitcast(dt.uint32).indirect(offs),
-           ["qu"] + keys, ["uq%d" % j for j in range(lo, hi)])
-        act(T.us[:, 128 * lo:128 * hi], T.su[:, 0:128].indirect(offs), Fn.Copy, ["qu"] + keys,
-            ["us%d" % j for j in range(lo, hi)])
-
-    XK = ["X%d" % k for k in range(8)]
-    X32K = ["X32_%d" % k for k in range(8)]
-    dma("S", "ldu", T.ut[:], T.u[:], [], ["ut"])
-    dma("Y", "ldx", T.Xt[:], T.x[:], [], XK)
-    dma("Y", "ldw", T.wq[:].bitcast(dt.uint8), T.wc[:], [], ["wq"])
-    dma("Y", "lds", T.wp[:], T.ws[:], [], ["wp"])
-    dma("Y", "ldv", T.vt[:], T.v[:], [], ["vt"])
-
-    fill(T.ones[:], 1.0, ["ones"])
-    iota(T.pi[:], [[1, 4]], 0, 1, ["pi"], whole=True)
-    iota(T.i1[:], [[1, C]], 128, -1, ["i1"], whole=True)
-    iota(T.c16[:], [[16, 20]], 0, 0, ["c16"])
-    keep(T.ctmp[:], T.ones[:, 0:512], [[-16, 8], [0, 64]], Op.is_ge, 0, 1, ["ones"], ["ctmp"])
-    keep(T.cg[:], T.ctmp[:], [[16, 8], [0, 64]], Op.is_ge, 15, -1, ["ctmp"], ["cg"])
-    iota(T.src[:], [[1, C]], -A, 0, ["src"])
-    iota(T.k32[:], [[0, 24], [1, 4]], 0, 0, ["k32"])
-    iota(T.a32[:], [[0, 2], [1, 4], [0, 4]], 0, 0, ["a32"])
-    keep(T.ctmp[:], T.ones[:, 0:512], [[-4, 32], [0, 4], [-512, 4]], Op.is_ge, 0, 1, ["ones"], ["ctmp"])
-    keep(T.ctl[:], T.ctmp[:], [[4, 32], [1, 4], [0, 4]], Op.is_gt, 0, -1, ["ctmp"], ["ctl"])
-    iota(T.tab[:], [[int(UNIT), 328]], 0, 0, ["tab"])
-    iota(T.jrow[:], [[1, ROW]], 0, 0, ["jrow"])
-    keep(T.ce[:], T.ones[:], [[-1, 516]], Op.is_equal, 3, 4, ["ones"], ["ce"])
-
-    put(T.R1[:], C, BIG, ["R1"])
-    put(T.R16b[:], C, 1.0, ["R16b"])
-    put(T.R16[:], C, 1.0, ["R16"])
-    put(T.R4[:], A, 1.0, ["R4"])
-    put(T.rows[:], 20, 0.0, ["rows%d" % c for c in range(20)])
-    put(T.R1[:, 0:C:16], 20, -BIG, ["R1"])
-    put(T.R16b[:, 0:C:16], 20, 0.0, ["R16b"])
-    put(T.R16[:, 0:C:16], 20, 0.0, ["R16"])
-    put(T.R4[:, 0:A:4], 40, 0.0, ["R4"])
-
-    for first, width, blocks in TILES:
-        lo = first + 16 * blocks[3]
-        fill(T.Gt[:, 4 * lo:4 * (first + width)], 0.0, ["G%s" % b for b in blocks])
-    ts(T.pt[:, 0:4], T.pi[:], 3, None, Op.bitwise_and, None, ["pi"], ["pt0"])
-    ts(T.pt[:, 4:5], T.pi[:, 0:1], 2, 3, Op.logical_shift_right, Op.bitwise_and, ["pi"], ["pt1"])
-    ts(T.pt[:, 5:6], T.pi[:, 0:1], 15, None, Op.bitwise_and, None, ["pi"], ["pt2"])
-    ts(T.i1m[:], T.i1[:], 15, None, Op.bitwise_and, None, ["i1"], ["i1m"])
-    cp(T.cols[:, 0:6], T.pt[:, 0:6], ["pt0", "pt1", "pt2"], ["cols"])
-    ts(T.m16[:], T.i1m[:], 0.0, None, Op.is_equal, None, ["i1m"], ["m16"])
-    cp(T.offU[:, 0:8], T.c16[:, 0:8], ["c16"], ["offUa"])
-    for j in range(4):
-        ts(T.offU[:, 8 + 8 * j:16 + 8 * j], T.c16[:, 0:8], col("cols", j), 4.0, Op.add, Op.add, ["c16", "cols"], ["offU%d" % j])
-    ts(T.offU[:, 40:48], T.c16[:, 0:8], col("cols", 0), 8.0, Op.add, Op.add, ["c16", "cols"], ["offU4"])
-    affine(T.K1[:], T.m16[:], 2 * BIG, -BIG, ["m16"], ["K1"])
-    affine(col("cols", 9), col("cols", 5), -1.0, 15.0, ["cols"], ["c9"])
-    affine(col("cols", 6), col("cols", 0), 1.0, float(4 * A), ["cols"], ["c6"])
-    affine(T.cst[:], T.c16[:], 1.0, col("cols", 9), ["c16", "c9"], ["cst"])
-    quant(T.qu[:], T.su[:], T.ut[:], ["ut"], ["qu"])
-    quant(T.qx[:], T.sx[:], T.Xt[:], XK, ["qx"])
-    pick(0, 1, ["offUa"])
-
-    def scalar_constants():
-        put(T.Call[:], 224, 0.0, ["Call"])
-        act(T.X32[:], T.Xt[:], Fn.Copy, XK, X32K, scale=32.0)
-        put(T.vp[:], 384, 0.0, ["vp0", "vp1", "vp2", "vp3"])
-        put(T.kill[:], A, -BIG, ["kill"])
-        put(T.one14[:], 14, 1.0, ["one14"])
-        put(T.like[:, 0:PAD], PAD, -BIG, ["like"])
-        put(T.rm[:, 0:PAD], PAD, -BIG, ["rm"])
-        put(T.Bh[:, 0:PAD], PAD, 0.0, ["Bhp"])
-        act(col("cols", 7), col("cols", 0), Fn.Copy, ["cols"], ["c7"], scale=512.0)
-        act(col("cols", 8), col("cols", 4), Fn.Copy, ["cols"], ["c8"], scale=6.0)
-
-    def tick_constants(part):
-        if part == 0:
-            ts(T.cx[:, 64:96], T.a32[:], col("cols", 4), VETO, Op.not_equal, Op.mult, ["a32", "cols"], ["cx2"])
-            ts(T.cx[:, 0:32], T.k32[:, 0:32], col("cols", 0), VETO, Op.is_lt, Op.mult, ["k32", "cols"], ["cx0"])
-            ts(T.cx[:, 32:64], T.k32[:, 0:32], col("cols", 0), None, Op.is_equal, None, ["k32", "cols"], ["cx1"])
-        elif part == 1:
-            ts(T.cx[:, 64:96], T.cx[:, 64:96], -(LIFE - 0.5) * UNIT, None, Op.add, None, ["cx2"], ["cx2"])
-            quant(block("cq", 1), block("cs", 1), T.ctl[:], ["ctl"], ["cq1"])
-        elif part == 2:
-            tt(T.cx[:, 96:128], T.cx[:, 64:96], T.cx[:, 32:64], Op.mult, ["cx2", "cx1"], ["cx3"])
-        elif part == 3:
-            tt(T.cx[:, 32:64], T.cx[:, 96:128], T.cx[:, 0:32], Op.add, ["cx3", "cx0"], ["cx1"])
+            run("V", lambda: v.tensor_scalar(out[0], a[0], raw(s1), None, o0), [a, s1], [out])
         else:
-            for t in range(TICKS - 1):
-                act(T.Call[:, 36 * t:36 * t + 4], T.cx[:, 32 + 4 * t:36 + 4 * t], Fn.Copy, ["cx1", "Call"], ["Call%d" % t])
+            run("V", lambda: v.tensor_scalar(out[0], a[0], raw(s1), raw(s2), o0, o1), [a, s1, s2], [out])
 
-    def unpackers(b):
-        quant(block("cq", 2 + b), block("cs", 2 + b), T.ce[:, 3 - b:515 - b], ["ce"], ["cqE%d" % b])
+    def tt(out, a, b, op):
+        run("V", lambda: v.tensor_tensor(out[0], a[0], b[0], op), [a, b], [out])
+
+    def cp(out, a):
+        run("V", lambda: v.tensor_copy(out[0], a[0]), [a], [out])
+
+    def scan(out, d0, d1, init, o0, o1):
+        run("V", lambda: v.tensor_tensor_scan(out[0], d0[0], d1[0], raw(init), o0, o1), [d0, d1, init], [out])
+
+    def total(out, a):
+        run("V", lambda: v.tensor_reduce(out[0], a[0], AxisListType.X, Op.add), [a], [out])
+
+    def turn(out, a):
+        run("V", lambda: v.transpose(out[0], a[0]), [a], [out])
+
+    def fill(out, c):
+        run("V", lambda: v.memset(out[0], c), [], [out])
+
+    def quant(q, sc, tile):
+        run("V", lambda: v.quantize_mx(q[0], sc[0], tile[0]), [tile], [q, sc])
+
+    def act(out, a, fn=Fn.Copy, scale=1.0, bias=0.0, total=None):
+        run("S", lambda: s.activation(out[0], a[0], fn, bias=raw(bias), scale=raw(scale), accum_out=raw(total)),
+            [a, scale, bias], [out, total])
+
+    def affine(out, a, scale, bias):
+        act(out, a, Fn.Identity, scale, bias)
+
+    def put(out, n, c):
+        act(out, at("ones", 0, n), scale=c)
+
+    def mm(bank, n, lq, ls, rq, rs, start=True, stop=True):
+        out = at(bank, 0, n)
+        run("P", lambda: g.tensor.matmul_mx(out[0], lq[0], ls[0], rq[0], rs[0], start, stop), [lq, ls, rq, rs], [out])
+
+    def iota(out, pattern, base=0):
+        run("Gc", lambda: g.iota(out[0], pattern, base, 0, allow_small_or_imprecise_dtypes=True), [], [out])
+
+    def pick(lo, hi):
+        offs = at("offU", 8 * lo, 8 * hi)
+        cp(words(at("uq", 128 * lo, 128 * hi)), words(at("qu"), offs))
+        out, src = at("us", 128 * lo, 128 * hi), by(at("su"), offs)
+        run("S", lambda: s.activation(out[0], src[0], Fn.Copy), [src], [out])
+
+    def by_u(bank, j, rq, rs, n):
+        mm(bank, n, block("uq", j), block("us", j), rq, rs)
+
+    load("S", "ldu", at("ut"), T.ut[:], T.u[:])
+    for h in range(2):
+        load("Y", "ldx%d" % h, half("Xt", h, 4), half("Xt", h, 4)[0], T.x[:, 4 * A * h:4 * A * (h + 1)])
+    order("Y", [at("Xt")], [])
+    load("Y", "ldw", at("wq"), T.wq[:].bitcast(dt.uint8), T.wc[:])
+    load("Y", "lds", at("wp"), T.wp[:], T.ws[:])
+    load("Y", "ldv", at("vt"), T.vt[:], T.v[:])
+
+    fill(at("ones"), 1.0)
+    run("Gc", lambda: g.iota(T.pi[:], [[1, 1]], 0, 1), [], [at("pi")])
+    iota(at("c16"), [[16, 20]])
+    iota(at("j16"), [[0, 10], [int(DROP), 16]])
+    iota(at("g128"), [[1, 8], [0, 16]])
+    iota(at("k128"), [[0, 32], [1, 4]])
+    iota(at("j4"), [[0, 40], [int(DROP), 4]])
+    iota(at("sgn"), [[0, 8], [-2, 2], [0, 4]], 1)
+    iota(at("src"), [[1, C]])
+    run("Gc", lambda: g.affine_select(T.ce[:], T.ones[:], [[-1, 516]], Op.is_equal, 0.0, 3, 4), [at("ones")], [at("ce")])
+    iota(at("tab", 0, TAB), [[-UNIT, TAB]])
+    iota(at("tab", TAB, 2 * TAB), [[UNIT, TAB]])
+
+    fill(at("Gc"), 0.0)
+    for j, (shift, keep) in enumerate([(0, 3), (2, 3), (0, 15), (4, 7), (2, 1)]):
+        ts(col("pt", j), at("pi"), shift, Op.logical_shift_right, keep, Op.bitwise_and)
+    cp(at("offU", 0, 8), at("c16", 0, 8))
+    put(at("Rc"), C, -BIG)
+    put(at("ck"), 516, 0.0)
+    for first, width, blocks in TILES[:3]:
+        fill(at("Gt", 4 * (first + 16 * blocks[3]), 4 * (first + 16 * blocks[3] + 48)), 0.0)
+    cp(at("cols", 0, 5), at("pt", 0, 5))
+    for first, width, blocks in TILES[3:]:
+        fill(at("Gt", 4 * (first + 16 * blocks[3]), 4 * (first + width)), 0.0)
+    affine(cc("q0"), cc("q"), DROP, 0.0)
+    affine(cc("q4"), cc("q"), DROP, -LIFT)
+    affine(cc("rc"), cc("q"), LIFT - 1, 15 - 15 * LIFT - DROP)
+    affine(cc("l0"), cc("k"), 1.0, 4.0)
+    act(at("R1"), at("j16"), Fn.Sign)
+    affine(cc("a4"), cc("a"), DROP, -LIFT)
+    affine(cc("a3"), cc("a"), LIFT, -3 * LIFT - DROP)
+    affine(cc("tm"), cc("k"), 1.0, 4 * DROP)
+    affine(at("R1"), at("R1"), 2 * BIG, -BIG)
+    affine(at("Rc", 0, C, 16), at("c16"), 1.0, cc("rc"))
+    put(at("rowW"), 20, 0.0)
+
+    ts(cc("s"), cc("a"), 1.0, Op.max, cc("k"), Op.add)
+    for t in range(4):
+        ts(at("cg", t, 512, 4), at("g128"), cc("g"), Op.is_equal)
+    ts(cc("w"), cc("s"), 4.0, Op.is_ge, -4.0, Op.mult)
+    ts(at("K1"), at("j16"), cc("q0"), Op.not_equal, -2 * BIG, Op.mult)
+    quant(block("cq", 0), block("cs", 0), at("cg"))
+    ts(cc("kp"), cc("w"), cc("s"), Op.add, 4.0, Op.add)
+    ts(cc("sg0"), cc("w"), 0.5, Op.mult, 1.0, Op.add)
+    ts(at("offU", 24, 32), at("c16", 0, 8), cc("k"), Op.add, 8.0, Op.add)
+    for first, width, blocks in TILES[1:3]:
+        quant(at("gq", first + A, first + width), at("gs", first + A, first + width), at("Gc", 0, 4 * (width - A)))
+    ts(cc("lo"), cc("kp"), cc("l0"), Op.min)
+    ts(cc("hi"), cc("kp"), cc("l0"), Op.max)
+    ts(cc("sg"), cc("a"), 1.0, Op.min, cc("sg0"), Op.mult)
+    quant(at("qu"), at("su"), at("ut"))
+    ts(at("offU", 8, 16), at("c16", 0, 8), cc("lo"), Op.add)
+    ts(at("offU", 16, 24), at("c16", 0, 8), cc("hi"), Op.add)
+    pick(0, 1)
+
+    def class_constants():
+        ts(at("kq"), at("k128"), cc("k"), Op.is_equal, cc("sg"), Op.mult)
+        ts(at("lift4"), at("j4"), cc("a4"), Op.subtract, LIFT, Op.min)
+        yield
+        tt(at("ck", 1, 513, 4), at("kq"), at("cg", 0, 512, 4), Op.mult)
+        put(at("lift4", 3, A, 4), 40, cc("a3"))
+        yield
+        for h in range(2):
+            quant(block("cq", 1 + h), block("cs", 1 + h), at("ck", 1 - h, 513 - h))
+            yield
+
+    def tick_constants():
+        affine(cc("fb"), cc("k"), 16.0, -32.0)
+        act(cc("lim"), cc("a"), Fn.Sign)
+        affine(cc("l1"), cc("k"), -1.0 / 16, 0.0)
+        put(at("vp"), 384, 0.0)
+        put(at("kill"), A, -BIG)
+        put(at("like", A, A + 16), 16, -BIG)
+        put(at("step", 0, 1), 1, 1.0)
+        put(at("nil"), 64, 0.0)
+        put(at("s16"), 4, 1.0 / 16)
+        act(at("k4"), at("k128", 0, 96), scale=4.0)
+        affine(cc("pad"), cc("q"), 1.0, float(A))
+        affine(cc("a6"), cc("a"), 6.0, 0.0)
+        affine(cc("mo"), cc("odd"), float(TAB), cc("l1"))
+        affine(cc("lim"), cc("lim"), VETO, (LIFE - 0.5) * UNIT)
+
+    def tick_columns():
+        ts(at("Bv"), at("k128", 0, 64), cc("k"), Op.is_lt, VETO, Op.mult)
+        ts(cc("even"), cc("a"), 2.0, Op.is_lt)
+        ts(cc("late"), cc("a"), 2.0, Op.is_ge)
+        ts(cc("one"), cc("a"), 1.0, Op.is_equal)
+        tt(at("Bv"), at("Bv"), at("sgn"), Op.mult)
 
     def slot(c):
         for first, width, blocks in TILES:
             if c in blocks:
-                n = C if c is None else 16 * c
-                return T.Gt[:, 4 * first + blocks.index(c):4 * (first + n):4], n
+                return at("Gt", 4 * first + blocks.index(c), 4 * (first + 16 * c), 4)
+
+    def diag(h):
+        return at("Gt", 4 * A * h, 4 * A * (h + 1), 4)
+
+    score = ("p0", "p7")
+
+    def scores(h, last):
+        quant(half("qx", h), half("sx", h), half("Xt", h, 4))
+        if last:
+            mm(score[h], A, at("qv"), at("sv"), half("qx", h), half("sx", h))
+            return
+        by_u(score[h], 0, half("qx", h), half("sx", h), A)
+        if h == 0:
+            by_u("p3", 0, half("qx", 0), half("sx", 0), A)
+        else:
+            by_u("p1", 0, at("qx"), at("sx"), C)
+            by_u("p2", 0, at("qx"), at("sx"), C)
 
     def tastes():
-        for j in range(4):
-            mm("p%d" % (4 + j), C, block("uq", 1 + j), block("us", 1 + j), T.qx[:], T.sx[:],
-               ["uq%d" % (1 + j), "us%d" % (1 + j), "qx"])
+        by_u("p6", 2, at("qx"), at("sx"), C)
+        by_u("p5", 1, at("qx"), at("sx"), C)
 
-    halves = ((0, A), (A, C))
+    def mask(h):
+        tt(half("msk", h), at(score[h], 0, A), at("K1"), Op.add)
+
+    def hold(h):
+        scan(half("own", h), at("R1"), half("msk", h), -BIG, Op.min, Op.max)
+
+    def own(c):
+        return col("own", 16 * c + 15)
+
+    def diagonal(h):
+        tt(diag(h), at(score[h], 0, A), half("own", h), Op.is_le)
+
+    def segments(h):
+        scan(half("seg", h), half("Rc", h), diag(h), -BIG, Op.max, Op.subtract)
+
+    def spare_room(c):
+        return at("junk", 8 * c * (c - 1), 8 * c * (c + 1))
+
+    def beats(c):
+        if c in ON_SCALAR:
+            act(spare_room(c), at("p3" if c < 10 else "p1", 0, 16 * c), Fn.Sign, -1.0, own(c))
+        else:
+            ts(slot(c), at("p0" if c < 10 else "p2", 0, 16 * c), own(c), Op.is_lt)
+
+    def row(c):
+        if c in ON_SCALAR:
+            act(slot(c), spare_room(c), Fn.Relu, total=col("rowW", c))
+        else:
+            act(spare_room(c), slot(c), total=col("rowW", c))
+
+    def by_scalar(blocks):
+        for i, c in enumerate(blocks):
+            beats(c)
+            if i:
+                row(blocks[i - 1])
+        row(blocks[-1])
+
+    def pack(lo, hi):
+        quant(at("gq", lo, hi), at("gs", lo, hi), at("Gt", 4 * lo, 4 * hi))
+
+    def fold(k, h, start=False, stop=False):
+        first, width, blocks = TILES[k]
+        lo, hi = (first + A, first + width) if h else (first, first + min(A, width))
+        mm(("p3", "p4")[h], hi - lo, block("cq", 0), block("cs", 0), at("gq", lo, hi), at("gs", lo, hi), start, stop)
+
+    def ends(name, h):
+        return at(name, A * h + 15, A * (h + 1), 16)
+
+    def ranks(h):
+        scan(half("Hs", h), at(("p3", "p4")[h], 0, A), half("lift", h), -DROP, Op.max, Op.add)
+
+    def places(h):
+        ts(at("offR", 10 * h, 10 * h + 10), at("b1") if h else ends("Hs", 0), DROP, Op.add)
+
+    def spread(h):
+        cp(by(at("Ow"), at("offR", 10 * h, 10 * h + 10)), half("src", h))
+
+    def prefer(h):
+        tt(at("Gc", h, 4 * A, 4), at("p5", A * h, A * (h + 1)), half("Qs", h), Op.is_ge)
+
+    def standing(a):
+        tt(at("vp", 96 * a, 96 * a + 80), at("cum", a, C, 4), at("fk", a, C, 4), Op.mult)
+
+    def take(lo, hi):
+        tt(at("Zt", 4 * lo, 4 * hi), by(at("Bm"), at("offZ", lo // 4, hi // 4)), at("Xh", 4 * lo, 4 * hi), Op.add)
+
+    def layer(h):
+        quant(half("qz", h), half("sz", h), half("Zt", h, 4))
+        for b in range(4):
+            mm("p%d" % (4 * h + b), A, block("wq", b), block("wp", b), half("qz", h), half("sz", h))
+
+    def plane(name, k):
+        return at(name, 4 * A * (k // 4) + k % 4, 4 * A * (k // 4 + 1), 4)
+
+    def grow(k):
+        tt(plane("X32", k), at("p%d" % k, 0, A), plane("X32", k), Op.add)
+
+    def shrink(k, on_vector=False):
+        if on_vector:
+            ts(plane("Xt", k), plane("X32", k), 1.0 / 32, Op.mult)
+        else:
+            act(plane("Xt", k), plane("X32", k), scale=1.0 / 32)
+
+    scores(0, False)
+    scores(1, False)
+    pick(1, 4)
+    tick_constants()
+    mask(0)
+    for h in range(2):
+        ts(half("lift", h), at("j16"), cc("q4"), Op.subtract, LIFT, Op.min)
+    hold(0)
+    tastes()
+    setup = class_constants()
 
     for rnd, step in enumerate(STEPS):
         last = rnd == len(STEPS) - 1
         peer = T.cores[rank ^ step]
-        qm, sm, lq, ls = T["qm%d" % rnd], T["sm%d" % rnd], T["lq%d" % rnd], T["ls%d" % rnd]
+        qm, sm, lq, ls = [at(n % rnd) for n in ("qm%d", "sm%d", "lq%d", "ls%d")]
 
-        mm("p0", C, block("uq", 0), block("us", 0), T.qx[:], T.sx[:], ["uq0", "us0", "qx"])
-        mm("p1", C, block("uq", 0), block("us", 0), T.qx[:], T.sx[:], ["uq0", "us0", "qx"])
+        def aside():
+            next(setup, None)
 
-        def hold(h):
-            lo, hi = halves[h]
-            scan(T.own[:, lo:hi], T.R1[:, lo:hi], T.msk[:, lo:hi], -BIG, Op.min, Op.max, ["R1", "msk%d" % h], ["own%d" % h])
-
-        if rnd == 0:
-            pick(1, 4, ["offU0", "offU1", "offU2"])
-            tt(T.msk[:, 0:A], T.p0[:, 0:A], T.K1[:, 0:A], Op.min, ["p0", "K1"], ["msk0"])
-            tt(T.msk[:, A:C], T.p0[:, A:C], T.K1[:, A:C], Op.min, ["p0", "K1"], ["msk1"])
-            hold(0)
-        else:
-            tastes()
-            tt(T.msk[:, 0:A], T.p2[:, 0:A], T.K1[:, 0:A], Op.min, ["p2", "K1"], ["msk0"])
-            hold(0)
-            tt(T.msk[:, A:C], T.p3[:, 0:A], T.K1[:, A:C], Op.min, ["p3", "K1"], ["msk1"])
-        hold(1)
-
-        def own(c):
-            return col("own", 16 * c + 15)
-
-        for i, c in enumerate(ON_SCALAR):
-            n = 16 * c
-            act(T.sg[:, C * i:C * i + n], T.p1[:, 0:n], Fn.Sign, ["p1", "own1"], ["sg%d" % i], bias=own(c), scale=-1.0)
-        for i, c in enumerate(ON_SCALAR):
-            view, n = slot(c)
-            act(view, T.sg[:, C * i:C * i + n], Fn.Relu, ["sg%d" % i], ["G%d" % c, "rows%d" % c], accum_out=col("rows", c))
-
-        def beats(c):
-            view, n = slot(c)
-            ts(view, T.p0[:, 0:n], own(c), None, Op.is_lt, None, ["p0", "own%d" % (c // 10)], ["G%d" % c])
-
-        def row(c):
-            view, n = slot(c)
-            act(T.junk[:, 8 * c * (c - 1):8 * c * (c + 1)], view, Fn.Copy, ["G%d" % c], ["junk%d" % c, "rows%d" % c],
-                accum_out=col("rows", c))
-
-        def compare(c):
+        aside()
+        by_scalar([c for c in ON_SCALAR if c < 10])
+        diagonal(0)
+        for c in (6, 5):
             beats(c)
+        mask(1)
+        for c in (4, 3, 2, 1):
+            beats(c)
+        hold(1)
+        for c in (6, 5):
             row(c)
+        by_scalar([c for c in ON_SCALAR if c >= 10])
+        for c in (4, 3, 2, 1):
+            row(c)
+        segments(0)
+        for c in (19, 18, 17):
+            beats(c)
+        diagonal(1)
+        pack(896, 1152)
+        pack(0, 320)
+        fold(0, 0, start=True)
+        fold(0, 1, start=True)
+        fold(3, 0)
+        fold(4, 0)
+        for c in (16, 15):
+            beats(c)
+        for c in (19, 18, 17, 16):
+            row(c)
+        segments(1)
+        pack(320, 576)
+        fold(1, 0)
+        fold(1, 1)
+        pack(608, 800)
+        fold(2, 0, stop=True)
+        fold(2, 1, stop=True)
+        tt(ends("lift", 0), ends("seg", 0), at("rowW", 0, 10), Op.subtract)
+        act(at("Qs"), at("p6", 0, C))
+        total(col("rowW", 15), slot(15))
+        cp(ends("lift", 1), ends("seg", 1))
+        aside()
+        ranks(0)
+        ranks(1)
+        places(0)
+        aside()
+        tt(at("b1"), ends("Hs", 1), at("rowW", 10, 20), Op.subtract)
+        spread(0)
+        places(1)
+        prefer(0)
+        spread(1)
+        aside()
+        prefer(1)
+        scan(at("Os"), at("Ow", 0, A), at("lift4"), -DROP, Op.max, Op.add)
+        quant(at("kc"), at("ks"), at("Gc"))
+        for h, bank in enumerate(("p7", "p1")):
+            mm(bank, A, block("cq", 1 + h), block("cs", 1 + h), at("kc"), at("ks"))
+        ts(at("offM"), at("Os", 3, A, 4), 4.0, Op.mult, cc("tm"), Op.add)
+        act(at("Mt", 2 * A, 4 * A), by(at("Xt"), at("offM", 20, 40)))
+        cp(at("Mt", 0, 2 * A), by(at("Xt"), at("offM", 0, 20)))
+        for h, bank in enumerate(("p7", "p1")):
+            act(half("fk", h), at(bank, 0, A), Fn.Relu, 16.0, cc("fb"))
+        quant(qm, sm, at("Mt"))
 
-        def fold(k):
-            f0, width, blocks = TILES[k]
-            quant(T.gq[:, f0:f0 + width], T.gs[:, f0:f0 + width], T.Gt[:, 4 * f0:4 * (f0 + width)],
-                  ["G%s" % b for b in blocks], ["gq%d" % k])
-            mm("p2", width, block("cq", 0), block("cs", 0), T.gq[:, f0:f0 + width], T.gs[:, f0:f0 + width],
-               ["cq0", "gq%d" % k], start=k == 0, stop=k == len(TILES) - 1)
-
-        diag, _ = slot(None)
-        compare(9)
-        tt(diag, T.p0[:, 0:C], T.own[:], Op.is_le, ["p0", "own0", "own1"], ["GNone"])
-        for c in (17, 16, 15):
-            compare(c)
-        scan(T.seg[:], T.R16b[:], diag, 0.0, Op.mult, Op.add, ["R16b", "GNone"], ["seg"])
-        for c in (14, 13):
-            compare(c)
-        if rnd == 0:
-            quant(block("cq", 0), block("cs", 0), T.cg[:], ["cg"], ["cq0"])
-        fold(0)
-        tt(T.b1[:], T.cst[:], T.seg[:, 15:C:16], Op.subtract, ["cst", "seg"], ["b1"])
-        compare(12)
-        fold(1)
-        for c in (11, 10, 8, 7):
-            compare(c)
-        fold(2)
-        for c in (6, 5, 4, 3, 2, 1):
-            compare(c)
-        fold(3)
-        fold(4)
-        if rnd == 0:
-            ts(T.st[:], T.k32[:, 0:4], col("cols", 4), None, Op.is_equal, None, ["k32", "cols"], ["st"])
-            pick(4, 6, ["offU3", "offU4"])
-            tastes()
-        act(T.r1[:], T.p5[:, 0:C], Fn.Copy, ["p5"], ["r1"])
-        if rnd == 0:
-            scalar_constants()
-        tt(T.b2[:], T.b1[:], T.rows[:], Op.subtract, ["b1"] + ["rows%d" % c for c in range(20)], ["b2"])
-        for h, (lo, hi) in enumerate(halves):
-            tt(T.Hm[:, lo:hi], T.p2[:, lo:hi], T.m16[:, lo:hi], Op.mult, ["p2", "m16"], ["Hm%d" % h])
-        for h, (lo, hi) in enumerate(halves):
-            scan(T.Hs[:, lo:hi], T.R16[:, lo:hi], T.Hm[:, lo:hi], 0.0, Op.mult, Op.add, ["R16", "Hm%d" % h], ["Hs%d" % h])
-        if rnd == 0:
-            tick_constants(0)
-        tt(T.rk[:], T.Hs[:, 15:C:16], T.b2[:], Op.add, ["Hs0", "Hs1", "b2"], ["rk"])
-        tt(T.mx[:], T.p6[:, 0:C], T.r1[:], Op.max, ["p6", "r1"], ["mx"])
-        cp(T.offR[:], T.rk[:], ["rk"], ["offR"])
-        if rnd == 0:
-            tick_constants(1)
-        cp(T.Ow[:].indirect(T.offR[:]), T.src[:], ["offR", "src"], ["Ow"])
-        tt(T.mx[:], T.p7[:, 0:C], T.mx[:], Op.max, ["p7", "mx"], ["mx"])
-        act(T.H3[:, 3:A:4], T.Ow[:, 3:A:4], Fn.Copy, ["Ow", "st"], ["H33"], scale=col("st", 3))
-        for a in range(3):
-            ts(T.H3[:, a:A:4], T.Ow[:, a:A:4], col("st", a), None, Op.mult, None, ["Ow", "st"], ["H3%d" % a])
-        if rnd == 0:
-            tick_constants(2)
-        scan(T.H3s[:], T.R4[:], T.H3[:], 0.0, Op.mult, Op.add, ["R4", "H30", "H31", "H32", "H33"], ["H3s"])
-        if rnd == 0:
-            tick_constants(3)
-        ts(T.offM[:], T.H3s[:, 3:A:4], 4.0, col("cols", 6), Op.mult, Op.add, ["H3s", "c6"], ["offM"])
-        act(T.Mt[:, 2 * A:4 * A], T.Xt[:].indirect(T.offM[:, 20:40]), Fn.Copy, XK + ["offM"], ["Mb"])
-        cp(T.Mt[:, 0:2 * A], T.Xt[:].indirect(T.offM[:, 0:20]), XK + ["offM"], ["Ma"])
-        quant(qm[:], sm[:], T.Mt[:], ["Ma", "Mb"], ["qm"])
-
-        order("Gc", ["qm"], [])
+        order("Gc", [qm, sm], [])
         rid, pid, _ = topo.addr(peer)
-        mask = topo.mask(core, peer)
         lanes = len(topo.engines(core, peer))
         arr = "arr%d" % rnd
-        g.remote_dma(lq[:].bitcast(dt.uint8), qm[:].bitcast(dt.uint8), T.sem[arr], T.sem.sent, pid, rid, mask)
-        g.remote_dma(ls[:], sm[:], T.sem[arr], T.sem.sent, pid, rid, mask)
+        g.remote_dma(lq[0].bitcast(dt.uint8), qm[0].bitcast(dt.uint8), T.sem[arr], T.sem.sent, pid, rid, topo.mask(core, peer))
+        g.remote_dma(ls[0], sm[0], T.sem[arr], T.sem.sent, pid, rid, topo.mask(core, peer))
         count["sent"] = count.get("sent", 0) + 2 * lanes
-        writer["land"] = (arr, 2 * lanes, {arr: 2 * lanes})
-        writer.pop("qm")
+        for view in (lq, ls):
+            wrote[view[1]] = [(view[2], (arr, 2 * lanes, {arr: 2 * lanes}))]
+        if rnd == 0:
+            iota(at("jq"), [[1, A], [0, 4]])
 
+        act(at("Xh"), at("Xt"), scale=0.5)
+        scan(half("cum", 0), half("fk", 0), half("fk", 0), cc("k"), Op.add, Op.max)
         if rnd == 0:
-            tick_constants(4)
-        act(T.Xh[:], T.Xt[:], Fn.Copy, XK, ["Xh"], scale=0.5)
-        tt(diag, T.p4[:, 0:C], T.mx[:], Op.is_ge, ["p4", "mx"], ["GNone"])
-        quant(T.gq[:, 0:C], T.gs[:, 0:C], T.Gt[:, 0:4 * C], ["G%s" % b for b in TILES[0][2]], ["gq0"])
-        mm("p2", C, block("cq", 1), block("cs", 1), T.gq[:, 0:C], T.gs[:, 0:C], ["cq1", "gq0"])
-        if rnd == 0:
+            act(at("X32"), at("Xt"), scale=32.0)
+            tick_columns()
             for b in range(4):
-                unpackers(b)
-        tt(T.fk[:], T.p2[:, 0:C], diag, Op.is_lt, ["p2", "GNone"], ["fk"])
-        scan(T.cum[:], T.fk[:], T.fk[:], col("cols", 7), Op.add, Op.max, ["fk", "c7"], ["cum"])
-        ts(col("mcol", 0), col("cum", C - 1), col("cols", 7), None, Op.subtract, None, ["cum", "c7"], ["mcol"])
-
-        def standing(a):
-            tt(T.vp[:, 96 * a:96 * a + 80], T.cum[:, a:C:4], T.fk[:, a:C:4], Op.mult, ["cum", "fk"], ["vp%d" % a])
-
+                quant(block("cq", 3 + b), block("cs", 3 + b), at("ce", 3 - b, 515 - b))
+            ts(at("offY"), at("c16", 0, 6), 1.0 / 16, Op.mult, cc("a6"), Op.add)
+        scan(half("cum", 1), half("fk", 1), half("fk", 1), col("cum", A - 1), Op.add, Op.max)
+        ts(at("offm"), at("s16"), col("cum", C - 1), Op.mult, cc("mo"), Op.add)
         standing(0)
-        ts(T.offm[:], T.one14[:], col("mcol", 0), None, Op.mult, None, ["one14", "mcol"], ["offm"])
-        standing(1)
-        tt(T.Wt[:], T.tab[:].indirect(T.offm[:]), T.Call[:], Op.add,
-           ["tab", "offm", "Call"] + ["Call%d" % t for t in range(TICKS - 1)], ["Wt"])
+        tt(at("Wt"), by(at("tab"), at("offm")), at("Bv"), Op.add)
 
-        spare = [[] for _ in range(TICKS)]
-        spare[1] += [lambda: standing(2), lambda: standing(3)]
-        if rnd == 0:
-            spare[1].append(lambda: ts(T.offY[:], T.c16[:, 0:6], 1.0 / 16, col("cols", 8), Op.mult, Op.add, ["c16", "c8"], ["offY"]))
-        spare[2].append(lambda: turn(T.vT[:], T.vp[:], ["vp0", "vp1", "vp2", "vp3"], ["vT"]))
-        spare[3].append(lambda: tt(T.s01[:], T.vT[:, 0:384:16], T.vT[:, 1:384:16], Op.add, ["vT"], ["s01"]))
-        spare[3].append(lambda: tt(T.s23[:], T.vT[:, 2:384:16], T.vT[:, 3:384:16], Op.add, ["vT"], ["s23"]))
-        spare[3].append(lambda: tt(T.sa[:], T.s01[:], T.s23[:], Op.add, ["s01", "s23"], ["sa"]))
-        spare[4].append(lambda: ts(T.si[:], T.sa[:], -1.0, 16.0, Op.add, Op.mult, ["sa"], ["si"]))
-        spare[4].append(lambda: ts(T.a1[:], T.si[:], 16 * (TICKS - 1), None, Op.bitwise_and, None, ["si"], ["a1"]))
-        spare[4].append(lambda: ts(T.a2[:], T.si[:], 11, 12, Op.arith_shift_right, Op.bitwise_and, ["si"], ["a2"]))
-        spare[5].append(lambda: tt(T.s3[:], T.a1[:], T.a2[:], Op.add, ["a1", "a2"], ["s3"]))
-        spare[5].append(lambda: tt(T.Yb[:], T.s3[:].indirect(T.offY[:]), T.k32[:], Op.add, ["s3", "offY", "k32"], ["Yb"]))
-        spare[6].append(lambda: turn(T.YT[:], T.Yb[:], ["Yb"], ["YT"]))
-        spare[7].append(lambda: cp(T.offZ[:], T.YT[:, 0:80], ["YT"], ["offZ"]))
+        spare = [lambda: standing(1), lambda: standing(2), lambda: standing(3),
+                 lambda: turn(at("vT", 0, 192), at("vp", 0, 192)),
+                 lambda: turn(at("vT", 192, 384), at("vp", 192, 384)),
+                 lambda: (tt(at("s01"), at("vT", 0, 384, 16), at("vT", 1, 384, 16), Op.add),
+                          tt(at("s23"), at("vT", 2, 384, 16), at("vT", 3, 384, 16), Op.add)),
+                 lambda: tt(at("sa"), at("s01"), at("s23"), Op.add),
+                 lambda: ts(at("si"), at("sa"), 1.0 / 16, Op.mult, -16.0, Op.add),
+                 lambda: ts(at("a1"), at("si"), 16 * (TICKS - 1) + 3, Op.bitwise_and),
+                 lambda: tt(at("Yb"), by(at("a1"), at("offY")), at("k4"), Op.add),
+                 lambda: turn(at("YT"), at("Yb")),
+                 lambda: cp(at("offZ"), at("YT", 0, 80))]
         if last:
-            spare[7].append(lambda: quant(T.qv[:], T.sv[:], T.vt[:], ["vt"], ["qv"]))
+            spare.append(lambda: quant(at("qv"), at("sv"), at("vt")))
 
-        mm("p3", A, block("uq", 5), block("us", 5), lq[:], ls[:], ["uq5", "us5", "land"])
+        def next_spare():
+            if spare:
+                spare.pop(0)()
+
+        by_u("p0", 3, lq, ls, A)
         for b in range(4):
-            mm("p%d" % (4 + b), A, block("cq", 2 + b), block("cs", 2 + b), lq[:], ls[:], ["cqE%d" % b, "land"])
+            mm("p%d" % (2 + b), A, block("cq", 3 + b), block("cs", 3 + b), lq, ls)
+
+        def meals(lo, hi, first, on_vector=False):
+            out, src = at("Bm", 16 * lo, 16 * hi), by(at("Bh"), at("offB", first, first + hi - lo))
+            if on_vector:
+                cp(out, src)
+            else:
+                act(out, src)
 
         for t in range(TICKS):
-            cc = t // 4
+            meal, k = col("meal", t), t // 2
+            scan(at("rm"), at("like", 0, A) if t else at("p0", 0, A), at("kill"), -BIG, Op.max, Op.max)
+            act(at("step", 1, A + 1), at("rm"), Fn.Sign, -1.0, col("rm", A - 1), meal)
             if t == 0:
-                scan(T.rm[:, PAD:ROW], T.p3[:, 0:A], T.kill[:], -BIG, Op.max, Op.max, ["p3", "kill"], ["rm"])
+                cp(at("like", 0, A), at("p0", 0, A))
+                for b in range(4):
+                    act(at("Bh", b, 4 * A, 4), at("p%d" % (2 + b), 0, A), scale=0.5)
             else:
-                scan(T.rm[:, PAD:ROW], T.like[:, PAD:ROW], T.kill[:], -BIG, Op.max, Op.max, ["like", "kill"], ["rm"])
-            act(T.sg[:, 0:ROW], T.rm[:], Fn.Sign, ["rm"], ["sg0", "meal%d" % t], bias=col("rm", ROW - 1), scale=-1.0,
-                accum_out=col("meal", t))
-            keys = ["meal%d" % t, "st"] + (["hist%d" % (t - 1)] if t % 4 else [])
-            if t % 4 == 0:
-                act(col("hist", t), col("meal", t), Fn.Copy, keys, ["hist%d" % t], scale=col("st", 0))
-            elif t % 4 < 3:
-                affine(col("hist", t), col("meal", t), col("st", t % 4), col("hist", t - 1), keys, ["hist%d" % t])
-            if 2 <= t < 6:
-                b = t - 2
-                act(T.Bh[:, PAD + A * b:PAD + A * (b + 1)], T["p%d" % (4 + b)][:, 0:A], Fn.Copy, ["p%d" % (4 + b)],
-                    ["Bh%d" % b], scale=0.5)
-            if t == 0:
-                cp(T.like[:, PAD:ROW], T.p3[:, 0:A], ["p3"], ["like"])
-            for job in spare[t]:
-                job()
-            if t % 4 == 0:
-                ts(col("off", cc), col("meal", t), col("st", 0), None, Op.mult, None, keys, ["off"])
-            else:
-                ts(col("off", cc), col("meal", t), col("st", t % 4), col("hist", t - 1), Op.mult, Op.add, keys, ["off"])
+                next_spare()
             if t == TICKS - 1:
                 break
-            ts(T.Rw[:], T.jrow[:], col("meal", t), None, Op.is_equal, None, ["jrow", "meal%d" % t], ["Rw"])
-            n = 16 * (cc + 1)
-            tt(T.prod[:, 0:n], T.Rw[:].indirect(T.off[:, 0:cc + 1]), T.Wt[:, 32 * t:32 * t + n], Op.mult, ["Rw", "off", "Wt"], ["prod"])
-            run("V", lambda: v.tensor_reduce(col("tot", 0), T.prod[:, 0:n], AxisListType.X, Op.add), ["prod"], ["tot"])
-            ts(col("off2", 0), col("tot", 0), col("cols", 5), col("meal", t), Op.max, Op.min, ["tot", "cols", "meal%d" % t], ["off2"])
-            cp(T.like[:].indirect(T.off2[:, 0:1]), T.kill[:, 0:16], ["off2", "kill"], ["like"])
-
-        planes = ["Bhp", "Bh0", "Bh1", "Bh2", "Bh3", "off"]
-        for b in (1, 3):
-            act(T.Bm[:, b:128:4], T.Bh[:, A * b:A * b + ROW].indirect(T.off[:]), Fn.Copy, planes, ["Bm%d" % b])
-        for b in (0, 2):
-            cp(T.Bm[:, b:128:4], T.Bh[:, A * b:A * b + ROW].indirect(T.off[:]), planes, ["Bm%d" % b])
-
-        def take(lo, hi, key):
-            tt(T.Zt[:, 4 * lo:4 * hi], T.Bm[:].indirect(T.offZ[:, lo // 4:hi // 4]), T.Xh[:, 4 * lo:4 * hi], Op.add,
-               ["Bm0", "Bm1", "Bm2", "Bm3", "offZ", "Xh"], [key])
-
-        def layer(h, keys):
-            lo, hi = halves[h]
-            quant(T.qz[:, lo:hi], T.sz[:, lo:hi], T.Zt[:, 4 * lo:4 * hi], keys, ["qz%d" % h])
-            for b in range(4):
-                mm("p%d" % (4 * h + b), A, block("wq", b), block("wp", b), T.qz[:, lo:hi], T.sz[:, lo:hi],
-                   ["wq", "wp", "qz%d" % h])
-
-        def grow(k):
-            h, b = k // 4, k % 4
-            big = T.X32[:, 4 * A * h + b:4 * A * (h + 1):4]
-            tt(big, T["p%d" % k][:, 0:A], big, Op.add, ["p%d" % k, X32K[k]], [X32K[k]])
-
-        def shrink(k, on_vector):
-            h, b = k // 4, k % 4
-            big = T.X32[:, 4 * A * h + b:4 * A * (h + 1):4]
-            new = T.Xt[:, 4 * A * h + b:4 * A * (h + 1):4]
-            if on_vector:
-                ts(new, big, 1.0 / 32, None, Op.mult, None, [X32K[k]], [XK[k]])
+            if t % 2 == 0:
+                ts(col("off", k), meal, cc("even"), Op.mult, cc("one"), Op.add)
+                if t < TICKS - 2:
+                    affine(col("hist", k), meal, cc("even"), cc("odd"))
             else:
-                act(new, big, Fn.Copy, [X32K[k]], [XK[k]], scale=1.0 / 32)
+                ts(col("off", k), meal, cc("late"), Op.mult, col("hist", k), Op.add)
+            ts(col("offB", t), meal, 4.0, Op.mult, cc("a"), Op.add)
+            n = 16 * (k + 1)
+            tt(at("prod", 0, n), by(at("step"), at("off", 0, k + 1)), at("Wt", 0, n), Op.mult)
+            if t % 2:
+                meals(t - 1, t + 1, t - 1)
+            elif t == TICKS - 2:
+                meals(t, t + 1, t)
+            scan(at("tot", 0, n), at("prod", 0, n), at("nil", 0, n), cc("lim"), Op.add, Op.add)
+            ts(col("off2", 0), col("tot", n - 1), meal, Op.max, cc("pad"), Op.min)
+            if t:
+                next_spare()
+            cp(by(at("like"), col("off2", 0)), at("kill", 0, 16))
 
-        take(0, A, "Z0")
-        take(A, A + 48, "Z1")
-        layer(0, ["Z0"])
-        take(A + 48, C, "Z2")
+        ts(col("offB", TICKS), meal, 4.0, Op.mult, cc("a"), Op.add)
+        meals(TICKS - 1, TICKS, TICKS, True)
         if last:
-            for t in range(4):
-                act(T.idt[:, t:128:4], T.tab[:].indirect(T.off[:]), Fn.Identity, ["tab", "off"], ["idt%d" % t],
-                    scale=1.0 / UNIT, bias=-float(PAD))
-            act(T.olw[:], T.idt[:].indirect(T.offZ[:]), Fn.Copy, ["idt0", "idt1", "idt2", "idt3", "offZ"], ["olw"])
+            act(at("idt", 0, 112), by(at("jq"), at("offB", 0, TICKS - 1)))
+            act(at("idt", 112, 128), by(at("jq"), col("offB", TICKS)))
+            act(at("olw"), by(at("idt"), at("offZ")))
+        take(0, A)
+        take(A, A + 48)
+        layer(0)
+        take(A + 48, C)
         grow(0)
-        shrink(0, False)
-        layer(1, ["Z1", "Z2"])
-        for k in range(1, 8):
+        shrink(0)
+        layer(1)
+        for k in range(1, 6):
             grow(k)
-            if k < 6:
-                shrink(k, False)
-        side = (T.qv[:], T.sv[:], ["qv"]) if last else (block("uq", 0), block("us", 0), ["uq0", "us0"])
-        quant(T.qx[:, 0:A], T.sx[:, 0:A], T.Xt[:, 0:4 * A], XK[0:4], ["qx", "qx0"])
-        mm("p2", A, side[0], side[1], T.qx[:, 0:A], T.sx[:, 0:A], side[2] + ["qx0"])
+            shrink(k)
+        scores(0, last)
+        grow(6)
+        grow(7)
         shrink(6, True)
         shrink(7, True)
-        quant(T.qx[:, A:C], T.sx[:, A:C], T.Xt[:, 4 * A:4 * C], XK[4:8], ["qx"])
-        mm("p3", A, side[0], side[1], T.qx[:, A:C], T.sx[:, A:C], side[2] + ["qx"])
+        if not last:
+            mask(0)
+            scores(1, last)
+            hold(0)
+            tastes()
 
-    act(T.olr[:], T.olw[:, 0:4 * C:4], Fn.Copy, ["olw"], ["olr"])
-    dma("Y", "stored", T.oc[:], T.qx[:].bitcast(dt.uint8), ["qx"], [])
-    cp(T.ys[:, 0:A], T.p2[:, 0:A], ["p2"], ["ys0"])
-    cp(T.ys[:, A:C], T.p3[:, 0:A], ["p3"], ["ys1"])
-    dma("S", "stored", T.ol[:], T.olr[0:128:16, :], ["olr"], [])
-    dma("Y", "stored", T.y[:], T.ys[:], ["ys0", "ys1"], [])
+    def results(h):
+        store("Y", T.oc[:, 4 * A * h:4 * A * (h + 1)], half("qx", h), half("qx", h)[0].bitcast(dt.uint8))
+
+    def product(h):
+        cp(half("ys", h), at(score[h], 0, A))
+        store("Y", T.y[:, A * h:A * (h + 1)], half("ys", h), half("ys", h)[0])
+
+    act(at("olr"), at("olw", 0, 4 * C, 4))
+    results(0)
+    store("S", T.ol[:], at("olr"), T.olr[0:128:16, :])
+    product(0)
+    scores(1, True)
+    results(1)
     for k in range(4):
-        dma("S", "stored", T.osc[4 * k:4 * k + 4, :], T.sx[32 * k:32 * k + 4, :], ["qx"], [])
+        store("S", T.osc[4 * k:4 * k + 4, :], at("sx"), T.sx[32 * k:32 * k + 4, :])
+    product(1)
     for sem in ("Gc", "sent", "S", "P", "V"):
         g.wait_ge(T.sem[sem], count[sem])
     g.sync.wait_ge(T.sem.stored, count["stored"])

@@ -14,14 +14,14 @@ ON_SCALAR = (9, 8, 7, 14, 13, 12, 11, 10)
 
 F32, BF, I32, U16, CODE, U8 = "float32", "bfloat16", "int32", "uint16", "float8_e4m3fn_x4", "uint8"
 SIZES = {
-    BF: dict(Xt=4 * C, X32=4 * C, Xh=4 * C, Zt=4 * C, Mt=4 * A, ut=512, vt=512, ones=516, cg=512, ck=516, ce=516, g128=128,
-             Gt=4 * WIDE, Gc=4 * A, junk=3072, step=A + 16, Bh=4 * A, Bm=128, kq=128),
-    F32: dict(j16=A, j4=A, c16=20, k128=128, k4=96, sgn=64, Bv=64, tab=2 * TAB, jq=4 * A, src=C, cols=32, K1=A, R1=A, Rc=C,
-              lift=C, lift4=A, msk=C, own=C, seg=C, rowW=20, b1=10, Hs=C, Ow=C, Os=A, Qs=C, fk=C, cum=C, s16=4,
-              Wt=64, vp=384, vT=384, s01=24, s23=24, sa=24, Yb=96, YT=96, like=A + 16, rm=A, kill=A, meal=8, hist=4,
-              prod=64, nil=64, tot=64, idt=128, olw=4 * C, olr=C, ys=C),
+    BF: dict(Xt=4 * C, X32=4 * C, Xh=4 * C, Zt=4 * C, Mt=4 * A, ut=512, vt=512, ones=4 * A, cg=512, ck=516, ce=516,
+             g128=128, Gt=4 * WIDE, Gc=4 * A, junk=3072, step=A + 16, Bh=4 * A, Bm=128, kq=128),
+    F32: dict(j16=A, j4=80, c16=20, k128=128, k4=32, sgn=16, Bv=16, tab=2 * TAB, jq=4 * A, src=C, cols=32, K1=80, R1=80,
+              Rc=C, lift=C, lift4=80, msk=C, own=C, seg=C, rowW=20, b1=10, Hs=C, Ow=C, Os=A, Qs=C, fk=C, cum=C,
+              Wt=16, Wc=16, Wk=16, alive=16, vp=384, vT=384, s01=24, s23=24, sa=24, Yb=96, YT=96, like=A + 16, rm=A,
+              kill=A, meal=8, prod=16, nil=16, tot=16, idt=128, olw=4 * C, olr=C, ys=C),
     I32: dict(pi=1, pt=8, si=24, a1=24),
-    U16: dict(offU=32, offR=20, offM=40, offm=4, offY=6, offZ=80, off=4, off2=2, offB=10),
+    U16: dict(offU=32, offR=20, offM=40, offm=2, offY=6, offZ=80, off=4, off2=2, offB=10),
     CODE: dict(qx=C, qz=C, qu=128, qv=128, uq=512, wq=512, cq=896, gq=WIDE, kc=A),
     U8: dict(sx=C, sz=C, su=128, sv=128, us=512, wp=512, cs=896, gs=WIDE, ks=A),
 }
@@ -32,8 +32,8 @@ SCRATCH = {_n: ("sbuf", [128, _w], _d) for _d in SIZES for _n, _w in SIZES[_d].i
 for _b in range(8):
     SCRATCH["p%d" % _b] = ("psum", [128, 512], F32)
 
-SEMAPHORES = ["V", "S", "P", "Gc", "ldx0", "ldx1", "ldu", "ldw", "lds", "ldv", "sent", "arr0", "arr1", "arr2", "stored"]
-COLS = ["k", "a", "q", "g", "odd", "q4", "q0", "a4", "a3", "rc", "tm", "mo", "even", "late", "one", "lim", "pad", "fb",
+SEMAPHORES = ["V", "S", "P", "Gc", "ldx", "ldu", "ldw", "lds", "ldv", "sent", "arr0", "arr1", "arr2", "stored"]
+COLS = ["k", "a", "q", "g", "odd", "q0", "a4", "a3", "rc", "tm", "mo", "even", "one", "lim", "pad", "fb",
         "a6", "s", "w", "kp", "lo", "hi", "sg0", "sg", "l0", "l1"]
 
 
@@ -183,88 +183,102 @@ def rank_program(g, core, T, topo):
     def iota(out, pattern, base=0):
         run("Gc", lambda: g.iota(out[0], pattern, base, 0, allow_small_or_imprecise_dtypes=True), [], [out])
 
-    def pick(lo, hi):
-        offs = at("offU", 8 * lo, 8 * hi)
-        cp(words(at("uq", 128 * lo, 128 * hi)), words(at("qu"), offs))
-        out, src = at("us", 128 * lo, 128 * hi), by(at("su"), offs)
+    def pick(j):
+        offs = at("offU", 8 * j, 8 * j + 8)
+        cp(words(block("uq", j)), words(at("qu"), offs))
+        out, src = block("us", j), by(at("su"), offs)
         run("S", lambda: s.activation(out[0], src[0], Fn.Copy), [src], [out])
 
     def by_u(bank, j, rq, rs, n):
         mm(bank, n, block("uq", j), block("us", j), rq, rs)
 
     load("S", "ldu", at("ut"), T.ut[:], T.u[:])
-    for h in range(2):
-        load("Y", "ldx%d" % h, half("Xt", h, 4), half("Xt", h, 4)[0], T.x[:, 4 * A * h:4 * A * (h + 1)])
+    load("Y", "ldx", at("Xt"), T.Xt[:], T.x[:])
     order("Y", [at("Xt")], [])
     load("Y", "ldw", at("wq"), T.wq[:].bitcast(dt.uint8), T.wc[:])
     load("Y", "lds", at("wp"), T.wp[:], T.ws[:])
     load("Y", "ldv", at("vt"), T.vt[:], T.v[:])
 
-    fill(at("ones"), 1.0)
     run("Gc", lambda: g.iota(T.pi[:], [[1, 1]], 0, 1), [], [at("pi")])
     iota(at("c16"), [[16, 20]])
     iota(at("j16"), [[0, 10], [int(DROP), 16]])
     iota(at("g128"), [[1, 8], [0, 16]])
     iota(at("k128"), [[0, 32], [1, 4]])
-    iota(at("j4"), [[0, 40], [int(DROP), 4]])
-    iota(at("sgn"), [[0, 8], [-2, 2], [0, 4]], 1)
     iota(at("src"), [[1, C]])
-    run("Gc", lambda: g.affine_select(T.ce[:], T.ones[:], [[-1, 516]], Op.is_equal, 0.0, 3, 4), [at("ones")], [at("ce")])
+    iota(at("j4"), [[0, 20], [int(DROP), 4]])
+    iota(at("sgn"), [[0, 2], [-2, 2], [0, 4]], 1)
+
+    fill(at("ones"), 1.0)
+    run("Gc", lambda: g.affine_select(T.ce[:], T.ones[:, 0:516], [[-1, 516]], Op.is_equal, 0.0, 3, 4), [at("ones")], [at("ce")])
     iota(at("tab", 0, TAB), [[-UNIT, TAB]])
     iota(at("tab", TAB, 2 * TAB), [[UNIT, TAB]])
-
-    fill(at("Gc"), 0.0)
+    fill(at("Zt", 0, 512), 0.0)
     for j, (shift, keep) in enumerate([(0, 3), (2, 3), (0, 15), (4, 7), (2, 1)]):
         ts(col("pt", j), at("pi"), shift, Op.logical_shift_right, keep, Op.bitwise_and)
     cp(at("offU", 0, 8), at("c16", 0, 8))
-    put(at("Rc"), C, -BIG)
-    put(at("ck"), 516, 0.0)
-    for first, width, blocks in TILES[:3]:
-        fill(at("Gt", 4 * (first + 16 * blocks[3]), 4 * (first + 16 * blocks[3] + 48)), 0.0)
+    for first, width, blocks in TILES:
+        put(at("Gt", 4 * (first + 16 * blocks[3]), 4 * (first + 16 * blocks[3] + 48)), 192, 0.0)
+    ts(cc("q0"), col("pt", 2), DROP, Op.mult)
     cp(at("cols", 0, 5), at("pt", 0, 5))
-    for first, width, blocks in TILES[3:]:
-        fill(at("Gt", 4 * (first + 16 * blocks[3]), 4 * (first + width)), 0.0)
-    affine(cc("q0"), cc("q"), DROP, 0.0)
-    affine(cc("q4"), cc("q"), DROP, -LIFT)
-    affine(cc("rc"), cc("q"), LIFT - 1, 15 - 15 * LIFT - DROP)
-    affine(cc("l0"), cc("k"), 1.0, 4.0)
-    act(at("R1"), at("j16"), Fn.Sign)
-    affine(cc("a4"), cc("a"), DROP, -LIFT)
-    affine(cc("a3"), cc("a"), LIFT, -3 * LIFT - DROP)
-    affine(cc("tm"), cc("k"), 1.0, 4 * DROP)
-    affine(at("R1"), at("R1"), 2 * BIG, -BIG)
-    affine(at("Rc", 0, C, 16), at("c16"), 1.0, cc("rc"))
-    put(at("rowW"), 20, 0.0)
-
-    ts(cc("s"), cc("a"), 1.0, Op.max, cc("k"), Op.add)
-    for t in range(4):
-        ts(at("cg", t, 512, 4), at("g128"), cc("g"), Op.is_equal)
-    ts(cc("w"), cc("s"), 4.0, Op.is_ge, -4.0, Op.mult)
-    ts(at("K1"), at("j16"), cc("q0"), Op.not_equal, -2 * BIG, Op.mult)
-    quant(block("cq", 0), block("cs", 0), at("cg"))
-    ts(cc("kp"), cc("w"), cc("s"), Op.add, 4.0, Op.add)
-    ts(cc("sg0"), cc("w"), 0.5, Op.mult, 1.0, Op.add)
-    ts(at("offU", 24, 32), at("c16", 0, 8), cc("k"), Op.add, 8.0, Op.add)
-    for first, width, blocks in TILES[1:3]:
-        quant(at("gq", first + A, first + width), at("gs", first + A, first + width), at("Gc", 0, 4 * (width - A)))
-    ts(cc("lo"), cc("kp"), cc("l0"), Op.min)
-    ts(cc("hi"), cc("kp"), cc("l0"), Op.max)
-    ts(cc("sg"), cc("a"), 1.0, Op.min, cc("sg0"), Op.mult)
+    for first in (TILES[1][0] + A, TILES[2][0] + A, TILES[4][0]):
+        quant(at("gq", first, first + 128), at("gs", first, first + 128), at("Zt", 0, 512))
+    act(at("R1"), at("j16", 0, 80), Fn.Sign)
     quant(at("qu"), at("su"), at("ut"))
-    ts(at("offU", 8, 16), at("c16", 0, 8), cc("lo"), Op.add)
-    ts(at("offU", 16, 24), at("c16", 0, 8), cc("hi"), Op.add)
-    pick(0, 1)
+    affine(cc("a4"), cc("a"), DROP, -LIFT)
+    act(at("Hs", 0, A), at("j16"), Fn.Relu, -1.0, cc("q0"))
+    ts(at("K1"), at("j16", 0, 80), cc("q0"), Op.not_equal, -2 * BIG, Op.mult)
+    ts(cc("s"), cc("a"), 1.0, Op.max, cc("k"), Op.add)
+    pick(0)
+    for h in range(2):
+        quant(half("qx", h), half("sx", h), half("Xt", h, 4))
+    affine(at("R1"), at("R1"), 2 * BIG, -BIG)
+    for h in range(2):
+        affine(half("lift", h), at("Hs", 0, A), -1.0, LIFT)
+    affine(cc("rc"), cc("q"), LIFT - 1, 15 - 15 * LIFT - DROP)
+    put(at("Rc"), C, -BIG)
+    affine(cc("l0"), cc("k"), 1.0, 4.0)
+    put(at("rowW"), 20, 0.0)
+    affine(at("Rc", 0, C, 16), at("c16"), 1.0, cc("rc"))
 
-    def class_constants():
-        ts(at("kq"), at("k128"), cc("k"), Op.is_equal, cc("sg"), Op.mult)
+    def later_constants():
+        for t in range(4):
+            ts(at("cg", t, 512, 4), at("g128"), cc("g"), Op.is_equal)
+        ts(cc("w"), cc("s"), 4.0, Op.is_ge, -4.0, Op.mult)
         ts(at("lift4"), at("j4"), cc("a4"), Op.subtract, LIFT, Op.min)
         yield
+        affine(cc("a3"), cc("a"), LIFT, -3 * LIFT - DROP)
+        affine(cc("tm"), cc("k"), 1.0, 4 * DROP)
+        ts(cc("kp"), cc("w"), cc("s"), Op.add, 4.0, Op.add)
+        yield
+        quant(block("cq", 0), block("cs", 0), at("cg"))
+        yield
+        ts(cc("lo"), cc("kp"), cc("l0"), Op.min)
+        ts(cc("hi"), cc("kp"), cc("l0"), Op.max)
+        put(at("lift4", 3, 80, 4), 20, cc("a3"))
+        put(at("ck"), 516, 0.0)
+        put(at("Gc"), 4 * A, 0.0)
+        yield
+        ts(at("offU", 8, 16), at("c16", 0, 8), cc("lo"), Op.add)
+        ts(at("offU", 16, 24), at("c16", 0, 8), cc("hi"), Op.add)
+        yield
+        ts(cc("sg0"), cc("w"), 0.5, Op.mult, 1.0, Op.add)
+        yield
+        pick(1)
+        yield
+        pick(2)
+        tastes()
+        act(half("X32", 0, 4), half("Xt", 0, 4), scale=32.0)
+        yield
+        ts(cc("sg"), cc("a"), 1.0, Op.min, cc("sg0"), Op.mult)
+        ts(at("offU", 24, 32), at("c16", 0, 8), cc("k"), Op.add, 8.0, Op.add)
+        yield
+        ts(at("kq"), at("k128"), cc("k"), Op.is_equal, cc("sg"), Op.mult)
+        yield
         tt(at("ck", 1, 513, 4), at("kq"), at("cg", 0, 512, 4), Op.mult)
-        put(at("lift4", 3, A, 4), 40, cc("a3"))
         yield
         for h in range(2):
             quant(block("cq", 1 + h), block("cs", 1 + h), at("ck", 1 - h, 513 - h))
-            yield
+        yield
 
     def tick_constants():
         affine(cc("fb"), cc("k"), 16.0, -32.0)
@@ -274,18 +288,16 @@ def rank_program(g, core, T, topo):
         put(at("kill"), A, -BIG)
         put(at("like", A, A + 16), 16, -BIG)
         put(at("step", 0, 1), 1, 1.0)
-        put(at("nil"), 64, 0.0)
-        put(at("s16"), 4, 1.0 / 16)
-        act(at("k4"), at("k128", 0, 96), scale=4.0)
+        put(at("nil"), 16, 0.0)
+        act(at("k4"), at("k128", 0, 32), scale=4.0)
         affine(cc("pad"), cc("q"), 1.0, float(A))
         affine(cc("a6"), cc("a"), 6.0, 0.0)
         affine(cc("mo"), cc("odd"), float(TAB), cc("l1"))
         affine(cc("lim"), cc("lim"), VETO, (LIFE - 0.5) * UNIT)
 
     def tick_columns():
-        ts(at("Bv"), at("k128", 0, 64), cc("k"), Op.is_lt, VETO, Op.mult)
+        ts(at("Bv"), at("k128", 0, 16), cc("k"), Op.is_lt, VETO, Op.mult)
         ts(cc("even"), cc("a"), 2.0, Op.is_lt)
-        ts(cc("late"), cc("a"), 2.0, Op.is_ge)
         ts(cc("one"), cc("a"), 1.0, Op.is_equal)
         tt(at("Bv"), at("Bv"), at("sgn"), Op.mult)
 
@@ -300,11 +312,14 @@ def rank_program(g, core, T, topo):
     score = ("p0", "p7")
 
     def scores(h, last):
-        quant(half("qx", h), half("sx", h), half("Xt", h, 4))
+        quant(piece("qx", h), piece("sx", h), piece("Xt", h, 4))
         if last:
-            mm(score[h], A, at("qv"), at("sv"), half("qx", h), half("sx", h))
+            mm(score[h], cut[1], at("qv"), at("sv"), piece("qx", h), piece("sx", h))
             return
         by_u(score[h], 0, half("qx", h), half("sx", h), A)
+        copies(h)
+
+    def copies(h):
         if h == 0:
             by_u("p3", 0, half("qx", 0), half("sx", 0), A)
         else:
@@ -315,11 +330,16 @@ def rank_program(g, core, T, topo):
         by_u("p6", 2, at("qx"), at("sx"), C)
         by_u("p5", 1, at("qx"), at("sx"), C)
 
+    def quarters(h):
+        return (0, 80) if h else (80, 0)
+
     def mask(h):
-        tt(half("msk", h), at(score[h], 0, A), at("K1"), Op.add)
+        for lo in quarters(h):
+            tt(at("msk", A * h + lo, A * h + lo + 80), at(score[h], lo, lo + 80), at("K1"), Op.add)
 
     def hold(h):
-        scan(half("own", h), at("R1"), half("msk", h), -BIG, Op.min, Op.max)
+        for lo in quarters(h):
+            scan(at("own", A * h + lo, A * h + lo + 80), at("R1"), at("msk", A * h + lo, A * h + lo + 80), -BIG, Op.min, Op.max)
 
     def own(c):
         return col("own", 16 * c + 15)
@@ -346,11 +366,11 @@ def rank_program(g, core, T, topo):
             act(spare_room(c), slot(c), total=col("rowW", c))
 
     def by_scalar(blocks):
-        for i, c in enumerate(blocks):
-            beats(c)
-            if i:
-                row(blocks[i - 1])
-        row(blocks[-1])
+        for i in range(len(blocks) + 2):
+            if i < len(blocks):
+                beats(blocks[i])
+            if i >= 2:
+                row(blocks[i - 2])
 
     def pack(lo, hi):
         quant(at("gq", lo, hi), at("gs", lo, hi), at("Gt", 4 * lo, 4 * hi))
@@ -375,85 +395,103 @@ def rank_program(g, core, T, topo):
     def prefer(h):
         tt(at("Gc", h, 4 * A, 4), at("p5", A * h, A * (h + 1)), half("Qs", h), Op.is_ge)
 
+    def classes():
+        quant(at("kc"), at("ks"), at("Gc"))
+        for h, bank in enumerate(("p7", "p1")):
+            mm(bank, A, block("cq", 1 + h), block("cs", 1 + h), at("kc"), at("ks"))
+
+    def members():
+        for h, bank in enumerate(("p7", "p1")):
+            act(half("fk", h), at(bank, 0, A), Fn.Relu, 16.0, cc("fb"))
+
     def standing(a):
         tt(at("vp", 96 * a, 96 * a + 80), at("cum", a, C, 4), at("fk", a, C, 4), Op.mult)
 
     def take(lo, hi):
         tt(at("Zt", 4 * lo, 4 * hi), by(at("Bm"), at("offZ", lo // 4, hi // 4)), at("Xh", 4 * lo, 4 * hi), Op.add)
 
+    cut = [0, A, C]
+
+    def piece(name, h, k=1):
+        return at(name, k * cut[h], k * cut[h + 1])
+
     def layer(h):
-        quant(half("qz", h), half("sz", h), half("Zt", h, 4))
+        quant(piece("qz", h), piece("sz", h), piece("Zt", h, 4))
         for b in range(4):
-            mm("p%d" % (4 * h + b), A, block("wq", b), block("wp", b), half("qz", h), half("sz", h))
+            mm("p%d" % (4 * h + b), cut[h + 1] - cut[h], block("wq", b), block("wp", b), piece("qz", h), piece("sz", h))
 
     def plane(name, k):
-        return at(name, 4 * A * (k // 4) + k % 4, 4 * A * (k // 4 + 1), 4)
+        return at(name, 4 * cut[k // 4] + k % 4, 4 * cut[k // 4 + 1], 4)
 
     def grow(k):
-        tt(plane("X32", k), at("p%d" % k, 0, A), plane("X32", k), Op.add)
+        tt(plane("X32", k), at("p%d" % k, 0, cut[k // 4 + 1] - cut[k // 4]), plane("X32", k), Op.add)
 
-    def shrink(k, on_vector=False):
-        if on_vector:
+    def shrink(k):
+        if k % 4 >= 2:
             ts(plane("Xt", k), plane("X32", k), 1.0 / 32, Op.mult)
         else:
             act(plane("Xt", k), plane("X32", k), scale=1.0 / 32)
 
-    scores(0, False)
-    scores(1, False)
-    pick(1, 4)
-    tick_constants()
-    mask(0)
+    setup = later_constants()
+
+    def aside():
+        next(setup, None)
+
     for h in range(2):
-        ts(half("lift", h), at("j16"), cc("q4"), Op.subtract, LIFT, Op.min)
+        by_u(score[h], 0, half("qx", h), half("sx", h), A)
+    copies(0)
+    copies(1)
+    aside()
+    mask(0)
+    mask(1)
+    aside()
     hold(0)
-    tastes()
-    setup = class_constants()
+    hold(1)
 
     for rnd, step in enumerate(STEPS):
         last = rnd == len(STEPS) - 1
         peer = T.cores[rank ^ step]
         qm, sm, lq, ls = [at(n % rnd) for n in ("qm%d", "sm%d", "lq%d", "ls%d")]
 
-        def aside():
-            next(setup, None)
-
         aside()
-        by_scalar([c for c in ON_SCALAR if c < 10])
+        by_scalar(ON_SCALAR[:3])
+        beats(6)
         diagonal(0)
-        for c in (6, 5):
+        if rnd:
+            mask(1)
+        for c in (5, 4, 3):
             beats(c)
-        mask(1)
-        for c in (4, 3, 2, 1):
+        if rnd:
+            hold(1)
+        row(6)
+        for c in (2, 1):
             beats(c)
-        hold(1)
-        for c in (6, 5):
-            row(c)
-        by_scalar([c for c in ON_SCALAR if c >= 10])
-        for c in (4, 3, 2, 1):
-            row(c)
         segments(0)
+        by_scalar(ON_SCALAR[3:])
+        for c in (5, 4, 3, 2, 1):
+            row(c)
         for c in (19, 18, 17):
             beats(c)
         diagonal(1)
-        pack(896, 1152)
+        for c in (16, 15):
+            beats(c)
         pack(0, 320)
         fold(0, 0, start=True)
         fold(0, 1, start=True)
+        pack(896, 1088)
         fold(3, 0)
         fold(4, 0)
-        for c in (16, 15):
-            beats(c)
         for c in (19, 18, 17, 16):
             row(c)
-        segments(1)
         pack(320, 576)
         fold(1, 0)
-        fold(1, 1)
         pack(608, 800)
         fold(2, 0, stop=True)
+        fold(1, 1)
         fold(2, 1, stop=True)
+        segments(1)
+        aside()
         tt(ends("lift", 0), ends("seg", 0), at("rowW", 0, 10), Op.subtract)
-        act(at("Qs"), at("p6", 0, C))
         total(col("rowW", 15), slot(15))
         cp(ends("lift", 1), ends("seg", 1))
         aside()
@@ -464,19 +502,26 @@ def rank_program(g, core, T, topo):
         tt(at("b1"), ends("Hs", 1), at("rowW", 10, 20), Op.subtract)
         spread(0)
         places(1)
-        prefer(0)
+        aside()
+        if rnd:
+            act(at("Qs"), at("p6", 0, C))
+            prefer(0)
         spread(1)
         aside()
-        prefer(1)
-        scan(at("Os"), at("Ow", 0, A), at("lift4"), -DROP, Op.max, Op.add)
-        quant(at("kc"), at("ks"), at("Gc"))
-        for h, bank in enumerate(("p7", "p1")):
-            mm(bank, A, block("cq", 1 + h), block("cs", 1 + h), at("kc"), at("ks"))
-        ts(at("offM"), at("Os", 3, A, 4), 4.0, Op.mult, cc("tm"), Op.add)
+        if rnd:
+            prefer(1)
+        for lo in (80, 0):
+            scan(at("Os", lo, lo + 80), at("Ow", lo, lo + 80), at("lift4"), -DROP, Op.max, Op.add)
+        aside()
+        for lo in (20, 0):
+            ts(at("offM", lo, lo + 20), at("Os", 4 * lo + 3, 4 * lo + 80, 4), 4.0, Op.mult, cc("tm"), Op.add)
+        if rnd:
+            classes()
+        aside()
         act(at("Mt", 2 * A, 4 * A), by(at("Xt"), at("offM", 20, 40)))
         cp(at("Mt", 0, 2 * A), by(at("Xt"), at("offM", 0, 20)))
-        for h, bank in enumerate(("p7", "p1")):
-            act(half("fk", h), at(bank, 0, A), Fn.Relu, 16.0, cc("fb"))
+        if rnd:
+            members()
         quant(qm, sm, at("Mt"))
 
         order("Gc", [qm, sm], [])
@@ -491,36 +536,50 @@ def rank_program(g, core, T, topo):
         if rnd == 0:
             iota(at("jq"), [[1, A], [0, 4]])
 
-        act(at("Xh"), at("Xt"), scale=0.5)
-        scan(half("cum", 0), half("fk", 0), half("fk", 0), cc("k"), Op.add, Op.max)
         if rnd == 0:
-            act(at("X32"), at("Xt"), scale=32.0)
+            aside()
+            act(at("Qs"), at("p6", 0, C))
+            pick(3)
+            tick_constants()
+            aside()
+            prefer(0)
+            prefer(1)
             tick_columns()
             for b in range(4):
                 quant(block("cq", 3 + b), block("cs", 3 + b), at("ce", 3 - b, 515 - b))
+                if b == 1:
+                    classes()
+                    members()
             ts(at("offY"), at("c16", 0, 6), 1.0 / 16, Op.mult, cc("a6"), Op.add)
+        act(at("Xh"), at("Xt"), scale=0.5)
+        if rnd == 0:
+            act(half("X32", 1, 4), half("Xt", 1, 4), scale=32.0)
+        scan(half("cum", 0), half("fk", 0), half("fk", 0), cc("k"), Op.add, Op.max)
         scan(half("cum", 1), half("fk", 1), half("fk", 1), col("cum", A - 1), Op.add, Op.max)
-        ts(at("offm"), at("s16"), col("cum", C - 1), Op.mult, cc("mo"), Op.add)
+        ts(col("offm", 0), col("cum", C - 1), 1.0 / 16, Op.mult, cc("mo"), Op.add)
         standing(0)
-        tt(at("Wt"), by(at("tab"), at("offm")), at("Bv"), Op.add)
+        tt(at("Wt"), by(at("tab"), col("offm", 0)), at("Bv"), Op.add)
+
+        def index(c):
+            tt(at("Yb", 16 * c, 16 * c + 32), by(at("a1"), at("offY", c, c + 2)), at("k4"), Op.add)
 
         spare = [lambda: standing(1), lambda: standing(2), lambda: standing(3),
-                 lambda: turn(at("vT", 0, 192), at("vp", 0, 192)),
-                 lambda: turn(at("vT", 192, 384), at("vp", 192, 384)),
-                 lambda: (tt(at("s01"), at("vT", 0, 384, 16), at("vT", 1, 384, 16), Op.add),
-                          tt(at("s23"), at("vT", 2, 384, 16), at("vT", 3, 384, 16), Op.add)),
+                 lambda: turn(at("vT", 0, 192), at("vp", 0, 192)), lambda: turn(at("vT", 192, 384), at("vp", 192, 384)), None,
+                 lambda: tt(at("s01"), at("vT", 0, 384, 16), at("vT", 1, 384, 16), Op.add),
+                 lambda: tt(at("s23"), at("vT", 2, 384, 16), at("vT", 3, 384, 16), Op.add),
                  lambda: tt(at("sa"), at("s01"), at("s23"), Op.add),
                  lambda: ts(at("si"), at("sa"), 1.0 / 16, Op.mult, -16.0, Op.add),
                  lambda: ts(at("a1"), at("si"), 16 * (TICKS - 1) + 3, Op.bitwise_and),
-                 lambda: tt(at("Yb"), by(at("a1"), at("offY")), at("k4"), Op.add),
-                 lambda: turn(at("YT"), at("Yb")),
+                 lambda: index(0), lambda: index(2), lambda: index(4), None,
+                 lambda: turn(at("YT"), at("Yb")), None,
                  lambda: cp(at("offZ"), at("YT", 0, 80))]
         if last:
             spare.append(lambda: quant(at("qv"), at("sv"), at("vt")))
 
         def next_spare():
-            if spare:
-                spare.pop(0)()
+            job = spare.pop(0) if spare else None
+            if job:
+                job()
 
         by_u("p0", 3, lq, ls, A)
         for b in range(4):
@@ -534,34 +593,34 @@ def rank_program(g, core, T, topo):
                 act(out, src)
 
         for t in range(TICKS):
-            meal, k = col("meal", t), t // 2
+            meal = col("meal", t)
+            if 0 < t < TICKS - 1:
+                act(at("alive"), by(at("like"), col("off", 2)), Fn.Sign, 1.0, BIG)
             scan(at("rm"), at("like", 0, A) if t else at("p0", 0, A), at("kill"), -BIG, Op.max, Op.max)
             act(at("step", 1, A + 1), at("rm"), Fn.Sign, -1.0, col("rm", A - 1), meal)
             if t == 0:
                 cp(at("like", 0, A), at("p0", 0, A))
                 for b in range(4):
                     act(at("Bh", b, 4 * A, 4), at("p%d" % (2 + b), 0, A), scale=0.5)
-            else:
-                next_spare()
             if t == TICKS - 1:
                 break
-            if t % 2 == 0:
-                ts(col("off", k), meal, cc("even"), Op.mult, cc("one"), Op.add)
-                if t < TICKS - 2:
-                    affine(col("hist", k), meal, cc("even"), cc("odd"))
-            else:
-                ts(col("off", k), meal, cc("late"), Op.mult, col("hist", k), Op.add)
+            if t:
+                tt(at("Wk"), at("Wc") if t > 1 else at("Wt"), at("alive"), Op.mult)
+                tt(at("Wc"), at("Wk"), at("Wt"), Op.add)
+            ts(col("off", 0), meal, cc("even"), Op.mult, cc("one"), Op.add)
             ts(col("offB", t), meal, 4.0, Op.mult, cc("a"), Op.add)
-            n = 16 * (k + 1)
-            tt(at("prod", 0, n), by(at("step"), at("off", 0, k + 1)), at("Wt", 0, n), Op.mult)
+            if t < TICKS - 2:
+                cp(col("off", 2), meal)
+            tt(at("prod"), by(at("step"), col("off", 0)), at("Wc") if t else at("Wt"), Op.mult)
             if t % 2:
                 meals(t - 1, t + 1, t - 1)
             elif t == TICKS - 2:
                 meals(t, t + 1, t)
-            scan(at("tot", 0, n), at("prod", 0, n), at("nil", 0, n), cc("lim"), Op.add, Op.add)
-            ts(col("off2", 0), col("tot", n - 1), meal, Op.max, cc("pad"), Op.min)
-            if t:
-                next_spare()
+            next_spare()
+            scan(at("tot"), at("prod"), at("nil"), cc("lim"), Op.add, Op.add)
+            next_spare()
+            ts(col("off2", 0), col("tot", 15), meal, Op.max, cc("pad"), Op.min)
+            next_spare()
             cp(by(at("like"), col("off2", 0)), at("kill", 0, 16))
 
         ts(col("offB", TICKS), meal, 4.0, Op.mult, cc("a"), Op.add)
@@ -570,21 +629,30 @@ def rank_program(g, core, T, topo):
             act(at("idt", 0, 112), by(at("jq"), at("offB", 0, TICKS - 1)))
             act(at("idt", 112, 128), by(at("jq"), col("offB", TICKS)))
             act(at("olw"), by(at("idt"), at("offZ")))
-        take(0, A)
-        take(A, A + 48)
+            cut[1] = C - 128
+        take(0, cut[1])
+        take(cut[1], cut[1] + 32)
         layer(0)
-        take(A + 48, C)
-        grow(0)
-        shrink(0)
-        layer(1)
-        for k in range(1, 6):
+        take(cut[1] + 32, C)
+        for k in (0, 1):
             grow(k)
             shrink(k)
-        scores(0, last)
-        grow(6)
-        grow(7)
-        shrink(6, True)
-        shrink(7, True)
+        layer(1)
+        for k in (2, 3):
+            grow(k)
+        for k in (2, 3):
+            shrink(k)
+        for k in (4, 5):
+            grow(k)
+            shrink(k)
+        if not last:
+            scores(0, last)
+        for k in (6, 7):
+            grow(k)
+        if last:
+            scores(0, last)
+        for k in (6, 7):
+            shrink(k)
         if not last:
             mask(0)
             scores(1, last)
@@ -592,21 +660,22 @@ def rank_program(g, core, T, topo):
             tastes()
 
     def results(h):
-        store("Y", T.oc[:, 4 * A * h:4 * A * (h + 1)], half("qx", h), half("qx", h)[0].bitcast(dt.uint8))
-
-    def product(h):
-        cp(half("ys", h), at(score[h], 0, A))
-        store("Y", T.y[:, A * h:A * (h + 1)], half("ys", h), half("ys", h)[0])
+        store("Y", T.oc[:, 4 * cut[h]:4 * cut[h + 1]], piece("qx", h), piece("qx", h)[0].bitcast(dt.uint8))
 
     act(at("olr"), at("olw", 0, 4 * C, 4))
     results(0)
     store("S", T.ol[:], at("olr"), T.olr[0:128:16, :])
-    product(0)
-    scores(1, True)
+    quant(piece("qx", 1), piece("sx", 1), piece("Xt", 1, 4))
+    for bank in ("p7", "p1"):
+        mm(bank, 128, at("qv"), at("sv"), piece("qx", 1), piece("sx", 1))
+    cp(piece("ys", 0), at(score[0], 0, cut[1]))
     results(1)
     for k in range(4):
-        store("S", T.osc[4 * k:4 * k + 4, :], at("sx"), T.sx[32 * k:32 * k + 4, :])
-    product(1)
+        store("YSSS"[k], T.osc[4 * k:4 * k + 4, :], at("sx"), T.sx[32 * k:32 * k + 4, :])
+    store("Y", T.y[:, 0:cut[1]], piece("ys", 0), piece("ys", 0)[0])
+    cp(at("ys", C - 128, C - 64), at("p7", 0, 64))
+    act(at("ys", C - 64, C), at("p1", 64, 128))
+    store("Y", T.y[:, cut[1]:C], piece("ys", 1), piece("ys", 1)[0])
     for sem in ("Gc", "sent", "S", "P", "V"):
         g.wait_ge(T.sem[sem], count[sem])
     g.sync.wait_ge(T.sem.stored, count["stored"])

from concourse.mybir import dt, AluOpType, AxisListType, ActivationFunctionType

C, A, LIFE, TICKS = 320, 160, 80, 8
STEPS = [2, 1, 3]
BIG = 1.0e29
UNIT = 512
VETO = 2.0e6
LIFT, DROP = 1024.0, 4096.0
TAB = 328
TILES = [(0, 320, [None, 19, 18, 17]), (320, 288, [16, 15, 14, 13]), (608, 288, [12, 11, 10, 9]),
         (896, 128, [8, 7, 6, 5]), (1024, 128, [4, 3, 2, 1])]
WIDE = 1152
ON_SCALAR = (9, 8, 7, 14, 13, 12, 11, 10)

F32, BF, I32, U16, CODE, U8 = "float32", "bfloat16", "int32", "uint16", "float8_e4m3fn_x4", "uint8"
SIZES = {
    BF: dict(Xt=4 * C, X32=4 * C, Xh=4 * C, Zt=4 * C, Mt=4 * A, ut=512, vt=512, ones=4 * A, cg=512, ck=516, ce=516,
             g128=128, Gt=4 * WIDE, Gc=4 * A, junk=3072, step=A + 16, Bh=4 * A, Bm=128, kq=128),
    F32: dict(j16=A, j4=80, c16=20, k128=128, k4=32, sgn=16, Bv=16, tab=2 * TAB, jq=4 * A, src=C, cols=32, K1=80, R1=80,
              Rc=C, lift=C, lift4=80, msk=C, own=C, seg=C, rowW=20, b1=10, Hs=C, Ow=C, Os=A, Qs=C, fk=C, cum=C,
              Wt=16, Wc=16, Wk=16, alive=16, vp=384, vT=384, s01=24, s23=24, sa=24, Yb=96, YT=96, like=A + 16, rm=A,
              kill=A, meal=8, prod=16, nil=16, tot=16, idt=128, olw=4 * C, olr=C, ys=C),
    I32: dict(pi=1, pt=8, si=24, a1=24),
    U16: dict(offU=32, offR=20, offM=40, offm=2, offY=6, offZ=80, off=4, off2=2, offB=10),
    CODE: dict(qx=C, qz=C, qu=128, qv=128, uq=512, wq=512, cq=896, gq=WIDE, kc=A),
    U8: dict(sx=C, sz=C, su=128, sv=128, us=512, wp=512, cs=896, gs=WIDE, ks=A),
}
for _r in range(3):
    SIZES[CODE].update({"qm%d" % _r: A, "lq%d" % _r: A})
    SIZES[U8].update({"sm%d" % _r: A, "ls%d" % _r: A})
SCRATCH = {_n: ("sbuf", [128, _w], _d) for _d in SIZES for _n, _w in SIZES[_d].items()}
for _b in range(8):
    SCRATCH["p%d" % _b] = ("psum", [128, 512], F32)

SEMAPHORES = ["V", "S", "P", "Gc", "ldx", "ldu", "ldw", "lds", "ldv", "sent", "arr0", "arr1", "arr2", "stored"]
COLS = ["k", "a", "q", "g", "odd", "q0", "a4", "a3", "rc", "tm", "mo", "even", "one", "lim", "pad", "fb",
        "a6", "s", "w", "kp", "lo", "hi", "sg0", "sg", "l0", "l1"]


def rank_program(g, core, T, topo):
    rank = T.rank_of(core)
    if rank is None:
        return
    Op, Fn = AluOpType, ActivationFunctionType
    queue = {"V": g.vector, "S": g.scalar, "P": g.tensor, "Gc": g, "Y": g.sync}
    count = {}
    known = {e: {} for e in queue}
    wrote, read = {}, {}

    def at(name, lo=0, hi=None, step=1):
        hi = SCRATCH[name][1][1] if hi is None else hi
        if SCRATCH[name][0] == "psum":
            bits = 1
        elif step == 1:
            bits = (1 << hi) - (1 << lo)
        else:
            bits = sum(1 << i for i in range(lo, hi, step))
        return (T[name][:, lo:hi:step] if step > 1 else T[name][:, lo:hi], name, bits, None)

    def by(win, off):
        return (win[0].indirect(off[0]), win[1], win[2], off)

    def words(view, off=None):
        ap = view[0].bitcast(dt.uint32)
        return (ap if off is None else ap.indirect(off[0]), view[1], view[2], off)

    def col(name, j):
        return at(name, j, j + 1)

    def cc(name):
        return col("cols", COLS.index(name))

    def block(name, j):
        return at(name, 128 * j, 128 * j + 128)

    def half(name, h, k=1):
        return at(name, k * A * h, k * A * (h + 1))

    def raw(x):
        return x[0] if isinstance(x, tuple) else x

    def wait(e, ev):
        sem, val, clock = ev
        if known[e].get(sem, 0) >= val:
            return
        queue[e].wait_ge(T.sem[sem], val)
        for name, n in clock.items():
            if known[e].get(name, 0) < n:
                known[e][name] = n

    def sides(reads, writes):
        reads = [x for x in reads if isinstance(x, tuple)]
        writes = [x for x in writes if isinstance(x, tuple)]
        return reads + [x[3] for x in reads + writes if x[3] is not None], writes

    def order(e, reads, writes):
        need = []
        for _, name, bits, _ in reads:
            need += [ev for m, ev in wrote.get(name, []) if m & bits]
            if SCRATCH[name][0] == "psum":
                need += [ev for m, ev in read.get(name, []) if ev[0] != e]
        for _, name, bits, _ in writes:
            need += [ev for m, ev in wrote.get(name, []) if m & bits and not e == ev[0] == "P"]
            need += [ev for m, ev in read.get(name, []) if m & bits]
        best = {}
        for ev in need:
            if ev[0] not in best or best[ev[0]][1] < ev[1]:
                best[ev[0]] = ev
        for ev in sorted(best.values(), key=lambda x: -len(x[2])):
            wait(e, ev)

    def note(e, sem, inc, reads, writes):
        count[sem] = count.get(sem, 0) + inc
        clock = dict(known[e])
        clock[sem] = count[sem]
        ev = (sem, count[sem], clock)
        for _, name, bits, _ in writes:
            for book in (wrote, read):
                book[name] = [(m & ~bits, x) for m, x in book.get(name, []) if m & ~bits]
            wrote[name].append((bits, ev))
        for _, name, bits, _ in reads:
            read.setdefault(name, []).append((bits, ev))

    def run(e, call, reads, writes):
        reads, writes = sides(reads, writes)
        order(e, reads, writes)
        call().then_inc(T.sem[e], 1)
        note(e, e, 1, reads, writes)

    def load(e, sem, view, ap, src):
        order(e, [], [view])
        queue[e].dma_start(ap, src).then_inc(T.sem[sem], 16)
        note(e, sem, 16, [], [view])

    def store(e, dst, view, ap):
        order(e, [view], [])
        queue[e].dma_start(dst, ap).then_inc(T.sem.stored, 16)
        count["stored"] = count.get("stored", 0) + 16

    v, s = g.vector, g.scalar

    def ts(out, a, s1, o0, s2=None, o1=None):
        if s2 is None:
            run("V", lambda: v.tensor_scalar(out[0], a[0], raw(s1), None, o0), [a, s1], [out])
        else:
            run("V", lambda: v.tensor_scalar(out[0], a[0], raw(s1), raw(s2), o0, o1), [a, s1, s2], [out])

    def tt(out, a, b, op):
        run("V", lambda: v.tensor_tensor(out[0], a[0], b[0], op), [a, b], [out])

    def cp(out, a):
        run("V", lambda: v.tensor_copy(out[0], a[0]), [a], [out])

    def scan(out, d0, d1, init, o0, o1):
        run("V", lambda: v.tensor_tensor_scan(out[0], d0[0], d1[0], raw(init), o0, o1), [d0, d1, init], [out])

    def total(out, a):
        run("V", lambda: v.tensor_reduce(out[0], a[0], AxisListType.X, Op.add), [a], [out])

    def turn(out, a):
        run("V", lambda: v.transpose(out[0], a[0]), [a], [out])

    def fill(out, c):
        run("V", lambda: v.memset(out[0], c), [], [out])

    def quant(q, sc, tile):
        run("V", lambda: v.quantize_mx(q[0], sc[0], tile[0]), [tile], [q, sc])

    def act(out, a, fn=Fn.Copy, scale=1.0, bias=0.0, total=None):
        run("S", lambda: s.activation(out[0], a[0], fn, bias=raw(bias), scale=raw(scale), accum_out=raw(total)),
            [a, scale, bias], [out, total])

    def affine(out, a, scale, bias):
        act(out, a, Fn.Identity, scale, bias)

    def put(out, n, c):
        act(out, at("ones", 0, n), scale=c)

    def mm(bank, n, lq, ls, rq, rs, start=True, stop=True):
        out = at(bank, 0, n)
        run("P", lambda: g.tensor.matmul_mx(out[0], lq[0], ls[0], rq[0], rs[0], start, stop), [lq, ls, rq, rs], [out])

    def iota(out, pattern, base=0):
        run("Gc", lambda: g.iota(out[0], pattern, base, 0, allow_small_or_imprecise_dtypes=True), [], [out])

    def pick(j):
        offs = at("offU", 8 * j, 8 * j + 8)
        cp(words(block("uq", j)), words(at("qu"), offs))
        out, src = block("us", j), by(at("su"), offs)
        run("S", lambda: s.activation(out[0], src[0], Fn.Copy), [src], [out])

    def by_u(bank, j, rq, rs, n):
        mm(bank, n, block("uq", j), block("us", j), rq, rs)

    load("S", "ldu", at("ut"), T.ut[:], T.u[:])
    load("Y", "ldx", at("Xt"), T.Xt[:], T.x[:])
    order("Y", [at("Xt")], [])
    load("Y", "ldw", at("wq"), T.wq[:].bitcast(dt.uint8), T.wc[:])
    load("Y", "lds", at("wp"), T.wp[:], T.ws[:])
    load("Y", "ldv", at("vt"), T.vt[:], T.v[:])

    run("Gc", lambda: g.iota(T.pi[:], [[1, 1]], 0, 1), [], [at("pi")])
    iota(at("c16"), [[16, 20]])
    iota(at("j16"), [[0, 10], [int(DROP), 16]])
    iota(at("g128"), [[1, 8], [0, 16]])
    iota(at("k128"), [[0, 32], [1, 4]])
    iota(at("src"), [[1, C]])
    iota(at("j4"), [[0, 20], [int(DROP), 4]])
    iota(at("sgn"), [[0, 2], [-2, 2], [0, 4]], 1)

    fill(at("ones"), 1.0)
    run("Gc", lambda: g.affine_select(T.ce[:], T.ones[:, 0:516], [[-1, 516]], Op.is_equal, 0.0, 3, 4), [at("ones")], [at("ce")])
    iota(at("tab", 0, TAB), [[-UNIT, TAB]])
    iota(at("tab", TAB, 2 * TAB), [[UNIT, TAB]])
    fill(at("Zt", 0, 512), 0.0)
    for j, (shift, keep) in enumerate([(0, 3), (2, 3), (0, 15), (4, 7), (2, 1)]):
        ts(col("pt", j), at("pi"), shift, Op.logical_shift_right, keep, Op.bitwise_and)
    cp(at("offU", 0, 8), at("c16", 0, 8))
    for first, width, blocks in TILES:
        put(at("Gt", 4 * (first + 16 * blocks[3]), 4 * (first + 16 * blocks[3] + 48)), 192, 0.0)
    ts(cc("q0"), col("pt", 2), DROP, Op.mult)
    cp(at("cols", 0, 5), at("pt", 0, 5))
    for first in (TILES[1][0] + A, TILES[2][0] + A, TILES[4][0]):
        quant(at("gq", first, first + 128), at("gs", first, first + 128), at("Zt", 0, 512))
    act(at("R1"), at("j16", 0, 80), Fn.Sign)
    quant(at("qu"), at("su"), at("ut"))
    affine(cc("a4"), cc("a"), DROP, -LIFT)
    act(at("Hs", 0, A), at("j16"), Fn.Relu, -1.0, cc("q0"))
    ts(at("K1"), at("j16", 0, 80), cc("q0"), Op.not_equal, -2 * BIG, Op.mult)
    ts(cc("s"), cc("a"), 1.0, Op.max, cc("k"), Op.add)
    pick(0)
    for h in range(2):
        quant(half("qx", h), half("sx", h), half("Xt", h, 4))
    affine(at("R1"), at("R1"), 2 * BIG, -BIG)
    for h in range(2):
        affine(half("lift", h), at("Hs", 0, A), -1.0, LIFT)
    affine(cc("rc"), cc("q"), LIFT - 1, 15 - 15 * LIFT - DROP)
    put(at("Rc"), C, -BIG)
    affine(cc("l0"), cc("k"), 1.0, 4.0)
    put(at("rowW"), 20, 0.0)
    affine(at("Rc", 0, C, 16), at("c16"), 1.0, cc("rc"))

    def later_constants():
        for t in range(4):
            ts(at("cg", t, 512, 4), at("g128"), cc("g"), Op.is_equal)
        ts(cc("w"), cc("s"), 4.0, Op.is_ge, -4.0, Op.mult)
        ts(at("lift4"), at("j4"), cc("a4"), Op.subtract, LIFT, Op.min)
        yield
        affine(cc("a3"), cc("a"), LIFT, -3 * LIFT - DROP)
        affine(cc("tm"), cc("k"), 1.0, 4 * DROP)
        ts(cc("kp"), cc("w"), cc("s"), Op.add, 4.0, Op.add)
        yield
        quant(block("cq", 0), block("cs", 0), at("cg"))
        yield
        ts(cc("lo"), cc("kp"), cc("l0"), Op.min)
        ts(cc("hi"), cc("kp"), cc("l0"), Op.max)
        put(at("lift4", 3, 80, 4), 20, cc("a3"))
        put(at("ck"), 516, 0.0)
        put(at("Gc"), 4 * A, 0.0)
        yield
        ts(at("offU", 8, 16), at("c16", 0, 8), cc("lo"), Op.add)
        ts(at("offU", 16, 24), at("c16", 0, 8), cc("hi"), Op.add)
        yield
        ts(cc("sg0"), cc("w"), 0.5, Op.mult, 1.0, Op.add)
        yield
        pick(1)
        yield
        pick(2)
        tastes()
        act(half("X32", 0, 4), half("Xt", 0, 4), scale=32.0)
        yield
        ts(cc("sg"), cc("a"), 1.0, Op.min, cc("sg0"), Op.mult)
        ts(at("offU", 24, 32), at("c16", 0, 8), cc("k"), Op.add, 8.0, Op.add)
        yield
        ts(at("kq"), at("k128"), cc("k"), Op.is_equal, cc("sg"), Op.mult)
        yield
        tt(at("ck", 1, 513, 4), at("kq"), at("cg", 0, 512, 4), Op.mult)
        yield
        for h in range(2):
            quant(block("cq", 1 + h), block("cs", 1 + h), at("ck", 1 - h, 513 - h))
        yield

    def tick_constants():
        affine(cc("fb"), cc("k"), 16.0, -32.0)
        act(cc("lim"), cc("a"), Fn.Sign)
        affine(cc("l1"), cc("k"), -1.0 / 16, 0.0)
        put(at("vp"), 384, 0.0)
        put(at("kill"), A, -BIG)
        put(at("like", A, A + 16), 16, -BIG)
        put(at("step", 0, 1), 1, 1.0)
        put(at("nil"), 16, 0.0)
        act(at("k4"), at("k128", 0, 32), scale=4.0)
        affine(cc("pad"), cc("q"), 1.0, float(A))
        affine(cc("a6"), cc("a"), 6.0, 0.0)
        affine(cc("mo"), cc("odd"), float(TAB), cc("l1"))
        affine(cc("lim"), cc("lim"), VETO, (LIFE - 0.5) * UNIT)

    def tick_columns():
        ts(at("Bv"), at("k128", 0, 16), cc("k"), Op.is_lt, VETO, Op.mult)
        ts(cc("even"), cc("a"), 2.0, Op.is_lt)
        ts(cc("one"), cc("a"), 1.0, Op.is_equal)
        tt(at("Bv"), at("Bv"), at("sgn"), Op.mult)

    def slot(c):
        for first, width, blocks in TILES:
            if c in blocks:
                return at("Gt", 4 * first + blocks.index(c), 4 * (first + 16 * c), 4)

    def diag(h):
        return at("Gt", 4 * A * h, 4 * A * (h + 1), 4)

    score = ("p0", "p7")

    def scores(h, last):
        quant(piece("qx", h), piece("sx", h), piece("Xt", h, 4))
        if last:
            mm(score[h], cut[1], at("qv"), at("sv"), piece("qx", h), piece("sx", h))
            return
        by_u(score[h], 0, half("qx", h), half("sx", h), A)
        copies(h)

    def copies(h):
        if h == 0:
            by_u("p3", 0, half("qx", 0), half("sx", 0), A)
        else:
            by_u("p1", 0, at("qx"), at("sx"), C)
            by_u("p2", 0, at("qx"), at("sx"), C)

    def tastes():
        by_u("p6", 2, at("qx"), at("sx"), C)
        by_u("p5", 1, at("qx"), at("sx"), C)

    def quarters(h):
        return (0, 80) if h else (80, 0)

    def mask(h):
        for lo in quarters(h):
            tt(at("msk", A * h + lo, A * h + lo + 80), at(score[h], lo, lo + 80), at("K1"), Op.add)

    def hold(h):
        for lo in quarters(h):
            scan(at("own", A * h + lo, A * h + lo + 80), at("R1"), at("msk", A * h + lo, A * h + lo + 80), -BIG, Op.min, Op.max)

    def own(c):
        return col("own", 16 * c + 15)

    def diagonal(h):
        tt(diag(h), at(score[h], 0, A), half("own", h), Op.is_le)

    def segments(h):
        scan(half("seg", h), half("Rc", h), diag(h), -BIG, Op.max, Op.subtract)

    def spare_room(c):
        return at("junk", 8 * c * (c - 1), 8 * c * (c + 1))

    def beats(c):
        if c in ON_SCALAR:
            act(spare_room(c), at("p3" if c < 10 else "p1", 0, 16 * c), Fn.Sign, -1.0, own(c))
        else:
            ts(slot(c), at("p0" if c < 10 else "p2", 0, 16 * c), own(c), Op.is_lt)

    def row(c):
        if c in ON_SCALAR:
            act(slot(c), spare_room(c), Fn.Relu, total=col("rowW", c))
        else:
            act(spare_room(c), slot(c), total=col("rowW", c))

    def by_scalar(blocks):
        for i in range(len(blocks) + 2):
            if i < len(blocks):
                beats(blocks[i])
            if i >= 2:
                row(blocks[i - 2])

    def pack(lo, hi):
        quant(at("gq", lo, hi), at("gs", lo, hi), at("Gt", 4 * lo, 4 * hi))

    def fold(k, h, start=False, stop=False):
        first, width, blocks = TILES[k]
        lo, hi = (first + A, first + width) if h else (first, first + min(A, width))
        mm(("p3", "p4")[h], hi - lo, block("cq", 0), block("cs", 0), at("gq", lo, hi), at("gs", lo, hi), start, stop)

    def ends(name, h):
        return at(name, A * h + 15, A * (h + 1), 16)

    def ranks(h):
        scan(half("Hs", h), at(("p3", "p4")[h], 0, A), half("lift", h), -DROP, Op.max, Op.add)

    def places(h):
        ts(at("offR", 10 * h, 10 * h + 10), at("b1") if h else ends("Hs", 0), DROP, Op.add)

    def spread(h):
        cp(by(at("Ow"), at("offR", 10 * h, 10 * h + 10)), half("src", h))

    def prefer(h):
        tt(at("Gc", h, 4 * A, 4), at("p5", A * h, A * (h + 1)), half("Qs", h), Op.is_ge)

    def classes():
        quant(at("kc"), at("ks"), at("Gc"))
        for h, bank in enumerate(("p7", "p1")):
            mm(bank, A, block("cq", 1 + h), block("cs", 1 + h), at("kc"), at("ks"))

    def members():
        for h, bank in enumerate(("p7", "p1")):
            act(half("fk", h), at(bank, 0, A), Fn.Relu, 16.0, cc("fb"))

    def standing(a):
        tt(at("vp", 96 * a, 96 * a + 80), at("cum", a, C, 4), at("fk", a, C, 4), Op.mult)

    def take(lo, hi):
        tt(at("Zt", 4 * lo, 4 * hi), by(at("Bm"), at("offZ", lo // 4, hi // 4)), at("Xh", 4 * lo, 4 * hi), Op.add)

    cut = [0, A, C]

    def piece(name, h, k=1):
        return at(name, k * cut[h], k * cut[h + 1])

    def layer(h):
        quant(piece("qz", h), piece("sz", h), piece("Zt", h, 4))
        for b in range(4):
            mm("p%d" % (4 * h + b), cut[h + 1] - cut[h], block("wq", b), block("wp", b), piece("qz", h), piece("sz", h))

    def plane(name, k):
        return at(name, 4 * cut[k // 4] + k % 4, 4 * cut[k // 4 + 1], 4)

    def grow(k):
        tt(plane("X32", k), at("p%d" % k, 0, cut[k // 4 + 1] - cut[k // 4]), plane("X32", k), Op.add)

    def shrink(k):
        if k % 4 >= 2:
            ts(plane("Xt", k), plane("X32", k), 1.0 / 32, Op.mult)
        else:
            act(plane("Xt", k), plane("X32", k), scale=1.0 / 32)

    setup = later_constants()

    def aside():
        next(setup, None)

    for h in range(2):
        by_u(score[h], 0, half("qx", h), half("sx", h), A)
    copies(0)
    copies(1)
    aside()
    mask(0)
    mask(1)
    aside()
    hold(0)
    hold(1)

    for rnd, step in enumerate(STEPS):
        last = rnd == len(STEPS) - 1
        peer = T.cores[rank ^ step]
        qm, sm, lq, ls = [at(n % rnd) for n in ("qm%d", "sm%d", "lq%d", "ls%d")]

        aside()
        by_scalar(ON_SCALAR[:3])
        beats(6)
        diagonal(0)
        if rnd:
            mask(1)
        for c in (5, 4, 3):
            beats(c)
        if rnd:
            hold(1)
        row(6)
        for c in (2, 1):
            beats(c)
        segments(0)
        by_scalar(ON_SCALAR[3:])
        for c in (5, 4, 3, 2, 1):
            row(c)
        for c in (19, 18, 17):
            beats(c)
        diagonal(1)
        for c in (16, 15):
            beats(c)
        pack(0, 320)
        fold(0, 0, start=True)
        fold(0, 1, start=True)
        pack(896, 1088)
        fold(3, 0)
        fold(4, 0)
        for c in (19, 18, 17, 16):
            row(c)
        pack(320, 576)
        fold(1, 0)
        pack(608, 800)
        fold(2, 0, stop=True)
        fold(1, 1)
        fold(2, 1, stop=True)
        segments(1)
        aside()
        tt(ends("lift", 0), ends("seg", 0), at("rowW", 0, 10), Op.subtract)
        total(col("rowW", 15), slot(15))
        cp(ends("lift", 1), ends("seg", 1))
        aside()
        ranks(0)
        ranks(1)
        places(0)
        aside()
        tt(at("b1"), ends("Hs", 1), at("rowW", 10, 20), Op.subtract)
        spread(0)
        places(1)
        aside()
        if rnd:
            act(at("Qs"), at("p6", 0, C))
            prefer(0)
        spread(1)
        aside()
        if rnd:
            prefer(1)
        for lo in (80, 0):
            scan(at("Os", lo, lo + 80), at("Ow", lo, lo + 80), at("lift4"), -DROP, Op.max, Op.add)
        aside()
        for lo in (20, 0):
            ts(at("offM", lo, lo + 20), at("Os", 4 * lo + 3, 4 * lo + 80, 4), 4.0, Op.mult, cc("tm"), Op.add)
        if rnd:
            classes()
        aside()
        act(at("Mt", 2 * A, 4 * A), by(at("Xt"), at("offM", 20, 40)))
        cp(at("Mt", 0, 2 * A), by(at("Xt"), at("offM", 0, 20)))
        if rnd:
            members()
        quant(qm, sm, at("Mt"))

        order("Gc", [qm, sm], [])
        rid, pid, _ = topo.addr(peer)
        lanes = len(topo.engines(core, peer))
        arr = "arr%d" % rnd
        g.remote_dma(lq[0].bitcast(dt.uint8), qm[0].bitcast(dt.uint8), T.sem[arr], T.sem.sent, pid, rid, topo.mask(core, peer))
        g.remote_dma(ls[0], sm[0], T.sem[arr], T.sem.sent, pid, rid, topo.mask(core, peer))
        count["sent"] = count.get("sent", 0) + 2 * lanes
        for view in (lq, ls):
            wrote[view[1]] = [(view[2], (arr, 2 * lanes, {arr: 2 * lanes}))]
        if rnd == 0:
            iota(at("jq"), [[1, A], [0, 4]])

        if rnd == 0:
            aside()
            act(at("Qs"), at("p6", 0, C))
            pick(3)
            tick_constants()
            aside()
            prefer(0)
            prefer(1)
            tick_columns()
            for b in range(4):
                quant(block("cq", 3 + b), block("cs", 3 + b), at("ce", 3 - b, 515 - b))
                if b == 1:
                    classes()
                    members()
            ts(at("offY"), at("c16", 0, 6), 1.0 / 16, Op.mult, cc("a6"), Op.add)
        act(at("Xh"), at("Xt"), scale=0.5)
        if rnd == 0:
            act(half("X32", 1, 4), half("Xt", 1, 4), scale=32.0)
        scan(half("cum", 0), half("fk", 0), half("fk", 0), cc("k"), Op.add, Op.max)
        scan(half("cum", 1), half("fk", 1), half("fk", 1), col("cum", A - 1), Op.add, Op.max)
        ts(col("offm", 0), col("cum", C - 1), 1.0 / 16, Op.mult, cc("mo"), Op.add)
        standing(0)
        tt(at("Wt"), by(at("tab"), col("offm", 0)), at("Bv"), Op.add)

        def index(c):
            tt(at("Yb", 16 * c, 16 * c + 32), by(at("a1"), at("offY", c, c + 2)), at("k4"), Op.add)

        spare = [lambda: standing(1), lambda: standing(2), lambda: standing(3),
                 lambda: turn(at("vT", 0, 192), at("vp", 0, 192)), lambda: turn(at("vT", 192, 384), at("vp", 192, 384)), None,
                 lambda: tt(at("s01"), at("vT", 0, 384, 16), at("vT", 1, 384, 16), Op.add),
                 lambda: tt(at("s23"), at("vT", 2, 384, 16), at("vT", 3, 384, 16), Op.add),
                 lambda: tt(at("sa"), at("s01"), at("s23"), Op.add),
                 lambda: ts(at("si"), at("sa"), 1.0 / 16, Op.mult, -16.0, Op.add),
                 lambda: ts(at("a1"), at("si"), 16 * (TICKS - 1) + 3, Op.bitwise_and),
                 lambda: index(0), lambda: index(2), lambda: index(4), None,
                 lambda: turn(at("YT"), at("Yb")), None,
                 lambda: cp(at("offZ"), at("YT", 0, 80))]
        if last:
            spare.append(lambda: quant(at("qv"), at("sv"), at("vt")))

        def next_spare():
            job = spare.pop(0) if spare else None
            if job:
                job()

        by_u("p0", 3, lq, ls, A)
        for b in range(4):
            mm("p%d" % (2 + b), A, block("cq", 3 + b), block("cs", 3 + b), lq, ls)

        def meals(lo, hi, first, on_vector=False):
            out, src = at("Bm", 16 * lo, 16 * hi), by(at("Bh"), at("offB", first, first + hi - lo))
            if on_vector:
                cp(out, src)
            else:
                act(out, src)

        for t in range(TICKS):
            meal = col("meal", t)
            if 0 < t < TICKS - 1:
                act(at("alive"), by(at("like"), col("off", 2)), Fn.Sign, 1.0, BIG)
            scan(at("rm"), at("like", 0, A) if t else at("p0", 0, A), at("kill"), -BIG, Op.max, Op.max)
            act(at("step", 1, A + 1), at("rm"), Fn.Sign, -1.0, col("rm", A - 1), meal)
            if t == 0:
                cp(at("like", 0, A), at("p0", 0, A))
                for b in range(4):
                    act(at("Bh", b, 4 * A, 4), at("p%d" % (2 + b), 0, A), scale=0.5)
            if t == TICKS - 1:
                break
            if t:
                tt(at("Wk"), at("Wc") if t > 1 else at("Wt"), at("alive"), Op.mult)
                tt(at("Wc"), at("Wk"), at("Wt"), Op.add)
            ts(col("off", 0), meal, cc("even"), Op.mult, cc("one"), Op.add)
            ts(col("offB", t), meal, 4.0, Op.mult, cc("a"), Op.add)
            if t < TICKS - 2:
                cp(col("off", 2), meal)
            tt(at("prod"), by(at("step"), col("off", 0)), at("Wc") if t else at("Wt"), Op.mult)
            if t % 2:
                meals(t - 1, t + 1, t - 1)
            elif t == TICKS - 2:
                meals(t, t + 1, t)
            next_spare()
            scan(at("tot"), at("prod"), at("nil"), cc("lim"), Op.add, Op.add)
            next_spare()
            ts(col("off2", 0), col("tot", 15), meal, Op.max, cc("pad"), Op.min)
            next_spare()
            cp(by(at("like"), col("off2", 0)), at("kill", 0, 16))

        ts(col("offB", TICKS), meal, 4.0, Op.mult, cc("a"), Op.add)
        meals(TICKS - 1, TICKS, TICKS, True)
        if last:
            act(at("idt", 0, 112), by(at("jq"), at("offB", 0, TICKS - 1)))
            act(at("idt", 112, 128), by(at("jq"), col("offB", TICKS)))
            act(at("olw"), by(at("idt"), at("offZ")))
            cut[1] = C - 128
        take(0, cut[1])
        take(cut[1], cut[1] + 32)
        layer(0)
        take(cut[1] + 32, C)
        for k in (0, 1):
            grow(k)
            shrink(k)
        layer(1)
        for k in (2, 3):
            grow(k)
        for k in (2, 3):
            shrink(k)
        for k in (4, 5):
            grow(k)
            shrink(k)
        if not last:
            scores(0, last)
        for k in (6, 7):
            grow(k)
        if last:
            scores(0, last)
        for k in (6, 7):
            shrink(k)
        if not last:
            mask(0)
            scores(1, last)
            hold(0)
            tastes()

    def results(h):
        store("Y", T.oc[:, 4 * cut[h]:4 * cut[h + 1]], piece("qx", h), piece("qx", h)[0].bitcast(dt.uint8))

    act(at("olr"), at("olw", 0, 4 * C, 4))
    results(0)
    store("S", T.ol[:], at("olr"), T.olr[0:128:16, :])
    quant(piece("qx", 1), piece("sx", 1), piece("Xt", 1, 4))
    for bank in ("p7", "p1"):
        mm(bank, 128, at("qv"), at("sv"), piece("qx", 1), piece("sx", 1))
    cp(piece("ys", 0), at(score[0], 0, cut[1]))
    results(1)
    for k in range(4):
        store("YSSS"[k], T.osc[4 * k:4 * k + 4, :], at("sx"), T.sx[32 * k:32 * k + 4, :])
    store("Y", T.y[:, 0:cut[1]], piece("ys", 0), piece("ys", 0)[0])
    cp(at("ys", C - 128, C - 64), at("p7", 0, 64))
    act(at("ys", C - 64, C), at("p1", 64, 128))
    store("Y", T.y[:, cut[1]:C], piece("ys", 1), piece("ys", 1)[0])
    for sem in ("Gc", "sent", "S", "P", "V"):
        g.wait_ge(T.sem[sem], count[sem])
    g.sync.wait_ge(T.sem.stored, count["stored"])
